import numpy as np, ml_dtypes
CORES = [9,25,41,57]
N = 4
BF = ml_dtypes.bfloat16
def gentries(a):
    return np.ascontiguousarray(a.reshape(8, 16, -1).transpose(0, 2, 1)).reshape(8, -1)
def gtable(e):
    e = np.asarray(e); return np.ascontiguousarray(e.reshape(8, -1, 16).transpose(0, 2, 1)).reshape(128, -1).astype(np.int32)
S, Q, T, CAP, RO = 2048, 4, 256, 128, 4
B = Q * S
def near(rng, c, a):
    return np.clip(np.take_along_axis(c, a[:, :, None, :], 3) + rng.integers(-40, 41, (N, 8, 16, T)), 0, 255)
def parts(rng):
    c = rng.integers(0, 256, (N, 8, 16, S)); g = rng.integers(-16, 16, (N, 8, 16, B))
    H = S >> 4; hub = np.argsort(rng.random((N, 8, S)), axis=2)[..., :H]
    i = np.minimum((H * rng.random((N, 8, 16 * S)) ** 2).astype(np.int64), H - 1)
    u = np.take_along_axis(hub, i, 2).reshape(N, 8, 16, S); u = np.where(rng.random(u.shape) < 0.5, u, rng.integers(0, S, u.shape))
    i = np.minimum((H * rng.random((N, 8, T)) ** 2).astype(np.int64), H - 1)
    a = np.take_along_axis(hub, i, 2); a = np.where(rng.random(a.shape) < 0.5, a, rng.integers(0, S, a.shape))
    h = rng.integers(0, Q, (N, 8, S)); e = rng.choice(np.array([0.1, 0.3, 0.6]), (N, 8, 1))
    f = np.where(rng.random((N, 8, S)) < e, 0, rng.integers(0, Q + 1, (N, 8, S)))
    return c, u, g, h, f, a, near(rng, c, a)
def pack(c, u, g, h, f, a, z):
    return {"xs": np.ascontiguousarray(c.reshape(N, 128, S)).astype(np.float32).astype(BF), "su": np.ascontiguousarray(u.reshape(N, 128, S)).astype(np.int32),
            "gs": np.ascontiguousarray(g.reshape(N, 128, B)).astype(np.float32).astype(BF), "hd0": h.astype(np.int32), "fl0": f.astype(np.int32),
            "a0": np.stack([gtable(v) for v in a]), "z0": np.ascontiguousarray(z.reshape(N, 128, T)).astype(np.float32).astype(BF)}
def setup_inputs(rng):
    return pack(*parts(rng))
def setup_inputs_room(rng):
    c, u, g, h, f, a, z = parts(rng); num = (CAP, CAP + 1, T, CAP - 1, 1, 0, CAP, CAP + 1)
    for r in range(N):
        for k in range(8):
            j = (r + k) % 8; o = rng.permutation(S)[:T]; a[r, k] = o
            full = rng.integers(1, Q + 1, T)
            if j in (3, 5, 6):
                full[:] = 1 if j == 5 else Q
                u[r, k] = np.arange(S)
            f[r, k, o] = np.where(rng.permutation(T) < num[j], 0, full)
    return pack(c, u, g, h, f, a, near(rng, c, a))
def setup_inputs_crowd(rng):
    c, u, g, h, f, a, z = parts(rng)
    for r in range(N):
        for k in range(8):
            j = (r + k) % 8
            if j == 7: continue
            o = np.concatenate([rng.permutation(np.array([0, S - 1])), 1 + rng.permutation(S - 2)])
            if j < 4:
                n = (1, 2, 5, 12)[j]; a[r, k] = o[rng.integers(0, n, T)]; u[r, k] = o[rng.integers(0, n, (16, S))]
            else:
                w = (Q, Q, Q + 1)[j - 4]; o = o[:(T + w - 1) // w]
                a[r, k] = rng.permutation(np.repeat(o, w)[:T]); f[r, k, o] = (Q, 0, 0)[j - 4]
    return pack(c, u, g, h, f, a, near(rng, c, a))
def setup_inputs_ties(rng):
    c, u, g, h, f, a, z = parts(rng); pro = rng.integers(2, 254, (8, 16, 3))
    for k in range(8):
        if k % 2 == 0:
            c[:, k] = pro[k][:, np.arange(S) % 3]; g[:, k] = 2 * rng.integers(0, 2, (N, 16, B)) - 1; f[:, k] = f[:, k] * (rng.random((N, S)) < 0.5)
            if k % 4 == 2:
                g[:, k] = g[:, k] * rng.integers(0, 2, (N, 1, B)); u[:, k, 0] = np.where(rng.random((N, S)) < 0.5, np.arange(S), u[:, k, 0])
        else:
            c[:, k] = c[:, k][..., np.arange(S) // 2 * 2]; g[:, k] = g[:, k][..., np.arange(B) & 31]
    z = near(rng, c, a); z[:, ::2] = np.take_along_axis(c[:, ::2], a[:, ::2, None, :], 3)
    return pack(c, u, g, h, f, a, z)
def setup_inputs_ends(rng):
    c, u, g, h, f, a, z = parts(rng)
    c = 255 * rng.integers(0, 2, c.shape); g = 31 * rng.integers(0, 2, g.shape) - 16; z = 255 * rng.integers(0, 2, z.shape)
    k = rng.integers(0, 3, (N, 8, 1, T)); z = np.where(k == 0, 0, np.where(k == 1, 255, z))
    p = rng.permutation(8)
    f[:, p[0]] = 0; f[:, p[1]] = Q; h[:, p[2]] = Q - 1; h[:, p[3]] = 0
    for j in (4, 5, 6):
        w = p[j]; cw = rng.integers(0, 2, (N, 16, S)); zw = 255 - rng.integers(0, 2, (N, 16, T)); f[:, w] = Q * rng.integers(0, 2, (N, S))
        if j < 6:
            two = np.argsort(rng.random((N, 16, B)), axis=1) < 2
            gw = np.where(two, -rng.integers(1, 9, (N, 16, B)), rng.integers(6, 16, (N, 16, B)))
            if j == 5: cw = 255 - cw; zw = 255 - zw; gw = -gw
            g[:, w] = gw
        c[:, w] = cw; z[:, w] = zw
    a[..., 0] = 0; a[..., 1] = S - 1; a[..., T - 2] = 0; a[..., T - 1] = S - 1
    u = np.where(rng.random(u.shape) < 0.3, (S - 1) * rng.integers(0, 2, u.shape), u)
    return pack(c, u, g, h, f, a, z)
def setup_inputs_spread(rng):
    c, u, g, h, f, a, z = parts(rng)
    c = np.minimum((256 * rng.random(c.shape) ** np.exp2(rng.uniform(-3, 3, (N, 8, 1, S)))).astype(np.int64), 255)
    z = np.minimum((256 * rng.random(z.shape) ** np.exp2(rng.uniform(-3, 3, (N, 8, 1, T)))).astype(np.int64), 255)
    g = np.clip(np.floor((rng.random(g.shape) * 2 - 1) * np.exp2(rng.uniform(-2, 4, (N, 8, 1, B)))).astype(np.int64), -16, 15)
    m = rng.permuted(np.tile(np.arange(S), (N, 8, 1)), axis=2)
    i = np.minimum((S * rng.random((N, 8, 16 * S)) ** rng.uniform(1, 5, (N, 8, 1))).astype(np.int64), S - 1); u = np.take_along_axis(m, i, 2).reshape(N, 8, 16, S)
    i = np.minimum((S * rng.random((N, 8, T)) ** rng.uniform(1, 5, (N, 8, 1))).astype(np.int64), S - 1); a = np.take_along_axis(m, i, 2)
    f = np.minimum(((Q + 1) * rng.random((N, 8, S)) ** np.exp2(rng.uniform(-2, 2, (N, 8, 1)))).astype(np.int64), Q)
    return pack(c, u, g, h, f, a, z)
def check_inputs(d):
    bad = []
    for k, lo, hi in (("xs", 0, 255), ("su", 0, S - 1), ("gs", -16, 15), ("hd0", 0, Q - 1), ("fl0", 0, Q), ("a0", 0, S - 1), ("z0", 0, 255)):
        v = np.asarray(d[k]).astype(np.float64)
        if not (np.all(v >= lo) and np.all(v <= hi) and np.all(v == np.floor(v))): bad.append("range of " + k)
    return bad
def reference(xs, su, gs, hd0, fl0, a0, z0):
    X = xs.astype(np.float32).astype(np.int64).reshape(N, 8, 16, S); U = su.astype(np.int64).reshape(N, 8, 16, S)
    G = gs.astype(np.float32).astype(np.int64).reshape(N, 8, 16, B); hd = hd0.astype(np.int64); fl = fl0.astype(np.int64)
    a = np.stack([gentries(v) for v in a0]).astype(np.int64); z = z0.astype(np.float32).astype(np.int64).reshape(N, 8, 16, T)
    low = np.tri(T, k=-1, dtype=bool); odd = 2 * np.arange(16)[:, None] + 1
    for t in range(RO):
        same = a[:, :, :, None] == a[:, :, None, :]
        place = np.sum(same & low, axis=3); count = np.sum(same, axis=3)
        ha = np.take_along_axis(hd, a, 2); fa = np.take_along_axis(fl, a, 2)
        pop = place < fa; slot = Q * a + ((ha + place) & (Q - 1))
        zn = np.clip(z + np.take_along_axis(G, slot[:, :, None, :], 3), 0, 255)
        s = np.take_along_axis(U, a[:, :, None, :], 3)
        c = np.take_along_axis(X, s.reshape(N, 8, 1, 16 * T), 3).reshape(N, 8, 16, 16, T)
        best = np.argmin(np.sum(np.abs(c - zn[:, :, :, None, :]), axis=2), axis=2)
        to = np.take_along_axis(s, best[:, :, None, :], 2)[:, :, 0]
        gone = np.minimum(count, fa)
        np.put_along_axis(hd, a, (ha + gone) & (Q - 1), 2); np.put_along_axis(fl, a, fa - gone, 2)
        ask = ~pop & (np.add.accumulate((~pop).astype(np.int64), axis=2) <= CAP)
        d = 1 + t % (N - 1); XR = np.roll(X, -d, axis=0); GR = np.roll(G, -d, axis=0)
        u = np.sum(odd * z, axis=2) & 4095
        ix = (((u * u) >> 5)[:, :, None, :] + odd * u[:, :, None, :]) & (B - 1)
        cand = np.take_along_axis(GR, ix.reshape(N, 8, 1, 16 * T), 3).reshape(N, 8, 16, 16, T)
        goal = np.take_along_axis(XR, a[:, :, None, :], 3)
        m = np.argmin(np.sum(np.abs(z[:, :, :, None, :] + cand - goal[:, :, :, None, :]), axis=2), axis=2)
        seg = np.take_along_axis(cand, m[:, :, None, None, :], 3)[:, :, :, 0]
        put = ask & (place - fa < Q)
        for r in range(N):
            for g in range(8):
                w = np.flatnonzero(put[r, g])
                G[r, g][:, slot[r, g, w]] = seg[r, g][:, w]
                np.add.at(fl[r, g], a[r, g, w], 1)
        a = np.where(pop, to, a); z = np.where(pop[:, :, None, :], zn, z)
    return {"yz": z.reshape(N, 128, T).astype(np.float32).astype(BF), "ya": a.astype(np.float32), "yh": hd.astype(np.float32), "yf": fl.astype(np.float32)}

@@ -1,0 +1,590 @@
+from concourse.mybir import AluOpType as Op, ActivationFunctionType as Fn
+
+STEPS = 4
+ASKS = STEPS - 1
+NS = 4
+SBANK = ["ps6", "ps7", "ps0", "ps1"]
+B0, BD = 144, 8336
+PSUM = ["ps%d" % i for i in range(8)]
+SCRATCH = {}
+for _n in PSUM:
+    SCRATCH[_n] = ("psum", [128, 512], "float32")
+WIDE = {"xw": (2048, "bfloat16"), "sui": (4096, "int32"), "bank": (BD, "bfloat16"), "hm": (2048, "bfloat16"), "cc": (4096, "bfloat16"),
+        "mx": (4096, "bfloat16"), "cand": (2048, "bfloat16"), "mq": (2048, "bfloat16"), "eb": (4096, "bfloat16"), "lh": (2048, "bfloat16"),
+        "rh": (2048, "bfloat16"), "rd": (2048, "bfloat16"), "za": (256, "bfloat16"), "zb": (256, "bfloat16")}
+for _n, (_w, _d) in WIDE.items():
+    SCRATCH[_n] = ("sbuf", [128, _w], _d)
+NARROW = {
+    "float32": "pcol 1 p16 1 pdiv 1 odd 1 l16 1 ge8 1 is0 1 jf 256 pat16 256 patc8 128 mask16 256 qd16 128 gm 64 rpt 128 cw 128 cwt 128 e8f 8 dump 8 "
+               "als 16 al4 16 alof 16 ahif 16 arm 256 gc_ 256 d1 16 s1 16 s2 16 y1 16 p8 16 yv 16 oq 16 pp 16 sb 16 pt 16 wl 16 ks 256 ko 128 k1 128 "
+               "k2 64 k3 32 k4 16 arf 256 pv1 16 pv2 16 pv3 16 pv 16 ca 256 cb 128 cb2 128 cm 64 c1 32 c2 16 v2 8 um 128 q0 64 q1 64 q2 32 q3 16 "
+               "q6 8 ohf 128 oyf 128",
+    "int32": "ci 1 ci2 1 ci3 1 ji 256 jt 256 hi0 128 fi0 128 a0i 16 ai 16 alo 16 ahi 16 cdi 16 hh 16 tl 16 xx 16 x3 16 ri 16 rlo 16 rhi 16 lni 8 v1 8 qa 8 "
+             "ui 128 uu 128 usq 128 uv 128 us 128 ux 128 q4 8 q5 8 w1 128 w2 128 w3 128 w4 128",
+    "uint16": "e16 16 e8 8 alu 16 alou 16 suu 256 offu 16 sou 16 lnu 8 qau 8 cou 128 seu 8",
+    "bfloat16": "bo 128 bow 128 ob8 8 o16 8 o32 8 om16 8 idb 128 idn 128 tri 128 ones 128 quar 128 rp 128 i128 128 maskm 256 lanb 16 rowc 256 zer 16 dg 256 "
+                "blk 16 ay 256 zs 256 oh 256 goal 128",
+    "float16": "boh 128 ob8h 8 ob8k 8 arow 256 os 256 gmk 256 sp 256 aa 256 aq 128"}
+PACK = {}
+for _d, _t in NARROW.items():
+    _at, _f = 0, _t.split()
+    for _n, _w in zip(_f[::2], _f[1::2]):
+        PACK[_n] = ("pk_" + _d, _at, int(_w))
+        _at += -(-int(_w) // 16) * 16
+    SCRATCH["pk_" + _d] = ("sbuf", [128, _at], _d)
+for _t in range(ASKS):
+    for _n, _w, _d in (("qp", 8, "int32"), ("zq", 128, "bfloat16"), ("an", 128, "bfloat16"),
+                       ("qpin", 8, "int32"), ("zqin", 128, "bfloat16"), ("anin", 128, "bfloat16"), ("offr", 8, "uint16")):
+        SCRATCH["%s%d" % (_n, _t)] = ("sbuf", [128, _w], _d)
+LOADS = ["la", "ls", "lx", "lh0", "lf0", "lz", "lg"]
+SEMAPHORES = ["sv", "ss", "st", "sg", "sent", "sout"] + LOADS + ["%s%d" % (n, t) for t in range(ASKS) for n in ("rp", "rz", "ra")]
+
+
+def rank_program(g, core, T, topo):
+    rank = T.rank_of(core)
+    if rank is None:
+        return
+    N = len(T.cores)
+    qobj = {"v": g.vector, "s": g.scalar, "t": g.tensor, "g": g, "d": g.sync}
+    qsem = {"v": "sv", "s": "ss", "t": "st", "g": "sg"}
+    count = {"v": 0, "s": 0, "t": 0, "g": 0}
+    known = {q: {} for q in qobj}
+    recs = {}
+
+    def need(q, sem, n, snap):
+        kn = known[q]
+        if kn.get(sem, 0) < n:
+            qobj[q].wait_ge(T.sem[sem], n)
+            kn[sem] = n
+            for a, b in snap.items():
+                if kn.get(a, 0) < b:
+                    kn[a] = b
+
+    def access(q, reads, writes):
+        todo = {}
+        for wr, refs in ((False, reads), (True, writes)):
+            for name, lo, hi in refs:
+                for r in recs.get(name, ()):
+                    hit = r[3] != q if name in PSUM else r[0] < hi and lo < r[1] and (r[2] or wr)
+                    if hit and (r[4] not in todo or todo[r[4]][0] < r[5]):
+                        todo[r[4]] = (r[5], r[6])
+        for sem in sorted(todo, key=lambda s: -len(todo[s][1])):
+            need(q, sem, todo[sem][0], todo[sem][1])
+
+    def note(q, sem, n, reads, writes):
+        snap = dict(known[q])
+        for wr, refs in ((False, reads), (True, writes)):
+            for name, lo, hi in refs:
+                old = recs.get(name, [])
+                if name in PSUM:
+                    old = [r for r in old if r[3] != q]
+                elif wr:
+                    old = [r for r in old if not (lo <= r[0] and r[1] <= hi)]
+                else:
+                    old = [r for r in old if r[2] or r[3] != q or not (lo <= r[0] and r[1] <= hi)]
+                old.append((lo, hi, wr, q, sem, n, snap))
+                recs[name] = old
+
+    def op(q, out, ins, emit):
+        reads = [x for r in ins for x in r[1]]
+        access(q, reads, out[1])
+        count[q] += 1
+        emit(qobj[q]).then_inc(T.sem[qsem[q]], 1)
+        note(q, qsem[q], count[q], reads, out[1])
+
+    def R(name, a=0, b=None, st=1):
+        buf, base, w = PACK[name] if name in PACK else (name, 0, SCRATCH[name][1][1])
+        b = w if b is None else b
+        ap = T[buf][:, base + a:base + b] if st == 1 else T[buf][:, base + a:base + b:st]
+        return (ap, [(buf, base + a, base + b)])
+
+    def IND(win, off):
+        return (win[0].indirect(off[0]), win[1] + off[1])
+
+    def sc(x):
+        return x[0] if isinstance(x, tuple) else x
+
+    def tc(out, a):
+        op("v", out, [a], lambda e: e.tensor_copy(out[0], a[0]))
+
+    def tt(out, a, b, o):
+        op("v", out, [a, b], lambda e: e.tensor_tensor(out[0], a[0], b[0], o))
+
+    def ts(out, a, s1, o1, s2=None, o2=None):
+        ins = [a] + [s for s in (s1, s2) if isinstance(s, tuple)]
+        if o2 is None:
+            op("v", out, ins, lambda e: e.tensor_scalar(out[0], a[0], sc(s1), None, o1))
+        else:
+            op("v", out, ins, lambda e: e.tensor_scalar(out[0], a[0], sc(s1), sc(s2), o1, o2))
+
+    def act(out, a):
+        op("s", out, [a], lambda e: e.activation(out[0], a[0], Fn.Copy))
+
+    def actf(out, a, fn, bias, scale):
+        ins = [a] + [s for s in (bias, scale) if isinstance(s, tuple)]
+        op("s", out, ins, lambda e: e.activation(out[0], a[0], fn, bias=sc(bias), scale=sc(scale)))
+
+    def mm(out, l, r, start=True, stop=True):
+        op("t", out, [l, r], lambda e: e.matmul(out[0], l[0], r[0], start, stop))
+
+    def iota(out, pattern, cm):
+        op("g", out, [], lambda e: e.iota(out[0], pattern, 0, cm))
+
+    def fill(out, c):
+        op("v", out, [], lambda e: e.memset(out[0], c))
+
+    def landed(ref, q, sem, n):
+        for name, lo, hi in ref[1]:
+            recs.setdefault(name, []).append((lo, hi, True, q, sem, n, {}))
+
+    def load(q, out, src, sem):
+        qobj[q].dma_start(out[0], src).then_inc(T.sem[sem], 16)
+        landed(out, "dma", sem, 16)
+
+    sends = [0]
+
+    def send(to, out, src, sem):
+        dst = T.cores[to]
+        rid, pid = topo.addr(dst)[:2]
+        access("g", src[1], [])
+        g.remote_dma(out[0], src[0], T.sem[sem], T.sem["sent"], pid, rid, topo.mask(core, dst))
+        sends[0] += len(topo.engines(core, dst))
+
+    load("d", R("a0i"), T.a0[:, :], "la")
+    load("s", R("hi0"), T.hd0[:, :], "lh0")
+    load("s", R("fi0"), T.fl0[:, :], "lf0")
+    load("d", R("sui", 0, 2048), T.su[:, :], "ls")
+    load("s", R("za"), T.z0[:, :], "lz")
+    load("d", R("xw"), T.xs[:, :], "lx")
+    load("d", R("bank", B0, BD), T.gs[:, :], "lg")
+    arrive = {}
+    for t in range(ASKS):
+        asker, asked = T.cores[(rank - 1 - t % (N - 1)) % N], T.cores[(rank + 1 + t % (N - 1)) % N]
+        for n, sem, src in (("qpin", "rp", asker), ("zqin", "rz", asker), ("anin", "ra", asked)):
+            arrive["%s%d" % (sem, t)] = len(topo.engines(src, core))
+            landed(R("%s%d" % (n, t)), "rem", "%s%d" % (sem, t), len(topo.engines(src, core)))
+
+    iota(R("ci"), [[1, 1]], 1)
+    iota(R("ji"), [[1, 256]], 0)
+    iota(R("sui", 2048, 4096), [[1, 2048]], 0)
+    tc(R("pcol"), R("ci"))
+    tc(R("jf"), R("ji"))
+    ts(R("ci2"), R("ci"), 15, Op.bitwise_and)
+    ts(R("ci3"), R("ci"), 4, Op.arith_shift_right)
+    tc(R("p16"), R("ci2"))
+    tc(R("pdiv"), R("ci3"))
+    ts(R("jt"), R("ji"), 15, Op.bitwise_and)
+    tc(R("pat16"), R("jt"))
+    ts(R("mask16"), R("pat16"), R("p16"), Op.is_equal)
+    tc(R("e16"), R("ji", 0, 16))
+    ts(R("jt", 0, 128), R("ji", 0, 128), 4, Op.arith_shift_right)
+    tc(R("qd16"), R("jt", 0, 128))
+    ts(R("boh"), R("qd16"), R("pdiv"), Op.is_equal)
+    ts(R("ob8h"), R("jf", 0, 8), R("pdiv"), Op.is_equal)
+    ts(R("ob8k"), R("ob8h"), 1024.0, Op.mult)
+    ts(R("maskm"), R("pat16"), R("p16"), Op.is_le, 4096.0, Op.mult)
+    ts(R("ob8"), R("jf", 0, 8), R("pdiv"), Op.is_equal)
+    ts(R("idb"), R("jf", 0, 128), R("pcol"), Op.is_equal)
+    ts(R("lanb", 0, 8), R("jf", 0, 8), 0.0, Op.mult, R("pcol"), Op.add)
+    ts(R("lanb", 8, 16), R("lanb", 0, 8), 128.0, Op.add)
+    fill(R("ones"), 1.0)
+    fill(R("zer"), 0.0)
+    for j in range(16):
+        actf(R("hm", 128 * j, 128 * j + 128), R("ones"), Fn.Copy, 0.0, R("mask16", j, j + 1))
+    tc(R("als"), R("a0i"))
+    tt(R("os"), IND(R("als"), R("e16")), R("mask16"), Op.mult)
+
+    def spread(t):
+        mm(R("ps1", 0, 256), R("boh"), R("os"))
+        if t < STEPS:
+            mm(R("ps3", 256, 512), R("boh"), R("os"), True, False)
+            mm(R("ps3", 256, 512), R("idb"), R("maskm"), False, True)
+            act(R("arm"), R("ps3", 256, 512))
+        if t < ASKS:
+            for h in (0, 1):
+                o = R("ps1", 272 + 8 * h, 280 + 8 * h)
+                mm(o, R("os", 128 * h, 128 * h + 128), R("ob8k"), True, False)
+                mm(o, R("idb"), R("lanb", 8 * h, 8 * h + 8), False, True)
+
+    spread(0)
+    for c in range(15):
+        if c != 7:
+            fill(R("eb", 256 * c + 128 * (c >= 8), 272 * c + 16), 0.0)
+    fill(R("bank", 0, B0), 0.0)
+    ts(R("bo"), R("qd16"), R("pdiv"), Op.is_equal)
+    ts(R("rpt"), R("idb"), 512.0, Op.mult)
+    ts(R("cwt"), R("jf", 0, 128), R("pcol"), Op.is_gt)
+    tt(R("cwt"), R("cwt"), R("rpt"), Op.subtract)
+    ts(R("tri"), R("cwt"), 0.25, Op.mult)
+    fill(R("quar"), 0.25)
+    ts(R("ge8"), R("p16"), 8.0, Op.is_ge)
+    ts(R("e8f"), R("jf", 0, 8), 2.0, Op.mult, R("ge8"), Op.add)
+    tc(R("e8"), R("e8f"))
+    ts(R("jt", 0, 128), R("ji", 0, 128), 7, Op.bitwise_and)
+    ts(R("patc8"), R("jt", 0, 128), -32.0, Op.add)
+    ts(R("jt", 0, 64), R("ji", 0, 64), 3, Op.arith_shift_right)
+    ts(R("gm"), R("jt", 0, 64), R("pdiv"), Op.is_equal)
+    ts(R("cwt"), R("hi0"), 33.0, Op.mult)
+    ts(R("cw"), R("fi0"), 32.0, Op.mult)
+    tt(R("cw"), R("cw"), R("cwt"), Op.add)
+
+    def late_constants():
+        ts(R("dump"), R("jf", 0, 8), 16.0, Op.mult, R("p16"), Op.add)
+        ts(R("dump"), R("dump"), float(16 + 16384 - B0), Op.add)
+        ts(R("is0"), R("pcol"), 0.0, Op.is_equal)
+        ts(R("rowc"), R("pat16"), R("is0"), Op.mult)
+        ts(R("om16"), R("ob8"), -16.0, Op.mult)
+        ts(R("idn"), R("idb"), -1.0, Op.mult)
+        ts(R("o16"), R("ob8"), 16.0, Op.mult)
+        ts(R("o32"), R("ob8"), 32.0, Op.mult)
+        ts(R("i128"), R("jf", 0, 128), 0.0, Op.add)
+        ts(R("rpt"), R("pat16", 0, 128), 1.0, Op.add)
+        tt(R("rpt"), R("rpt"), R("bo"), Op.mult)
+        ts(R("rp"), R("rpt"), -1.0, Op.add)
+        ts(R("odd"), R("p16"), 2.0, Op.mult, 1.0, Op.add)
+        ts(R("bow"), R("bo"), R("odd"), Op.mult)
+        ts(R("l16"), R("pcol"), 16.0, Op.mult)
+
+    z = ["za", "zb"]
+
+    def centres(a, b):
+        for k in range(a, b):
+            act(R("cc", 1024 * k, 1024 * k + 1024), IND(R("xw"), R("suu", 64 * k, 64 * k + 64)))
+
+    def differences():
+        for c in range(16):
+            actf(R("rd", 128 * c, 128 * c + 128), R("i128"), Fn.Abs, R("alof", c, c + 1), 1.0)
+
+    def head(t):
+        tc(R("ai"), R("als"))
+        tc(R("alu"), R("als"))
+        ts(R("alo"), R("ai"), 127, Op.bitwise_and)
+        if t > 0:
+            tc(R("suu"), IND(R("sui", 0, 2048), R("alu")))
+        tc(R("alou"), R("alo"))
+        if t > 0:
+            centres(0, 2)
+        tc(R("arow"), R("ps1", 0, 256))
+        mm(R("ps2", 0, 16), R("ones"), R("zer"), True, False)
+        yield
+        act(R("gc_"), IND(R("cw"), R("alou")))
+        if t > 0:
+            centres(2, 4)
+        yield
+        for c in range(15):
+            ts(R("eb", 272 * c + 16, 256 * c + 256), R("arow", 16 * c + 16, 256), R("als", c, c + 1), Op.is_equal)
+            for h in (0, 1) if c < 7 else (1,):
+                mm(R("ps2", 8 * h, 8 * h + 8), R("eb", 256 * c + 128 * h, 256 * c + 128 * h + 128), R("ob8"), False, c == 14)
+            yield
+            if c == 6:
+                tt(R("dg"), IND(R("als"), R("e16")), R("arm"), Op.is_equal)
+                for h in (0, 1):
+                    mm(R("ps2", 8 * h, 8 * h + 8), R("dg", 128 * h, 128 * h + 128), R("ob8"), False, False)
+                yield
+        if t == 0:
+            tc(R("suu"), IND(R("sui", 0, 2048), R("alu")))
+            centres(0, 4)
+        tt(R("gmk"), IND(R("hm"), R("alu")), R("gc_"), Op.mult)
+        for h in (0, 1):
+            mm(R("ps7", 8 * h, 8 * h + 8), R("gmk", 128 * h, 128 * h + 128), R("ob8h"))
+        yield
+        ts(R("al4"), R("als"), 4.0, Op.mult, float(B0), Op.add)
+        ts(R("ahi"), R("ai"), 7, Op.arith_shift_right)
+        yield
+        tc(R("cdi"), R("ps7", 0, 16))
+        ts(R("alof"), R("alo"), -1.0, Op.mult)
+        ts(R("hh"), R("cdi"), 31, Op.bitwise_and)
+        ts(R("tl"), R("cdi"), 5, Op.arith_shift_right)
+        tt(R("xx"), R("hh"), R("ps2", 0, 16), Op.add)
+        tc(R("ahif"), R("ahi"))
+        if t > 0:
+            differences()
+        yield
+        tt(R("d1"), R("xx"), R("tl"), Op.subtract)
+        ts(R("x3"), R("xx"), 3, Op.bitwise_and)
+        ts(R("blk"), R("d1"), 0.0, Op.is_ge, 4.0, Op.mult)
+        mm(R("ps2", 32, 40), R("tri"), R("blk", 0, 8))
+        mm(R("ps2", 40, 48), R("tri"), R("blk", 8, 16), True, False)
+        mm(R("ps2", 40, 48), R("quar"), R("blk", 0, 8), False, True)
+        ts(R("s2"), R("d1"), 4.0, Op.is_lt)
+        tt(R("y1"), R("x3"), R("blk"), Op.add)
+        if t < ASKS:
+            ts(R("pv1"), R("x3"), 256.0, Op.mult)
+            tt(R("pv2"), R("pv1"), R("ps1", 272, 288), Op.add)
+        yield
+        ts(R("s1"), R("ps2", 32, 48), -384.0, Op.is_lt, 8.0, Op.mult)
+        tt(R("p8"), R("s1"), R("s2"), Op.mult)
+        tt(R("yv"), R("y1"), R("p8"), Op.add)
+        yield
+        tt(R("ay"), IND(R("yv"), R("e16")), R("mask16"), Op.mult)
+        for h in (0, 1):
+            mm(R("ps2", 48 + 8 * h, 56 + 8 * h), R("ay", 128 * h, 128 * h + 128), R("ob8"))
+        yield
+
+    def offsets(t):
+        ts(R("pp"), R("ps2", 48, 64), 4.0, Op.is_lt)
+        tt(R("oq"), R("ps2", 48, 64), R("al4"), Op.add)
+        tt(R("offu"), R("oq"), R("pp"), Op.mult)
+        yield
+        ts(R("sb"), R("ps2", 48, 64), 4.0, Op.is_ge, 2048.0, Op.mult)
+        tt(R("sou"), R("sb"), R("als"), Op.add)
+        ts(R("pt"), R("ps2", 48, 64), 8.0, Op.is_ge, 32.0, Op.mult)
+        tt(R("wl"), R("pp"), R("pt"), Op.add)
+        yield
+
+    made = [0]
+
+    def onehot(c):
+        if c >= made[0]:
+            made[0] = c + 1
+            ts(R("lh", 128 * c, 128 * c + 128), R("rp"), R("ahif", c, c + 1), Op.is_equal, R("wl", c, c + 1), Op.mult)
+
+    def onehots(n):
+        for _ in range(n):
+            if made[0] < 16:
+                onehot(made[0])
+
+    def ask(t):
+        to = (rank + 1 + t % (N - 1)) % N
+        tc(R("ri"), R("ps2", 32, 48))
+        ts(R("pv3"), R("p8"), 524288.0, Op.mult)
+        tt(R("pv"), R("pv2"), R("pv3"), Op.add)
+        ts(R("rlo"), R("ri"), 15, Op.bitwise_and)
+        ts(R("rhi"), R("ri"), 4, Op.arith_shift_right)
+        yield
+        tt(R("cb"), IND(R("rhi"), R("e8")), R("patc8"), Op.is_equal)
+        tt(R("ca"), IND(R("rlo"), R("e16")), R("pat16"), Op.is_equal)
+        tt(R("cb2"), IND(R("pv"), R("e8")), R("cb"), Op.mult)
+        for h in (0, 1):
+            mm(R("ps5", 384, 448), R("ca", 128 * h, 128 * h + 128), R("cb2", 64 * h, 64 * h + 64), h == 0, h == 1)
+        yield
+        if t == 0:
+            late_constants()
+        else:
+            onehots(8)
+        qp = R("qp%d" % t)
+        tt(R("cm"), R("ps5", 384, 448), R("gm"), Op.mult)
+        tt(R("c1"), R("cm", 0, 32), R("cm", 32, 64), Op.add)
+        tt(R("c2"), R("c1", 0, 16), R("c1", 16, 32), Op.add)
+        tt(qp, R("c2", 0, 8), R("c2", 8, 16), Op.add)
+        send(to, R("qpin%d" % t), qp, "rp%d" % t)
+        ts(R("lni"), qp, 255, Op.bitwise_and)
+        tc(R("lnu"), R("lni"))
+        act(R("zq%d" % t), IND(R(z[0]), R("lnu")))
+        send(to, R("zqin%d" % t), R("zq%d" % t), "rz%d" % t)
+        yield
+        ts(R("v1"), qp, 8, Op.arith_shift_right)
+        tt(R("v2"), R("v1"), R("dump"), Op.max)
+        ts(R("offr%d" % t), R("v2"), float(B0 - 16384), Op.add)
+        yield
+
+    def pops(t):
+        if t > 0:
+            wi, of, src = R("bank"), R("offr%d" % (t - 1)), R("anin%d" % (t - 1))
+            op("v", (None, wi[1]), [src, of], lambda e: e.tensor_copy(wi[0].indirect(of[0]), src[0]))
+        tt(R("zs"), IND(R("bank"), R("offu")), R(z[0]), Op.add)
+        ts(R(z[1]), R("zs"), 0.0, Op.max, 255.0, Op.min)
+        mm(R("ps3", 0, 256), R("ones"), R("rowc"), True, False)
+        for h in (0, 1):
+            for m in range(16 - NS):
+                mm(R("ps3", 128 * h + m, 128 * h + 128, 16), R("cc", 2048 * h + m, 2048 * h + 2048, 16), R("om16"), False, False)
+        for m in range(16 - NS, 16):
+            mm(R(SBANK[m % NS], 0, 256), R("idb"), R("cc", m, 4096, 16), True, False)
+        mm(R("ps4", 0, 256), R("idb"), R(z[1]))
+        for m in range(16 - NS, 16):
+            mm(R(SBANK[m % NS], 0, 256), R("idn"), R(z[1]), False, True)
+            actf(R("mx", 256 * m, 256 * m + 256), R(SBANK[m % NS], 0, 256), Fn.Abs, 0.0, 1.0)
+        tc(R("sp"), IND(R("sui"), R("sou")))
+        if t == 0:
+            differences()
+        for c in range(0, 16, 4):
+            actf(R("rh", 128 * c, 128 * c + 512), R("rd", 128 * c, 128 * c + 512), Fn.Relu, 1.0, -1.0)
+
+    def update(t):
+        for c in range(16):
+            onehot(c)
+            mm(R("ps5", 128, 256), R("lh", 128 * c, 128 * c + 128), R("rh", 128 * c, 128 * c + 128), c == 0, c == 15)
+            yield
+
+    def table():
+        tt(R("cw"), R("cw"), R("ps5", 128, 256), Op.add)
+
+    def dist(t):
+        for m in range(16 - NS):
+            tt(R("mx", 256 * m, 256 * m + 256), R("cc", m, 4096, 16), R("ps4", 0, 256), Op.max)
+            for h in (0, 1):
+                a = 256 * m + 128 * h
+                mm(R("ps3", 128 * h + m, 128 * h + 128, 16), R("mx", a, a + 128), R("o32"), False, False)
+            if m == 3:
+                for n in range(16 - NS, 16):
+                    for h in (0, 1):
+                        mm(R("ps3", 128 * h + n, 128 * h + 128, 16), R(z[1], 128 * h, 128 * h + 128), R("o16"), False, False)
+            if m == 15 - NS:
+                for n in range(16 - NS, 16):
+                    for h in (0, 1):
+                        a = 256 * n + 128 * h
+                        mm(R("ps3", 128 * h + n, 128 * h + 128, 16), R("mx", a, a + 128), R("o16"), False, h == 1 and n == 15)
+
+    def choose(t):
+        tc(R("ko"), R("ps3", 1, 256, 2))
+        tt(R("k1"), R("ps3", 0, 256, 2), R("ko"), Op.min)
+        act(R("ks"), R("ps3", 0, 256))
+        yield
+        src, w = "k1", 128
+        for d in ("k2", "k3", "k4"):
+            tt(R(d), R(src, 0, w, 2), R(src, 1, w, 2), Op.min)
+            src, w = d, w // 2
+            yield
+        tt(R("oh"), IND(R("k4"), R("e16")), R("ks"), Op.is_equal)
+        for h in (0, 1):
+            mm(R("ps0", 256 + 128 * h, 384 + 128 * h), R("oh", 128 * h, 128 * h + 128), R("idb"))
+        for _ in range(4):
+            yield
+        tt(R("os"), R("ps0", 256, 512), R("sp"), Op.mult)
+        if t + 1 < STEPS:
+            for h in (0, 1):
+                mm(R("ps0", 128 * h, 128 * h + 128), R("os", 128 * h, 128 * h + 128), R("boh"))
+            for _ in range(4):
+                yield
+            tt(R("aa"), R("ps0", 0, 256), R("mask16"), Op.mult)
+            for h in (0, 1):
+                mm(R("ps0", 256 + 8 * h, 264 + 8 * h), R("aa", 128 * h, 128 * h + 128), R("ob8h"))
+        spread(t + 1)
+        for _ in range(4):
+            yield
+        if t + 1 < STEPS:
+            tc(R("als"), R("ps0", 256, 272))
+        else:
+            act(R("arf"), R("ps1", 0, 256))
+        yield
+
+    def answer(t):
+        to = (rank - 1 - t % (N - 1)) % N
+        qpin, zqin = R("qpin%d" % t), R("zqin%d" % t)
+        ts(R("qa"), qpin, 10, Op.arith_shift_right, 2047, Op.bitwise_and)
+        tc(R("qau"), R("qa"))
+        act(R("goal"), IND(R("xw"), R("qau")))
+        mm(R("ps5", 0, 128), R("bow"), zqin)
+        mm(R("ps4", 256, 384), R("idn"), zqin, True, False)
+        mm(R("ps4", 256, 384), R("idb"), R("goal"), False, True)
+        tc(R("ui"), R("ps5", 0, 128))
+        yield
+        ts(R("uu"), R("ui"), 4095, Op.bitwise_and)
+        yield
+        tt(R("usq"), R("uu"), R("uu"), Op.mult)
+        ts(R("um"), R("uu"), R("odd"), Op.mult)
+        yield
+        ts(R("uv"), R("usq"), 5, Op.arith_shift_right)
+        yield
+        tt(R("us"), R("um"), R("uv"), Op.add)
+        yield
+        ts(R("ux"), R("us"), 8191, Op.bitwise_and)
+        yield
+        tc(R("cou"), R("ux"))
+        for k in range(2):
+            act(R("cand", 1024 * k, 1024 * k + 1024), IND(R("bank", B0, BD), R("cou", 64 * k, 64 * k + 64)))
+        yield "gathering"
+        mm(R("ps6", 0, 128), R("ones"), R("rowc", 0, 128), True, False)
+        for m in range(16):
+            mm(R("ps6", m, 128, 16), R("cand", m, 2048, 16), R("om16"), False, False)
+        for m in range(16):
+            tt(R("mq", 128 * m, 128 * m + 128), R("cand", m, 2048, 16), R("ps4", 256, 384), Op.max)
+            mm(R("ps6", m, 128, 16), R("mq", 128 * m, 128 * m + 128), R("o32"), False, m == 15)
+            yield
+        tc(R("q0"), R("ps6", 1, 128, 2))
+        tt(R("q1"), R("ps6", 0, 128, 2), R("q0"), Op.min)
+        src, w = "q1", 64
+        for d in ("q2", "q3", "q4"):
+            yield
+            tt(R(d), R(src, 0, w, 2), R(src, 1, w, 2), Op.min)
+            src, w = d, w // 2
+        yield
+        ts(R("q5"), R("q4"), 15, Op.bitwise_and)
+        yield
+        ts(R("q6"), R("q5"), R("l16"), Op.add)
+        yield
+        tt(R("aq"), IND(R("q6"), R("e16", 0, 8)), R("mask16", 0, 128), Op.mult)
+        mm(R("ps5", 448, 456), R("aq"), R("ob8h"))
+        yield
+        tc(R("seu"), R("ps5", 448, 456))
+        yield
+        tc(R("an%d" % t), IND(R("cand"), R("seu")))
+        send(to, R("anin%d" % t), R("an%d" % t), "ra%d" % t)
+        yield
+
+    def finish(t):
+        for _ in update(t):
+            yield
+        for _ in range(3):
+            yield
+        table()
+        ts(R("w1"), R("cw"), 1.0, Op.mult)
+        yield
+        ts(R("w2"), R("w1"), 31, Op.bitwise_and)
+        ts(R("w3"), R("w1"), 5, Op.arith_shift_right)
+        ts(R("w4"), R("w1"), 3, Op.bitwise_and)
+        yield
+        tt(R("oyf"), R("w3"), R("w2"), Op.subtract)
+        tc(R("ohf"), R("w4"))
+        yield
+
+    def run(gen):
+        for _ in gen:
+            pass
+
+    def until(x, tag):
+        for y in x:
+            yield
+            if y == tag:
+                return
+
+    def weave(*gens):
+        gens = list(gens)
+        while gens:
+            for x in list(gens):
+                if x in gens and next(x, "end") == "end":
+                    gens = [y for y in gens if y is not x]
+
+    nothing = iter(())
+    run(head(0))
+    for t in range(STEPS):
+        asks, more = t < ASKS, t + 1 < STEPS
+        weave(offsets(t), ask(t) if asks else nothing)
+        pops(t)
+        dist(t)
+        ch, ans = choose(t), answer(t) if asks else nothing
+        onehots(4)
+        next(ch)
+        if more:
+            weave(until(ans, "gathering"), ch, update(t))
+            nxt = head(t + 1)
+            next(nxt)
+            table()
+            for _ in range(5):
+                next(nxt)
+            weave(ans, nxt, ans)
+        else:
+            weave(finish(t), ch)
+        made[0] = 0
+        z.reverse()
+
+    outs = [0]
+
+    def store(dst, ap, ref):
+        access("d", ref[1], [])
+        g.sync.dma_start(dst, ap).then_inc(T.sem["sout"], 16)
+        outs[0] += 16
+
+    store(T.yz[:, :], R(z[0])[0], R(z[0]))
+    buf, base, w = PACK["arf"]
+    store(T.ya[:, :], T[buf][0:128:16, base:base + w], R("arf"))
+    store(T.yf[:, :], R("oyf")[0], R("oyf"))
+    store(T.yh[:, :], R("ohf")[0], R("ohf"))
+    g.sync.wait_ge(T.sem["sout"], outs[0])
+    for q in "vstg":
+        need("g", qsem[q], count[q], {})
+    for s in LOADS:
+        need("g", s, 16, {})
+    for s in sorted(arrive):
+        need("g", s, arrive[s], {})
+    g.wait_ge(T.sem["sent"], sends[0])

@@ -2,29 +2,30 @@ from concourse.mybir import AluOpType as Op, ActivationFunctionType as Fn
 
 STEPS = 4
 ASKS = STEPS - 1
-NS = 4
-SBANK = ["ps6", "ps7", "ps0", "ps1"]
-B0, BD = 144, 8336
+NS = [6, 6, 6, 6]
+B0, BD = 192, 8384
+X0 = B0 // 4
 PSUM = ["ps%d" % i for i in range(8)]
 SCRATCH = {}
 for _n in PSUM:
     SCRATCH[_n] = ("psum", [128, 512], "float32")
-WIDE = {"xw": (2048, "bfloat16"), "sui": (4096, "int32"), "bank": (BD, "bfloat16"), "hm": (2048, "bfloat16"), "cc": (4096, "bfloat16"),
-        "mx": (4096, "bfloat16"), "cand": (2048, "bfloat16"), "mq": (2048, "bfloat16"), "eb": (4096, "bfloat16"), "lh": (2048, "bfloat16"),
-        "rh": (2048, "bfloat16"), "rd": (2048, "bfloat16"), "za": (256, "bfloat16"), "zb": (256, "bfloat16")}
+WIDE = {"xw": (X0 + 2048, "bfloat16"), "sui": (4096, "int32"), "bank": (BD, "bfloat16"), "cc": (4096, "bfloat16"), "mx": (4096, "bfloat16"),
+        "cand": (2048, "bfloat16"), "mq": (2048, "bfloat16"), "eb": (4096, "bfloat16"), "hot": (2048, "bfloat16")}
+for _t in range(STEPS + 1):
+    WIDE["zz%d" % _t] = (256, "bfloat16")
 for _n, (_w, _d) in WIDE.items():
     SCRATCH[_n] = ("sbuf", [128, _w], _d)
 NARROW = {
-    "float32": "pcol 1 p16 1 pdiv 1 odd 1 l16 1 ge8 1 is0 1 jf 256 pat16 256 patc8 128 mask16 256 qd16 128 gm 64 rpt 128 cw 128 cwt 128 e8f 8 dump 8 "
-               "als 16 al4 16 alof 16 ahif 16 arm 256 gc_ 256 d1 16 s1 16 s2 16 y1 16 p8 16 yv 16 oq 16 pp 16 sb 16 pt 16 wl 16 ks 256 ko 128 k1 128 "
-               "k2 64 k3 32 k4 16 arf 256 pv1 16 pv2 16 pv3 16 pv 16 ca 256 cb 128 cb2 128 cm 64 c1 32 c2 16 v2 8 um 128 q0 64 q1 64 q2 32 q3 16 "
-               "q6 8 ohf 128 oyf 128",
-    "int32": "ci 1 ci2 1 ci3 1 ji 256 jt 256 hi0 128 fi0 128 a0i 16 ai 16 alo 16 ahi 16 cdi 16 hh 16 tl 16 xx 16 x3 16 ri 16 rlo 16 rhi 16 lni 8 v1 8 qa 8 "
-             "ui 128 uu 128 usq 128 uv 128 us 128 ux 128 q4 8 q5 8 w1 128 w2 128 w3 128 w4 128",
-    "uint16": "e16 16 e8 8 alu 16 alou 16 suu 256 offu 16 sou 16 lnu 8 qau 8 cou 128 seu 8",
-    "bfloat16": "bo 128 bow 128 ob8 8 o16 8 o32 8 om16 8 idb 128 idn 128 tri 128 ones 128 quar 128 rp 128 i128 128 maskm 256 lanb 16 rowc 256 zer 16 dg 256 "
-                "blk 16 ay 256 zs 256 oh 256 goal 128",
-    "float16": "boh 128 ob8h 8 ob8k 8 arow 256 os 256 gmk 256 sp 256 aa 256 aq 128"}
+    "float32": "pcol 1 p16 1 pdiv 1 odd 1 odd32 1 p8 1 is0 1 jf 256 pat16 256 patc 128 mask16 256 qd16 128 tmp 256 tm2 256 dump 8 idf 128 id4 128 "
+               "als 16 sl 256 y 16 put 16 w7 16 w 16 pv 16 ca 256 cb 128 cb2 128 qs 64 alof 16 lk 256 sp 256 ksc 256 kmin 256 kq 128 arf 256 "
+               "ohf 128 oyf 128",
+    "int32": "ci 1 ci2 1 ci3 1 ci4 1 ji 256 jt 256 hi0 128 fi0 128 a0i 16 ail 16 alo 16 ait 16 ahit 16 alot 16 lki 16 hfi 32 xi 16 x3 16 ri 16 rlo 16 "
+             "rhi 16 v1 8 dq 16 ui 128 uu 128 pr 128 ux 128 ki 8 mi 8 w1 128 w2 128 w3 128",
+    "uint16": "e16 16 et16 16 e15 16 e8 8 alu 16 alou 16 suu 256 offu 16 sou 16 dqu 16 cou 128 seu 8",
+    "bfloat16": "bo 128 bow 128 ob8 8 ob24 24 om8 8 o16 8 o32 8 om16 8 idb 128 idn 128 id256 128 idk 128 idm 128 tri 128 ones 128 quar 128 i128 128 "
+                "negm 256 rst 256 big 128 keep 64 gneg 64 lanb 16 rowc 128 crow 48 brow 16 q16 8 bs 128 dg 256 bn 32 ay 256 zs 256 oh 256 goal 128 "
+                "zq 128 aq 128 gc_ 256 ah 256 hfb 32 cw 128 ut 128",
+    "float16": "boh 128 ob8h 8 ob4h 8 arow 256 os 256"}
 PACK = {}
 for _d, _t in NARROW.items():
     _at, _f = 0, _t.split()
@@ -33,11 +34,74 @@ for _d, _t in NARROW.items():
         _at += -(-int(_w) // 16) * 16
     SCRATCH["pk_" + _d] = ("sbuf", [128, _at], _d)
 for _t in range(ASKS):
-    for _n, _w, _d in (("qp", 8, "int32"), ("zq", 128, "bfloat16"), ("an", 128, "bfloat16"),
-                       ("qpin", 8, "int32"), ("zqin", 128, "bfloat16"), ("anin", 128, "bfloat16"), ("offr", 8, "uint16")):
+    for _n, _w, _d in (("qp", 8, "int32"), ("an", 128, "bfloat16"), ("qpin", 8, "int32"), ("zin", 256, "bfloat16"), ("anin", 128, "bfloat16"),
+                       ("offr", 8, "uint16")):
         SCRATCH["%s%d" % (_n, _t)] = ("sbuf", [128, _w], _d)
 LOADS = ["la", "ls", "lx", "lh0", "lf0", "lz", "lg"]
 SEMAPHORES = ["sv", "ss", "st", "sg", "sent", "sout"] + LOADS + ["%s%d" % (n, t) for t in range(ASKS) for n in ("rp", "rz", "ra")]
+
+GATHER, SCATTER, LEAST, WAKE, HOP, DMA, BYTES = 1.56, 3.8, 64, 130, 1800, 1500, 200
+TENSOR, PATIENCE, SWEEPS = 1.0, 0.5, 6
+ORDER = []
+
+
+def plan(ops):
+    n = len(ops)
+    succ = [[] for _ in ops]
+    for i, o in enumerate(ops):
+        for p in o["pred"]:
+            succ[p].append(i)
+
+    def lag(p, i):
+        return ops[p]["cost"] + ops[p]["late"] + (0 if ops[p]["q"] == ops[i]["q"] == "t" else WAKE)
+
+    def sweep(before, after, gap, ready, way):
+        left = [len(x) for x in before]
+        pool = {q: [] for q in "vstgd"}
+        free = {q: 0.0 for q in pool}
+        for i in range(n):
+            if not left[i]:
+                pool[ops[i]["q"]].append(i)
+        order, end = [], [0.0] * n
+        while len(order) < n:
+            best = None
+            for q, L in pool.items():
+                if L:
+                    now = max(free[q], min(ready[i] for i in L))
+                    pick = max((i for i in L if ready[i] <= now), key=lambda i: (way[i], -i))
+                    soon = [i for i in L if way[i] > way[pick] and ready[i] < now + PATIENCE * ops[pick]["cost"]]
+                    if soon:
+                        pick = max(soon, key=lambda i: (way[i], -i))
+                    at = max(now, ready[pick])
+                    if best is None or at < best[0]:
+                        best = (at, pick)
+            at, i = best
+            q = ops[i]["q"]
+            pool[q].remove(i)
+            free[q] = end[i] = at + ops[i]["cost"]
+            order.append(i)
+            for s in after[i]:
+                ready[s] = max(ready[s], at + gap(i, s))
+                left[s] -= 1
+                if not left[s]:
+                    pool[ops[s]["q"]].append(s)
+        return order, end
+
+    pred = [o["pred"] for o in ops]
+    way = [0.0] * n
+    for i in range(n - 1, -1, -1):
+        way[i] = max([lag(i, s) + way[s] for s in succ[i]] + [ops[i]["cost"] + ops[i]["late"]])
+    best = None
+    for _ in range(SWEEPS):
+        for i in range(n):
+            if ops[i]["sem"] and not pred[i]:
+                way[i] = 1e9 - i
+        order, end = sweep(pred, succ, lag, [0.0] * n, way)
+        total = max(end[i] + ops[i]["late"] for i in range(n))
+        if best is None or total < best[0]:
+            best = (total, order)
+        way = sweep(succ, pred, lambda s, p: ops[s]["cost"] + lag(p, s) - ops[p]["cost"], [0.0 if succ[i] else float(ops[i]["late"]) for i in range(n)], end)[1]
+    return best[1]
 
 
 def rank_program(g, core, T, topo):
@@ -46,10 +110,404 @@ def rank_program(g, core, T, topo):
         return
     N = len(T.cores)
     qobj = {"v": g.vector, "s": g.scalar, "t": g.tensor, "g": g, "d": g.sync}
-    qsem = {"v": "sv", "s": "ss", "t": "st", "g": "sg"}
-    count = {"v": 0, "s": 0, "t": 0, "g": 0}
-    known = {q: {} for q in qobj}
+    ops = []
     recs = {}
+    turn = {}
+
+    def op(q, out, ins, emit, cost, late=0, sem=None):
+        i, pred = len(ops), set()
+        refs = [(False, x) for r in ins for x in r[1]] + [(True, x) for x in out[1]]
+        for wr, (name, lo, hi) in refs:
+            for r in recs.get(name, ()):
+                if r[0] < hi and lo < r[1] and (r[2] or wr):
+                    pred.add(r[3])
+        for name in sorted({x[0] for _, x in refs if x[0] in PSUM}):
+            has, cur, prev = turn.get(name, (q, [], []))
+            if has != q:
+                cur, prev = [], cur
+            pred.update(prev + (cur[-1:] if q == "t" else []))
+            turn[name] = (q, cur + [i], prev)
+        for wr, (name, lo, hi) in refs:
+            old = recs.get(name, [])
+            if wr:
+                old = [r for r in old if not (lo <= r[0] and r[1] <= hi)]
+            recs[name] = old + [(lo, hi, wr, i)]
+        pred.discard(i)
+        ops.append({"q": q, "pred": sorted(pred), "emit": emit, "cost": cost, "late": late, "sem": sem})
+
+    def R(name, a=0, b=None, st=1):
+        buf, base, w = PACK[name] if name in PACK else (name, 0, SCRATCH[name][1][1])
+        b = w if b is None else b
+        ap = T[buf][:, base + a:base + b] if st == 1 else T[buf][:, base + a:base + b:st]
+        size = 0 if buf in PSUM else 4 if SCRATCH[buf][2].endswith("32") else 2
+        return (ap, [(buf, base + a, base + b)], -(-(b - a) // st), size, False)
+
+    def C(name, j):
+        return R(name, j, j + 1)
+
+    def IND(win, off):
+        return (win[0].indirect(off[0]), win[1] + off[1], 16 * off[2], win[3], True)
+
+    def sc(x):
+        return x[0] if isinstance(x, tuple) else x
+
+    def cycles(out, ins, rate):
+        if ins[0][4]:
+            return LEAST + GATHER * out[2]
+        if rate is None:
+            rate = 0.5 if all(x[3] == 2 for x in [out] + ins) else 1
+        return max(LEAST, rate * out[2])
+
+    def tc(out, a):
+        op("v", out, [a], lambda e: e.tensor_copy(out[0], a[0]), cycles(out, [a], None))
+
+    def tt(out, a, b, o):
+        op("v", out, [a, b], lambda e: e.tensor_tensor(out[0], a[0], b[0], o), cycles(out, [a], 2 if a[3] and b[3] else 1))
+
+    def ts(out, a, s1, o1, s2=None, o2=None):
+        ins = [a] + [s for s in (s1, s2) if isinstance(s, tuple)]
+        args = (out[0], a[0], sc(s1), None, o1) if o2 is None else (out[0], a[0], sc(s1), sc(s2), o1, o2)
+        op("v", out, ins, lambda e: e.tensor_scalar(*args), cycles(out, [a], None))
+
+    def scan(out, a, b, o0, o1):
+        op("v", out, [a, b], lambda e: e.tensor_tensor_scan(out[0], a[0], b[0], 0.0, o0, o1), cycles(out, [a, b], None))
+
+    def act(out, a, fn=Fn.Copy):
+        op("s", out, [a], lambda e: e.activation(out[0], a[0], fn), cycles(out, [a], 1))
+
+    def mm(out, l, r, start=True, stop=True):
+        op("t", out, [l, r], lambda e: e.matmul(out[0], l[0], r[0], start, stop), TENSOR * max(LEAST, r[2]) * (4 if l[3] == 4 else 1))
+
+    def iota(out, pattern, cm):
+        op("g", out, [], lambda e: e.iota(out[0], pattern, 0, cm), 160 + 2 * out[2])
+
+    def fill(out, c):
+        op("v", out, [], lambda e: e.memset(out[0], c), cycles(out, [out], None))
+
+    loaded = [DMA]
+
+    def load(q, out, src, sem):
+        loaded[0] += 128 * out[2] * out[3] / BYTES
+        op(q, out, [], lambda e: e.dma_start(out[0], src), LEAST, loaded[0], (sem, 16))
+
+    sends, arrive = [0], {}
+
+    def send(to, frm, out, src, sem):
+        dst, peer = T.cores[(rank + to) % N], T.cores[(rank - to) % N]
+        rid, pid = topo.addr(dst)[:2]
+        arrive[sem] = len(topo.engines(peer, core))
+        sends[0] += len(topo.engines(core, dst))
+        op("g", out, [src], lambda e: e.remote_dma(out[0], src[0], T.sem[sem], T.sem["sent"], pid, rid, topo.mask(core, dst)),
+           HOP / 4, HOP + 128 * out[2] * out[3] / 80, (sem, arrive[sem]))
+
+    outs = [0]
+
+    def store(q, dst, ap, ref):
+        outs[0] += 16
+        op(q, (None, []), [ref], lambda e: e.dma_start(dst, ap), LEAST, DMA, ("sout", 16))
+
+    load("d", R("a0i"), T.a0[:, :], "la")
+    load("s", R("hi0"), T.hd0[:, :], "lh0")
+    load("s", R("fi0"), T.fl0[:, :], "lf0")
+    load("s", R("zz0"), T.z0[:, :], "lz")
+    load("d", R("sui", 0, 2048), T.su[:, :], "ls")
+    load("d", R("xw", X0), T.xs[:, :], "lx")
+    load("d", R("bank", B0), T.gs[:, :], "lg")
+
+    iota(R("ci"), [[1, 1]], 1)
+    iota(R("ji"), [[1, 256]], 0)
+    iota(R("sui", 2048, 4096), [[1, 2048]], 0)
+    tc(R("pcol"), R("ci"))
+    tc(R("jf"), R("ji"))
+    for name, tmp, c, o in (("p16", "ci2", 15, Op.bitwise_and), ("pdiv", "ci3", 4, Op.arith_shift_right), ("p8", "ci4", 7, Op.bitwise_and)):
+        ts(R(tmp), R("ci"), c, o)
+        tc(R(name), R(tmp))
+    ts(R("jt"), R("ji"), 15, Op.bitwise_and)
+    tc(R("pat16"), R("jt"))
+    ts(R("mask16"), R("pat16"), R("p16"), Op.is_equal)
+    tc(R("e16"), R("ji", 0, 16))
+    ts(R("e15"), R("jf", 0, 16), 16.0, Op.mult, 15.0, Op.add)
+    for h in (0, 1):
+        ts(R("et16", 8 * h, 8 * h + 8), R("jf", 0, 8), 2.0, Op.mult, float(h), Op.add)
+        ts(R("e8", 4 * h, 4 * h + 4), R("jf", 0, 4), 0.0, Op.mult, R("p8"), Op.add)
+        ts(R("e8", 4 * h, 4 * h + 4), R("e8", 4 * h, 4 * h + 4), 2.0, Op.mult, float(h), Op.add)
+        ts(R("lanb", h, 16, 2), R("jf", 0, 8), 0.0, Op.mult, R("pcol"), Op.add)
+    ts(R("lanb", 1, 16, 2), R("lanb", 1, 16, 2), 128.0, Op.add)
+    ts(R("jt", 0, 128), R("ji", 0, 128), 4, Op.arith_shift_right)
+    tc(R("qd16"), R("jt", 0, 128))
+    ts(R("boh"), R("qd16"), R("pdiv"), Op.is_equal)
+    ts(R("bo"), R("qd16"), R("pdiv"), Op.is_equal)
+    for name, c in (("ob8h", 1), ("ob4h", 4), ("ob8", 1), ("om8", -0.125), ("o16", 16), ("o32", 32), ("om16", -16)):
+        ts(R(name), R("jf", 0, 8), R("pdiv"), Op.is_equal, float(c), Op.mult)
+    for k in range(3):
+        ts(R("ob24", 8 * k, 8 * k + 8), R("jf", 0, 8), R("pdiv"), Op.is_equal)
+    for name, c in (("idb", 1), ("idn", -1), ("id256", 256), ("idk", 16384), ("idm", -0.0625), ("idf", 1), ("id4", 4)):
+        ts(R(name), R("jf", 0, 128), R("pcol"), Op.is_equal, float(c), Op.mult)
+    ts(R("negm"), R("pat16"), R("p16"), Op.not_equal, -4096.0, Op.mult)
+    ts(R("rst"), R("pat16"), 0.0, Op.is_equal, -8192.0, Op.mult)
+    ts(R("big"), R("pat16", 0, 128), 0.0, Op.is_equal, 2.0 ** 20, Op.mult)
+    ts(R("jt", 128, 192), R("ji", 0, 64), 7, Op.bitwise_and)
+    ts(R("keep"), R("jt", 128, 192), 0.0, Op.not_equal)
+    ts(R("gneg"), R("jt", 128, 192), R("pdiv"), Op.not_equal, -2.0 ** 31, Op.mult)
+    ts(R("jt", 0, 128), R("ji", 0, 128), 3, Op.arith_shift_right, 7, Op.bitwise_and)
+    ts(R("patc"), R("jt", 0, 128), -32.0, Op.add)
+    fill(R("ones"), 1.0)
+    fill(R("quar"), -2.0 ** -14)
+    ts(R("is0"), R("pcol"), 0.0, Op.is_equal)
+    ts(R("rowc"), R("pat16", 0, 128), R("is0"), Op.mult)
+    for k, c in enumerate((-1.0, -1.0, -5.0)):
+        ts(R("crow", 16 * k, 16 * k + 16), R("ones", 0, 16), R("is0"), Op.mult, c, Op.mult)
+    ts(R("brow"), R("ones", 0, 16), R("is0"), Op.mult, float(B0), Op.mult)
+    ts(R("tmp", 0, 128), R("jf", 0, 128), R("pcol"), Op.is_gt, -2.0 ** -14, Op.mult)
+    ts(R("tm2", 0, 128), R("idb"), 1.0 / 32, Op.mult)
+    tt(R("tri"), R("tmp", 0, 128), R("tm2", 0, 128), Op.add)
+    ts(R("i128"), R("jf", 0, 128), 0.0, Op.add)
+    ts(R("dump"), R("jf", 0, 8), 16.0, Op.mult, R("p16"), Op.add)
+    ts(R("q16"), R("dump"), 16.0, Op.mult)
+    ts(R("odd"), R("p16"), 2.0, Op.mult, 1.0, Op.add)
+    ts(R("odd32"), R("odd"), 32.0, Op.mult)
+    ts(R("bow"), R("bo"), R("odd"), Op.mult)
+    for c in range(15):
+        if c != 7:
+            fill(R("eb", 256 * c + 128 * (c >= 8), 272 * c + 16), 0.0)
+    fill(R("bank", 0, B0), 0.0)
+    fill(R("xw", 0, X0), 0.0)
+    ts(R("tmp", 128, 256), R("hi0"), 8.0, Op.mult)
+    tt(R("cw"), R("tmp", 128, 256), R("fi0"), Op.add)
+    tc(R("als"), R("a0i"))
+    tt(R("os"), IND(R("als"), R("e16")), R("mask16"), Op.mult)
+
+    RB, KB, SB = ("ps0", "ps7"), ("ps2", "ps5"), ("ps6", "ps7", "ps0")
+
+    def H(name, h, w=128):
+        return R(name, w * h, w * h + w)
+
+    def states(t, h):
+        mm(R(RB[h], 0, 128), R("idb"), H("negm", h), True, False)
+        mm(R(RB[h], 0, 128), R("boh"), H("os", h), False, False)
+        mm(R(RB[h], 128, 256), R("boh"), H("os", h), False, True)
+        scan(H("sl", h), H("rst", h), R(RB[h], 0, 128), Op.add, Op.max)
+        tc(H("arow", h), R(RB[h], 128, 256))
+        tt(H("dg", h), H("sl", h), R(RB[h], 128, 256), Op.is_equal)
+        tc(H("alu", h, 8), R("sl", 128 * h + 15, 128 * h + 128, 16))
+        tc(H("suu", h), IND(R("sui", 0, 2048), H("alu", h, 8)))
+        for k in (2 * h, 2 * h + 1):
+            act(H("cc", k, 1024), IND(R("xw", X0), H("suu", k, 64)))
+
+    def places(t):
+        al = R("sl", 15, 256, 16)
+        for h in (0, 1):
+            mm(R("ps1", 160 + h, 176, 2), H("os", h), R("ob8h"), h == 0, h == 1 and t == ASKS)
+        if t < ASKS:
+            mm(R("ps1", 176, 192), R("ones"), R("brow"), False, False)
+            mm(R("ps1", 176, 192), R("idk"), R("lanb"), False, False)
+            for h in (0, 1):
+                mm(R("ps1", 176 + h, 192, 2), H("os", h), R("ob4h"), False, h == 1)
+        tc(R("ait"), R("ps1", 160, 176))
+        ts(R("ahit"), R("ait"), 7, Op.arith_shift_right)
+        ts(R("alot"), R("ait"), 127, Op.bitwise_and)
+        tc(R("alof"), R("alot"))
+        tt(R("ah"), IND(R("ahit"), R("et16")), R("pat16"), Op.is_equal)
+        tc(R("ail"), al)
+        ts(R("alo"), R("ail"), 127, Op.bitwise_and)
+        tc(R("alou"), R("alo"))
+        act(R("gc_"), IND(R("cw"), R("alou")))
+        mm(R("ps6", 0, 256), R("id256"), R("ah"), True, False)
+        for h in (0, 1):
+            mm(H("ps6", h), H("gc_", h), R("idb"), False, h == 1)
+        scan(R("lk"), R("rst"), R("ps6", 0, 256), Op.add, Op.max)
+        tc(R("lki"), R("lk", 15, 256, 16))
+        ts(R("hfi", 0, 16), R("lki"), 3, Op.arith_shift_right, 3, Op.bitwise_and)
+        ts(R("hfi", 16, 32), R("lki"), 7, Op.bitwise_and)
+        tc(R("hfb"), R("hfi"))
+        mm(R("ps1", 0, 48), R("ones"), R("crow"), True, False)
+        for h in (0, 1):
+            mm(R("ps1", h, 48, 2), H("dg", h), R("ob24"), False, False)
+        for c in range(15):
+            ts(R("eb", 272 * c + 16, 256 * c + 256), R("arow", 16 * c + 16, 256), C("sl", 16 * c + 15), Op.is_equal)
+            for h in (0, 1) if c < 7 else (1,):
+                mm(R("ps1", h, 48, 2), H("eb", 2 * c + h), R("ob24"), False, False)
+        for h in (0, 1):
+            mm(R("ps1", h, 16, 2), R("idb"), H("hfb", h, 8), False, False)
+            for k in (1, 2):
+                mm(R("ps1", 16 * k + h, 16 * k + 16, 2), R("idn"), H("hfb", 2 + h, 8), False, h == 1 and k == 2)
+
+    def offsets(t):
+        al = R("sl", 15, 256, 16)
+        tc(R("xi"), R("ps1", 0, 16))
+        ts(R("bn"), R("ps1", 16, 48), 0.0, Op.is_ge, -16384.0, Op.mult)
+        mm(R("ps1", 64, 80), R("id4"), al, True, False)
+        mm(R("ps1", 80, 96), R("idf"), al, False, False)
+        ts(R("x3"), R("xi"), 3, Op.bitwise_and)
+        tt(R("y"), R("x3"), R("bn", 0, 16), Op.add)
+        tt(R("ay"), IND(R("y"), R("et16")), R("mask16"), Op.mult)
+        for k, o in ((64, "ob8"), (80, "om8")):
+            for h in (0, 1):
+                mm(R("ps1", k + 8 * h, k + 8 * h + 8), H("ay", h), R(o), False, k == 80 and h == 1)
+        ts(R("offu"), R("ps1", 64, 80), 16.0, Op.add)
+        ts(R("sou"), R("ps1", 80, 96), 0.375, Op.add)
+        act(R("sp"), IND(R("sui"), R("sou")))
+        mm(R("ps3", 384, 400), R("idm"), R("bn", 16, 32), True, False)
+        mm(R("ps3", 384, 400), R("tri"), R("bn", 0, 16), False, False)
+        mm(R("ps3", 385, 400, 2), R("quar"), R("bn", 0, 16, 2), False, True)
+        if t < ASKS:
+            tc(R("ri"), R("ps3", 384, 400))
+        ts(R("put"), R("ps3", 384, 400), -384.0, Op.is_lt)
+        ts(R("w7"), R("bn", 0, 16), 7.0 / 16384, Op.mult, 7.0, Op.add)
+        tt(R("w"), R("put"), R("w7"), Op.add)
+
+    def ask(t):
+        qp = R("qp%d" % t)
+        tt(R("pv"), R("x3"), R("ps1", 176, 192), Op.add)
+        ts(R("rlo"), R("ri"), 15, Op.bitwise_and)
+        ts(R("rhi"), R("ri"), 4, Op.arith_shift_right)
+        tt(R("cb"), IND(R("rhi"), R("e8")), R("patc"), Op.is_equal)
+        tt(R("ca"), IND(R("rlo"), R("et16")), R("pat16"), Op.is_equal)
+        tt(R("cb2"), IND(R("pv"), R("e8")), R("cb"), Op.mult)
+        mm(R("ps1", 96, 160), R("idb"), R("gneg"), True, False)
+        for h in (0, 1):
+            mm(R("ps1", 96, 160), H("ca", h), H("cb2", h, 64), False, h == 1)
+        scan(R("qs"), R("keep"), R("ps1", 96, 160), Op.mult, Op.max)
+        tc(qp, R("qs", 7, 64, 8))
+        send(1 + t % (N - 1), 0, R("qpin%d" % t), qp, "rp%d" % t)
+        ts(R("v1"), qp, 16383, Op.bitwise_and)
+        tt(R("offr%d" % t), R("v1"), R("dump"), Op.max)
+
+    def update(t):
+        mm(R("ps1", 192, 320), R("cw"), R("idb"), True, False)
+        for k in range(16):
+            col = 2 * (k % 8) + k // 8
+            ts(H("hot", k), R("i128"), C("alof", col), Op.is_equal, C("w", col), Op.mult)
+            mm(R("ps1", 192 + 16 * (k % 8), 208 + 16 * (k % 8)), H("hot", k), H("ah", k, 16), False, k == 15)
+        act(R("ut"), R("ps1", 192, 320))
+        mm(R("ps1", 320, 448), R("ut"), R("idb"))
+        if t < ASKS:
+            act(R("cw"), R("ps1", 320, 448))
+        else:
+            tc(R("w1"), R("ps1", 320, 448))
+            ts(R("w2"), R("w1"), 3, Op.arith_shift_right, 3, Op.bitwise_and)
+            ts(R("w3"), R("w1"), 7, Op.bitwise_and)
+            tc(R("ohf"), R("w2"))
+            tc(R("oyf"), R("w3"))
+
+    def pops(t):
+        zn = "zz%d" % (t + 1)
+        if t > 0:
+            wi, of, src = R("bank"), R("offr%d" % (t - 1)), R("anin%d" % (t - 1))
+            op("v", wi, [src, of], lambda e: e.tensor_copy(wi[0].indirect(of[0]), src[0]), LEAST + SCATTER * 128)
+        tt(R("zs"), IND(R("bank", B0 - 16), R("offu")), R("zz%d" % t), Op.add)
+        ts(R(zn), R("zs"), 0.0, Op.max, 255.0, Op.min)
+        mm(R("ps3", 0, 256), R("idb"), R(zn))
+        if t + 1 < ASKS:
+            send(1 + (t + 1) % (N - 1), 0, R("zin%d" % (t + 1)), R(zn), "rz%d" % (t + 1))
+
+    def dist(t):
+        zn, nv = "zz%d" % (t + 1), 16 - NS[t]
+        if t == 0 or NS[t] != NS[t - 1]:
+            ts(R("tm2", 128, 256), R("pat16", 0, 128), float(nv), Op.is_ge, 16.0, Op.mult)
+            tt(R("bs"), R("tm2", 128, 256), R("bo"), Op.mult)
+        parts = -(-NS[t] // 4)
+        chunks = [(h, list(range(nv, 16))[k::parts]) for h in (0, 1) for k in range(parts)]
+
+        def cc(h, m):
+            return R("cc", 2048 * h + m, 2048 * h + 2048, 16)
+
+        def mx(h, m):
+            return H("mx", 16 * h + m)
+
+        place = {}
+        for k, (h, ms) in enumerate(chunks):
+            bank = SB[k % len(SB)]
+            for j, m in enumerate(ms):
+                mm(H(bank, j), R("idb"), cc(h, m), j == 0, False)
+            for j, m in enumerate(ms):
+                mm(H(bank, j), R("idn"), H(zn, h), False, j == len(ms) - 1)
+            at = 16 * h + nv + sum(len(c[1]) for c in chunks[:k] if c[0] == h)
+            act(R("mx", 128 * at, 128 * (at + len(ms))), R(bank, 0, 128 * len(ms)), Fn.Abs)
+            for j, m in enumerate(ms):
+                place[h, m] = at + j
+        for h in (0, 1):
+            mm(R(KB[h], 0, 128), R("ones"), R("rowc"), True, False)
+            for m in range(nv):
+                mm(R(KB[h], m, 128, 16), cc(h, m), R("om16"), False, False)
+            if NS[t]:
+                mm(R(KB[h], 0, 128), H(zn, h), R("bs"), False, False)
+            for m in range(nv):
+                tt(mx(h, m), cc(h, m), H("ps3", h), Op.max)
+                mm(R(KB[h], m, 128, 16), mx(h, m), R("o32"), False, m == 15)
+            for m in range(nv, 16):
+                mm(R(KB[h], m, 128, 16), H("mx", place[h, m]), R("o16"), False, m == 15)
+
+    def choose(t, h):
+        scan(H("ksc", h), R("big"), R(KB[h], 0, 128), Op.add, Op.min)
+        act(H("kmin", h), IND(H("ksc", h), R("e15", 0, 8)))
+        tt(H("oh", h), H("kmin", h), R(KB[h], 0, 128), Op.is_equal)
+        mm(R(KB[h], 128, 256), H("oh", h), R("idb"))
+        tt(H("os", h), R(KB[h], 128, 256), H("sp", h), Op.mult)
+
+    def answer(t):
+        qpin = R("qpin%d" % t)
+        ts(R("dq", 0, 8), qpin, 14, Op.arith_shift_right)
+        ts(R("dq", 8, 16), qpin, 2, Op.arith_shift_right, 4095, Op.bitwise_and)
+        tc(R("dqu"), R("dq"))
+        act(R("zq"), IND(R("zin%d" % t), R("dqu", 0, 8)))
+        act(R("goal"), IND(R("xw"), R("dqu", 8, 16)))
+        mm(R("ps4", 0, 128), R("bow"), R("zq"))
+        mm(R("ps3", 256, 384), R("idn"), R("zq"), True, False)
+        mm(R("ps3", 256, 384), R("idb"), R("goal"), False, True)
+        tc(R("ui"), R("ps4", 0, 128))
+        ts(R("uu"), R("ui"), 4095, Op.bitwise_and)
+        ts(R("ps4", 128, 256), R("uu"), R("odd32"), Op.add)
+        tt(R("pr"), R("uu"), R("ps4", 128, 256), Op.mult)
+        ts(R("ux"), R("pr"), 5, Op.arith_shift_right, 8191, Op.bitwise_and)
+        tc(R("cou"), R("ux"))
+        for k in range(2):
+            act(H("cand", k, 1024), IND(R("bank", B0), H("cou", k, 64)))
+        mm(R("ps4", 256, 384), R("ones"), R("rowc"), True, False)
+        for m in range(16):
+            mm(R("ps4", 256 + m, 384, 16), R("cand", m, 2048, 16), R("om16"), False, False)
+            tt(H("mq", m), R("cand", m, 2048, 16), R("ps3", 256, 384), Op.max)
+            mm(R("ps4", 256 + m, 384, 16), H("mq", m), R("o32"), False, m == 15)
+        scan(R("kq"), R("big"), R("ps4", 256, 384), Op.add, Op.min)
+        tc(R("ki"), R("kq", 15, 128, 16))
+        ts(R("mi"), R("ki"), 15, Op.bitwise_and)
+        tt(R("aq"), IND(R("mi"), R("e16", 0, 8)), R("mask16", 0, 128), Op.mult)
+        mm(R("ps4", 384, 392), R("idb"), R("q16"), True, False)
+        mm(R("ps4", 384, 392), R("aq"), R("ob8"), False, True)
+        tc(R("seu"), R("ps4", 384, 392))
+        act(R("an%d" % t), IND(R("cand"), R("seu")))
+        send(-1 - t % (N - 1), 0, R("anin%d" % t), R("an%d" % t), "ra%d" % t)
+
+    send(1, 0, R("zin0"), R("zz0"), "rz0")
+    for h in (0, 1):
+        states(0, h)
+    for t in range(STEPS):
+        places(t)
+        offsets(t)
+        if t < ASKS:
+            ask(t)
+        update(t)
+        pops(t)
+        dist(t)
+        if t < ASKS:
+            answer(t)
+        for h in (0, 1):
+            choose(t, h)
+            if t + 1 < STEPS:
+                states(t + 1, h)
+            else:
+                mm(R(RB[h], 128, 256), R("boh"), H("os", h))
+                act(H("arf", h), R(RB[h], 128, 256))
+    store("d", T.yz[:, :], R("zz%d" % STEPS)[0], R("zz%d" % STEPS))
+    buf, base, w = PACK["arf"]
+    store("d", T.ya[:, :], T[buf][0:128:16, base:base + w], R("arf"))
+    store("d", T.yf[:, :], R("oyf")[0], R("oyf"))
+    store("d", T.yh[:, :], R("ohf")[0], R("ohf"))
+
+    qsem = {"v": "sv", "s": "ss", "t": "st", "g": "sg"}
+    count = {q: 0 for q in qsem}
+    known = {q: {} for q in qobj}
+    done = {}
 
     def need(q, sem, n, snap):
         kn = known[q]
@@ -60,526 +518,26 @@ def rank_program(g, core, T, topo):
                 if kn.get(a, 0) < b:
                     kn[a] = b
 
-    def access(q, reads, writes):
-        todo = {}
-        for wr, refs in ((False, reads), (True, writes)):
-            for name, lo, hi in refs:
-                for r in recs.get(name, ()):
-                    hit = r[3] != q if name in PSUM else r[0] < hi and lo < r[1] and (r[2] or wr)
-                    if hit and (r[4] not in todo or todo[r[4]][0] < r[5]):
-                        todo[r[4]] = (r[5], r[6])
+    if not ORDER:
+        ORDER.extend(plan(ops))
+    for i in ORDER:
+        o = ops[i]
+        q, todo = o["q"], {}
+        for p in o["pred"]:
+            sem, n, snap = done[p]
+            if not q == ops[p]["q"] == "t" and todo.get(sem, (0,))[0] < n:
+                todo[sem] = (n, snap)
         for sem in sorted(todo, key=lambda s: -len(todo[s][1])):
             need(q, sem, todo[sem][0], todo[sem][1])
-
-    def note(q, sem, n, reads, writes):
-        snap = dict(known[q])
-        for wr, refs in ((False, reads), (True, writes)):
-            for name, lo, hi in refs:
-                old = recs.get(name, [])
-                if name in PSUM:
-                    old = [r for r in old if r[3] != q]
-                elif wr:
-                    old = [r for r in old if not (lo <= r[0] and r[1] <= hi)]
-                else:
-                    old = [r for r in old if r[2] or r[3] != q or not (lo <= r[0] and r[1] <= hi)]
-                old.append((lo, hi, wr, q, sem, n, snap))
-                recs[name] = old
-
-    def op(q, out, ins, emit):
-        reads = [x for r in ins for x in r[1]]
-        access(q, reads, out[1])
-        count[q] += 1
-        emit(qobj[q]).then_inc(T.sem[qsem[q]], 1)
-        note(q, qsem[q], count[q], reads, out[1])
-
-    def R(name, a=0, b=None, st=1):
-        buf, base, w = PACK[name] if name in PACK else (name, 0, SCRATCH[name][1][1])
-        b = w if b is None else b
-        ap = T[buf][:, base + a:base + b] if st == 1 else T[buf][:, base + a:base + b:st]
-        return (ap, [(buf, base + a, base + b)])
-
-    def IND(win, off):
-        return (win[0].indirect(off[0]), win[1] + off[1])
-
-    def sc(x):
-        return x[0] if isinstance(x, tuple) else x
-
-    def tc(out, a):
-        op("v", out, [a], lambda e: e.tensor_copy(out[0], a[0]))
-
-    def tt(out, a, b, o):
-        op("v", out, [a, b], lambda e: e.tensor_tensor(out[0], a[0], b[0], o))
-
-    def ts(out, a, s1, o1, s2=None, o2=None):
-        ins = [a] + [s for s in (s1, s2) if isinstance(s, tuple)]
-        if o2 is None:
-            op("v", out, ins, lambda e: e.tensor_scalar(out[0], a[0], sc(s1), None, o1))
+        ins = o["emit"](qobj[q])
+        if o["sem"] is None:
+            count[q] += 1
+            ins.then_inc(T.sem[qsem[q]], 1)
+            done[i] = (qsem[q], count[q], dict(known[q]))
         else:
-            op("v", out, ins, lambda e: e.tensor_scalar(out[0], a[0], sc(s1), sc(s2), o1, o2))
-
-    def act(out, a):
-        op("s", out, [a], lambda e: e.activation(out[0], a[0], Fn.Copy))
-
-    def actf(out, a, fn, bias, scale):
-        ins = [a] + [s for s in (bias, scale) if isinstance(s, tuple)]
-        op("s", out, ins, lambda e: e.activation(out[0], a[0], fn, bias=sc(bias), scale=sc(scale)))
-
-    def mm(out, l, r, start=True, stop=True):
-        op("t", out, [l, r], lambda e: e.matmul(out[0], l[0], r[0], start, stop))
-
-    def iota(out, pattern, cm):
-        op("g", out, [], lambda e: e.iota(out[0], pattern, 0, cm))
-
-    def fill(out, c):
-        op("v", out, [], lambda e: e.memset(out[0], c))
-
-    def landed(ref, q, sem, n):
-        for name, lo, hi in ref[1]:
-            recs.setdefault(name, []).append((lo, hi, True, q, sem, n, {}))
-
-    def load(q, out, src, sem):
-        qobj[q].dma_start(out[0], src).then_inc(T.sem[sem], 16)
-        landed(out, "dma", sem, 16)
-
-    sends = [0]
-
-    def send(to, out, src, sem):
-        dst = T.cores[to]
-        rid, pid = topo.addr(dst)[:2]
-        access("g", src[1], [])
-        g.remote_dma(out[0], src[0], T.sem[sem], T.sem["sent"], pid, rid, topo.mask(core, dst))
-        sends[0] += len(topo.engines(core, dst))
-
-    load("d", R("a0i"), T.a0[:, :], "la")
-    load("s", R("hi0"), T.hd0[:, :], "lh0")
-    load("s", R("fi0"), T.fl0[:, :], "lf0")
-    load("d", R("sui", 0, 2048), T.su[:, :], "ls")
-    load("s", R("za"), T.z0[:, :], "lz")
-    load("d", R("xw"), T.xs[:, :], "lx")
-    load("d", R("bank", B0, BD), T.gs[:, :], "lg")
-    arrive = {}
-    for t in range(ASKS):
-        asker, asked = T.cores[(rank - 1 - t % (N - 1)) % N], T.cores[(rank + 1 + t % (N - 1)) % N]
-        for n, sem, src in (("qpin", "rp", asker), ("zqin", "rz", asker), ("anin", "ra", asked)):
-            arrive["%s%d" % (sem, t)] = len(topo.engines(src, core))
-            landed(R("%s%d" % (n, t)), "rem", "%s%d" % (sem, t), len(topo.engines(src, core)))
-
-    iota(R("ci"), [[1, 1]], 1)
-    iota(R("ji"), [[1, 256]], 0)
-    iota(R("sui", 2048, 4096), [[1, 2048]], 0)
-    tc(R("pcol"), R("ci"))
-    tc(R("jf"), R("ji"))
-    ts(R("ci2"), R("ci"), 15, Op.bitwise_and)
-    ts(R("ci3"), R("ci"), 4, Op.arith_shift_right)
-    tc(R("p16"), R("ci2"))
-    tc(R("pdiv"), R("ci3"))
-    ts(R("jt"), R("ji"), 15, Op.bitwise_and)
-    tc(R("pat16"), R("jt"))
-    ts(R("mask16"), R("pat16"), R("p16"), Op.is_equal)
-    tc(R("e16"), R("ji", 0, 16))
-    ts(R("jt", 0, 128), R("ji", 0, 128), 4, Op.arith_shift_right)
-    tc(R("qd16"), R("jt", 0, 128))
-    ts(R("boh"), R("qd16"), R("pdiv"), Op.is_equal)
-    ts(R("ob8h"), R("jf", 0, 8), R("pdiv"), Op.is_equal)
-    ts(R("ob8k"), R("ob8h"), 1024.0, Op.mult)
-    ts(R("maskm"), R("pat16"), R("p16"), Op.is_le, 4096.0, Op.mult)
-    ts(R("ob8"), R("jf", 0, 8), R("pdiv"), Op.is_equal)
-    ts(R("idb"), R("jf", 0, 128), R("pcol"), Op.is_equal)
-    ts(R("lanb", 0, 8), R("jf", 0, 8), 0.0, Op.mult, R("pcol"), Op.add)
-    ts(R("lanb", 8, 16), R("lanb", 0, 8), 128.0, Op.add)
-    fill(R("ones"), 1.0)
-    fill(R("zer"), 0.0)
-    for j in range(16):
-        actf(R("hm", 128 * j, 128 * j + 128), R("ones"), Fn.Copy, 0.0, R("mask16", j, j + 1))
-    tc(R("als"), R("a0i"))
-    tt(R("os"), IND(R("als"), R("e16")), R("mask16"), Op.mult)
-
-    def spread(t):
-        mm(R("ps1", 0, 256), R("boh"), R("os"))
-        if t < STEPS:
-            mm(R("ps3", 256, 512), R("boh"), R("os"), True, False)
-            mm(R("ps3", 256, 512), R("idb"), R("maskm"), False, True)
-            act(R("arm"), R("ps3", 256, 512))
-        if t < ASKS:
-            for h in (0, 1):
-                o = R("ps1", 272 + 8 * h, 280 + 8 * h)
-                mm(o, R("os", 128 * h, 128 * h + 128), R("ob8k"), True, False)
-                mm(o, R("idb"), R("lanb", 8 * h, 8 * h + 8), False, True)
-
-    spread(0)
-    for c in range(15):
-        if c != 7:
-            fill(R("eb", 256 * c + 128 * (c >= 8), 272 * c + 16), 0.0)
-    fill(R("bank", 0, B0), 0.0)
-    ts(R("bo"), R("qd16"), R("pdiv"), Op.is_equal)
-    ts(R("rpt"), R("idb"), 512.0, Op.mult)
-    ts(R("cwt"), R("jf", 0, 128), R("pcol"), Op.is_gt)
-    tt(R("cwt"), R("cwt"), R("rpt"), Op.subtract)
-    ts(R("tri"), R("cwt"), 0.25, Op.mult)
-    fill(R("quar"), 0.25)
-    ts(R("ge8"), R("p16"), 8.0, Op.is_ge)
-    ts(R("e8f"), R("jf", 0, 8), 2.0, Op.mult, R("ge8"), Op.add)
-    tc(R("e8"), R("e8f"))
-    ts(R("jt", 0, 128), R("ji", 0, 128), 7, Op.bitwise_and)
-    ts(R("patc8"), R("jt", 0, 128), -32.0, Op.add)
-    ts(R("jt", 0, 64), R("ji", 0, 64), 3, Op.arith_shift_right)
-    ts(R("gm"), R("jt", 0, 64), R("pdiv"), Op.is_equal)
-    ts(R("cwt"), R("hi0"), 33.0, Op.mult)
-    ts(R("cw"), R("fi0"), 32.0, Op.mult)
-    tt(R("cw"), R("cw"), R("cwt"), Op.add)
-
-    def late_constants():
-        ts(R("dump"), R("jf", 0, 8), 16.0, Op.mult, R("p16"), Op.add)
-        ts(R("dump"), R("dump"), float(16 + 16384 - B0), Op.add)
-        ts(R("is0"), R("pcol"), 0.0, Op.is_equal)
-        ts(R("rowc"), R("pat16"), R("is0"), Op.mult)
-        ts(R("om16"), R("ob8"), -16.0, Op.mult)
-        ts(R("idn"), R("idb"), -1.0, Op.mult)
-        ts(R("o16"), R("ob8"), 16.0, Op.mult)
-        ts(R("o32"), R("ob8"), 32.0, Op.mult)
-        ts(R("i128"), R("jf", 0, 128), 0.0, Op.add)
-        ts(R("rpt"), R("pat16", 0, 128), 1.0, Op.add)
-        tt(R("rpt"), R("rpt"), R("bo"), Op.mult)
-        ts(R("rp"), R("rpt"), -1.0, Op.add)
-        ts(R("odd"), R("p16"), 2.0, Op.mult, 1.0, Op.add)
-        ts(R("bow"), R("bo"), R("odd"), Op.mult)
-        ts(R("l16"), R("pcol"), 16.0, Op.mult)
-
-    z = ["za", "zb"]
-
-    def centres(a, b):
-        for k in range(a, b):
-            act(R("cc", 1024 * k, 1024 * k + 1024), IND(R("xw"), R("suu", 64 * k, 64 * k + 64)))
-
-    def differences():
-        for c in range(16):
-            actf(R("rd", 128 * c, 128 * c + 128), R("i128"), Fn.Abs, R("alof", c, c + 1), 1.0)
-
-    def head(t):
-        tc(R("ai"), R("als"))
-        tc(R("alu"), R("als"))
-        ts(R("alo"), R("ai"), 127, Op.bitwise_and)
-        if t > 0:
-            tc(R("suu"), IND(R("sui", 0, 2048), R("alu")))
-        tc(R("alou"), R("alo"))
-        if t > 0:
-            centres(0, 2)
-        tc(R("arow"), R("ps1", 0, 256))
-        mm(R("ps2", 0, 16), R("ones"), R("zer"), True, False)
-        yield
-        act(R("gc_"), IND(R("cw"), R("alou")))
-        if t > 0:
-            centres(2, 4)
-        yield
-        for c in range(15):
-            ts(R("eb", 272 * c + 16, 256 * c + 256), R("arow", 16 * c + 16, 256), R("als", c, c + 1), Op.is_equal)
-            for h in (0, 1) if c < 7 else (1,):
-                mm(R("ps2", 8 * h, 8 * h + 8), R("eb", 256 * c + 128 * h, 256 * c + 128 * h + 128), R("ob8"), False, c == 14)
-            yield
-            if c == 6:
-                tt(R("dg"), IND(R("als"), R("e16")), R("arm"), Op.is_equal)
-                for h in (0, 1):
-                    mm(R("ps2", 8 * h, 8 * h + 8), R("dg", 128 * h, 128 * h + 128), R("ob8"), False, False)
-                yield
-        if t == 0:
-            tc(R("suu"), IND(R("sui", 0, 2048), R("alu")))
-            centres(0, 4)
-        tt(R("gmk"), IND(R("hm"), R("alu")), R("gc_"), Op.mult)
-        for h in (0, 1):
-            mm(R("ps7", 8 * h, 8 * h + 8), R("gmk", 128 * h, 128 * h + 128), R("ob8h"))
-        yield
-        ts(R("al4"), R("als"), 4.0, Op.mult, float(B0), Op.add)
-        ts(R("ahi"), R("ai"), 7, Op.arith_shift_right)
-        yield
-        tc(R("cdi"), R("ps7", 0, 16))
-        ts(R("alof"), R("alo"), -1.0, Op.mult)
-        ts(R("hh"), R("cdi"), 31, Op.bitwise_and)
-        ts(R("tl"), R("cdi"), 5, Op.arith_shift_right)
-        tt(R("xx"), R("hh"), R("ps2", 0, 16), Op.add)
-        tc(R("ahif"), R("ahi"))
-        if t > 0:
-            differences()
-        yield
-        tt(R("d1"), R("xx"), R("tl"), Op.subtract)
-        ts(R("x3"), R("xx"), 3, Op.bitwise_and)
-        ts(R("blk"), R("d1"), 0.0, Op.is_ge, 4.0, Op.mult)
-        mm(R("ps2", 32, 40), R("tri"), R("blk", 0, 8))
-        mm(R("ps2", 40, 48), R("tri"), R("blk", 8, 16), True, False)
-        mm(R("ps2", 40, 48), R("quar"), R("blk", 0, 8), False, True)
-        ts(R("s2"), R("d1"), 4.0, Op.is_lt)
-        tt(R("y1"), R("x3"), R("blk"), Op.add)
-        if t < ASKS:
-            ts(R("pv1"), R("x3"), 256.0, Op.mult)
-            tt(R("pv2"), R("pv1"), R("ps1", 272, 288), Op.add)
-        yield
-        ts(R("s1"), R("ps2", 32, 48), -384.0, Op.is_lt, 8.0, Op.mult)
-        tt(R("p8"), R("s1"), R("s2"), Op.mult)
-        tt(R("yv"), R("y1"), R("p8"), Op.add)
-        yield
-        tt(R("ay"), IND(R("yv"), R("e16")), R("mask16"), Op.mult)
-        for h in (0, 1):
-            mm(R("ps2", 48 + 8 * h, 56 + 8 * h), R("ay", 128 * h, 128 * h + 128), R("ob8"))
-        yield
-
-    def offsets(t):
-        ts(R("pp"), R("ps2", 48, 64), 4.0, Op.is_lt)
-        tt(R("oq"), R("ps2", 48, 64), R("al4"), Op.add)
-        tt(R("offu"), R("oq"), R("pp"), Op.mult)
-        yield
-        ts(R("sb"), R("ps2", 48, 64), 4.0, Op.is_ge, 2048.0, Op.mult)
-        tt(R("sou"), R("sb"), R("als"), Op.add)
-        ts(R("pt"), R("ps2", 48, 64), 8.0, Op.is_ge, 32.0, Op.mult)
-        tt(R("wl"), R("pp"), R("pt"), Op.add)
-        yield
-
-    made = [0]
-
-    def onehot(c):
-        if c >= made[0]:
-            made[0] = c + 1
-            ts(R("lh", 128 * c, 128 * c + 128), R("rp"), R("ahif", c, c + 1), Op.is_equal, R("wl", c, c + 1), Op.mult)
-
-    def onehots(n):
-        for _ in range(n):
-            if made[0] < 16:
-                onehot(made[0])
-
-    def ask(t):
-        to = (rank + 1 + t % (N - 1)) % N
-        tc(R("ri"), R("ps2", 32, 48))
-        ts(R("pv3"), R("p8"), 524288.0, Op.mult)
-        tt(R("pv"), R("pv2"), R("pv3"), Op.add)
-        ts(R("rlo"), R("ri"), 15, Op.bitwise_and)
-        ts(R("rhi"), R("ri"), 4, Op.arith_shift_right)
-        yield
-        tt(R("cb"), IND(R("rhi"), R("e8")), R("patc8"), Op.is_equal)
-        tt(R("ca"), IND(R("rlo"), R("e16")), R("pat16"), Op.is_equal)
-        tt(R("cb2"), IND(R("pv"), R("e8")), R("cb"), Op.mult)
-        for h in (0, 1):
-            mm(R("ps5", 384, 448), R("ca", 128 * h, 128 * h + 128), R("cb2", 64 * h, 64 * h + 64), h == 0, h == 1)
-        yield
-        if t == 0:
-            late_constants()
-        else:
-            onehots(8)
-        qp = R("qp%d" % t)
-        tt(R("cm"), R("ps5", 384, 448), R("gm"), Op.mult)
-        tt(R("c1"), R("cm", 0, 32), R("cm", 32, 64), Op.add)
-        tt(R("c2"), R("c1", 0, 16), R("c1", 16, 32), Op.add)
-        tt(qp, R("c2", 0, 8), R("c2", 8, 16), Op.add)
-        send(to, R("qpin%d" % t), qp, "rp%d" % t)
-        ts(R("lni"), qp, 255, Op.bitwise_and)
-        tc(R("lnu"), R("lni"))
-        act(R("zq%d" % t), IND(R(z[0]), R("lnu")))
-        send(to, R("zqin%d" % t), R("zq%d" % t), "rz%d" % t)
-        yield
-        ts(R("v1"), qp, 8, Op.arith_shift_right)
-        tt(R("v2"), R("v1"), R("dump"), Op.max)
-        ts(R("offr%d" % t), R("v2"), float(B0 - 16384), Op.add)
-        yield
-
-    def pops(t):
-        if t > 0:
-            wi, of, src = R("bank"), R("offr%d" % (t - 1)), R("anin%d" % (t - 1))
-            op("v", (None, wi[1]), [src, of], lambda e: e.tensor_copy(wi[0].indirect(of[0]), src[0]))
-        tt(R("zs"), IND(R("bank"), R("offu")), R(z[0]), Op.add)
-        ts(R(z[1]), R("zs"), 0.0, Op.max, 255.0, Op.min)
-        mm(R("ps3", 0, 256), R("ones"), R("rowc"), True, False)
-        for h in (0, 1):
-            for m in range(16 - NS):
-                mm(R("ps3", 128 * h + m, 128 * h + 128, 16), R("cc", 2048 * h + m, 2048 * h + 2048, 16), R("om16"), False, False)
-        for m in range(16 - NS, 16):
-            mm(R(SBANK[m % NS], 0, 256), R("idb"), R("cc", m, 4096, 16), True, False)
-        mm(R("ps4", 0, 256), R("idb"), R(z[1]))
-        for m in range(16 - NS, 16):
-            mm(R(SBANK[m % NS], 0, 256), R("idn"), R(z[1]), False, True)
-            actf(R("mx", 256 * m, 256 * m + 256), R(SBANK[m % NS], 0, 256), Fn.Abs, 0.0, 1.0)
-        tc(R("sp"), IND(R("sui"), R("sou")))
-        if t == 0:
-            differences()
-        for c in range(0, 16, 4):
-            actf(R("rh", 128 * c, 128 * c + 512), R("rd", 128 * c, 128 * c + 512), Fn.Relu, 1.0, -1.0)
-
-    def update(t):
-        for c in range(16):
-            onehot(c)
-            mm(R("ps5", 128, 256), R("lh", 128 * c, 128 * c + 128), R("rh", 128 * c, 128 * c + 128), c == 0, c == 15)
-            yield
-
-    def table():
-        tt(R("cw"), R("cw"), R("ps5", 128, 256), Op.add)
-
-    def dist(t):
-        for m in range(16 - NS):
-            tt(R("mx", 256 * m, 256 * m + 256), R("cc", m, 4096, 16), R("ps4", 0, 256), Op.max)
-            for h in (0, 1):
-                a = 256 * m + 128 * h
-                mm(R("ps3", 128 * h + m, 128 * h + 128, 16), R("mx", a, a + 128), R("o32"), False, False)
-            if m == 3:
-                for n in range(16 - NS, 16):
-                    for h in (0, 1):
-                        mm(R("ps3", 128 * h + n, 128 * h + 128, 16), R(z[1], 128 * h, 128 * h + 128), R("o16"), False, False)
-            if m == 15 - NS:
-                for n in range(16 - NS, 16):
-                    for h in (0, 1):
-                        a = 256 * n + 128 * h
-                        mm(R("ps3", 128 * h + n, 128 * h + 128, 16), R("mx", a, a + 128), R("o16"), False, h == 1 and n == 15)
-
-    def choose(t):
-        tc(R("ko"), R("ps3", 1, 256, 2))
-        tt(R("k1"), R("ps3", 0, 256, 2), R("ko"), Op.min)
-        act(R("ks"), R("ps3", 0, 256))
-        yield
-        src, w = "k1", 128
-        for d in ("k2", "k3", "k4"):
-            tt(R(d), R(src, 0, w, 2), R(src, 1, w, 2), Op.min)
-            src, w = d, w // 2
-            yield
-        tt(R("oh"), IND(R("k4"), R("e16")), R("ks"), Op.is_equal)
-        for h in (0, 1):
-            mm(R("ps0", 256 + 128 * h, 384 + 128 * h), R("oh", 128 * h, 128 * h + 128), R("idb"))
-        for _ in range(4):
-            yield
-        tt(R("os"), R("ps0", 256, 512), R("sp"), Op.mult)
-        if t + 1 < STEPS:
-            for h in (0, 1):
-                mm(R("ps0", 128 * h, 128 * h + 128), R("os", 128 * h, 128 * h + 128), R("boh"))
-            for _ in range(4):
-                yield
-            tt(R("aa"), R("ps0", 0, 256), R("mask16"), Op.mult)
-            for h in (0, 1):
-                mm(R("ps0", 256 + 8 * h, 264 + 8 * h), R("aa", 128 * h, 128 * h + 128), R("ob8h"))
-        spread(t + 1)
-        for _ in range(4):
-            yield
-        if t + 1 < STEPS:
-            tc(R("als"), R("ps0", 256, 272))
-        else:
-            act(R("arf"), R("ps1", 0, 256))
-        yield
-
-    def answer(t):
-        to = (rank - 1 - t % (N - 1)) % N
-        qpin, zqin = R("qpin%d" % t), R("zqin%d" % t)
-        ts(R("qa"), qpin, 10, Op.arith_shift_right, 2047, Op.bitwise_and)
-        tc(R("qau"), R("qa"))
-        act(R("goal"), IND(R("xw"), R("qau")))
-        mm(R("ps5", 0, 128), R("bow"), zqin)
-        mm(R("ps4", 256, 384), R("idn"), zqin, True, False)
-        mm(R("ps4", 256, 384), R("idb"), R("goal"), False, True)
-        tc(R("ui"), R("ps5", 0, 128))
-        yield
-        ts(R("uu"), R("ui"), 4095, Op.bitwise_and)
-        yield
-        tt(R("usq"), R("uu"), R("uu"), Op.mult)
-        ts(R("um"), R("uu"), R("odd"), Op.mult)
-        yield
-        ts(R("uv"), R("usq"), 5, Op.arith_shift_right)
-        yield
-        tt(R("us"), R("um"), R("uv"), Op.add)
-        yield
-        ts(R("ux"), R("us"), 8191, Op.bitwise_and)
-        yield
-        tc(R("cou"), R("ux"))
-        for k in range(2):
-            act(R("cand", 1024 * k, 1024 * k + 1024), IND(R("bank", B0, BD), R("cou", 64 * k, 64 * k + 64)))
-        yield "gathering"
-        mm(R("ps6", 0, 128), R("ones"), R("rowc", 0, 128), True, False)
-        for m in range(16):
-            mm(R("ps6", m, 128, 16), R("cand", m, 2048, 16), R("om16"), False, False)
-        for m in range(16):
-            tt(R("mq", 128 * m, 128 * m + 128), R("cand", m, 2048, 16), R("ps4", 256, 384), Op.max)
-            mm(R("ps6", m, 128, 16), R("mq", 128 * m, 128 * m + 128), R("o32"), False, m == 15)
-            yield
-        tc(R("q0"), R("ps6", 1, 128, 2))
-        tt(R("q1"), R("ps6", 0, 128, 2), R("q0"), Op.min)
-        src, w = "q1", 64
-        for d in ("q2", "q3", "q4"):
-            yield
-            tt(R(d), R(src, 0, w, 2), R(src, 1, w, 2), Op.min)
-            src, w = d, w // 2
-        yield
-        ts(R("q5"), R("q4"), 15, Op.bitwise_and)
-        yield
-        ts(R("q6"), R("q5"), R("l16"), Op.add)
-        yield
-        tt(R("aq"), IND(R("q6"), R("e16", 0, 8)), R("mask16", 0, 128), Op.mult)
-        mm(R("ps5", 448, 456), R("aq"), R("ob8h"))
-        yield
-        tc(R("seu"), R("ps5", 448, 456))
-        yield
-        tc(R("an%d" % t), IND(R("cand"), R("seu")))
-        send(to, R("anin%d" % t), R("an%d" % t), "ra%d" % t)
-        yield
-
-    def finish(t):
-        for _ in update(t):
-            yield
-        for _ in range(3):
-            yield
-        table()
-        ts(R("w1"), R("cw"), 1.0, Op.mult)
-        yield
-        ts(R("w2"), R("w1"), 31, Op.bitwise_and)
-        ts(R("w3"), R("w1"), 5, Op.arith_shift_right)
-        ts(R("w4"), R("w1"), 3, Op.bitwise_and)
-        yield
-        tt(R("oyf"), R("w3"), R("w2"), Op.subtract)
-        tc(R("ohf"), R("w4"))
-        yield
-
-    def run(gen):
-        for _ in gen:
-            pass
-
-    def until(x, tag):
-        for y in x:
-            yield
-            if y == tag:
-                return
-
-    def weave(*gens):
-        gens = list(gens)
-        while gens:
-            for x in list(gens):
-                if x in gens and next(x, "end") == "end":
-                    gens = [y for y in gens if y is not x]
-
-    nothing = iter(())
-    run(head(0))
-    for t in range(STEPS):
-        asks, more = t < ASKS, t + 1 < STEPS
-        weave(offsets(t), ask(t) if asks else nothing)
-        pops(t)
-        dist(t)
-        ch, ans = choose(t), answer(t) if asks else nothing
-        onehots(4)
-        next(ch)
-        if more:
-            weave(until(ans, "gathering"), ch, update(t))
-            nxt = head(t + 1)
-            next(nxt)
-            table()
-            for _ in range(5):
-                next(nxt)
-            weave(ans, nxt, ans)
-        else:
-            weave(finish(t), ch)
-        made[0] = 0
-        z.reverse()
-
-    outs = [0]
-
-    def store(dst, ap, ref):
-        access("d", ref[1], [])
-        g.sync.dma_start(dst, ap).then_inc(T.sem["sout"], 16)
-        outs[0] += 16
-
-    store(T.yz[:, :], R(z[0])[0], R(z[0]))
-    buf, base, w = PACK["arf"]
-    store(T.ya[:, :], T[buf][0:128:16, base:base + w], R("arf"))
-    store(T.yf[:, :], R("oyf")[0], R("oyf"))
-    store(T.yh[:, :], R("ohf")[0], R("ohf"))
+            if o["sem"][0] not in arrive:
+                ins.then_inc(T.sem[o["sem"][0]], 16)
+            done[i] = o["sem"] + ({},)
     g.sync.wait_ge(T.sem["sout"], outs[0])
     for q in "vstg":
         need("g", qsem[q], count[q], {})

@@ -2,7 +2,8 @@ from concourse.mybir import AluOpType as Op, ActivationFunctionType as Fn
 
 STEPS = 4
 ASKS = STEPS - 1
-NS = [6, 6, 6, 6]
+NS = [(8, 0)] * 4
+SHARES = sorted({16 - n for x in NS for n in x} - {0, 16})
 B0, BD = 192, 8384
 X0 = B0 // 4
 PSUM = ["ps%d" % i for i in range(8)]
@@ -20,10 +21,10 @@ NARROW = {
                "als 16 sl 256 y 16 put 16 w7 16 w 16 pv 16 ca 256 cb 128 cb2 128 qs 64 alof 16 lk 256 sp 256 ksc 256 kmin 256 kq 128 arf 256 "
                "ohf 128 oyf 128",
     "int32": "ci 1 ci2 1 ci3 1 ci4 1 ji 256 jt 256 hi0 128 fi0 128 a0i 16 ail 16 alo 16 ait 16 ahit 16 alot 16 lki 16 hfi 32 xi 16 x3 16 ri 16 rlo 16 "
-             "rhi 16 v1 8 dq 16 ui 128 uu 128 pr 128 ux 128 ki 8 mi 8 w1 128 w2 128 w3 128",
+             "rhi 16 v1 8 dq 16 ui 256 uu 256 pr 256 ux 256 ki 8 mi 8 w1 128 w2 128 w3 128",
     "uint16": "e16 16 et16 16 e15 16 e8 8 alu 16 alou 16 suu 256 offu 16 sou 16 dqu 16 cou 128 seu 8",
-    "bfloat16": "bo 128 bow 128 ob8 8 ob24 24 om8 8 o16 8 o32 8 om16 8 idb 128 idn 128 id256 128 idk 128 idm 128 tri 128 ones 128 quar 128 i128 128 "
-                "negm 256 rst 256 big 128 keep 64 gneg 64 lanb 16 rowc 128 crow 48 brow 16 q16 8 bs 128 dg 256 bn 32 ay 256 zs 256 oh 256 goal 128 "
+    "bfloat16": "bo 128 bow 128 ob8 8 ob24 24 om8 8 o16 8 o32 8 om16 8 idb 128 idn 128 id256 128 idk 128 idm 128 id32 128 tri 128 ones 128 quar 128 i128 128 "
+                "negm 256 rst 256 big 128 keep 64 gneg 64 lanb 16 rowc 128 crow 48 brow 16 q16 8 bs 512 dg 256 bn 32 ay 256 zs 256 oh 256 goal 128 "
                 "zq 128 aq 128 gc_ 256 ah 256 hfb 32 cw 128 ut 128",
     "float16": "boh 128 ob8h 8 ob4h 8 arow 256 os 256"}
 PACK = {}
@@ -41,7 +42,8 @@ LOADS = ["la", "ls", "lx", "lh0", "lf0", "lz", "lg"]
 SEMAPHORES = ["sv", "ss", "st", "sg", "sent", "sout"] + LOADS + ["%s%d" % (n, t) for t in range(ASKS) for n in ("rp", "rz", "ra")]
 
 GATHER, SCATTER, LEAST, WAKE, HOP, DMA, BYTES = 1.56, 3.8, 64, 130, 1800, 1500, 200
-TENSOR, PATIENCE, SWEEPS = 1.0, 0.5, 6
+TENSOR, PATIENCE, SWEEPS = 0.75, 0.25, 6
+ROWS = ("cc", "cand", "mx", "mq", "eb", "hot")
 ORDER = []
 
 
@@ -49,10 +51,12 @@ def plan(ops):
     n = len(ops)
     succ = [[] for _ in ops]
     for i, o in enumerate(ops):
-        for p in o["pred"]:
+        for p in o["pred"] + o["row"]:
             succ[p].append(i)
 
     def lag(p, i):
+        if p in ops[i]["row"]:
+            return ops[p]["cost"]
         return ops[p]["cost"] + ops[p]["late"] + (0 if ops[p]["q"] == ops[i]["q"] == "t" else WAKE)
 
     def sweep(before, after, gap, ready, way):
@@ -87,7 +91,7 @@ def plan(ops):
                     pool[ops[s]["q"]].append(s)
         return order, end
 
-    pred = [o["pred"] for o in ops]
+    pred = [o["pred"] + o["row"] for o in ops]
     way = [0.0] * n
     for i in range(n - 1, -1, -1):
         way[i] = max([lag(i, s) + way[s] for s in succ[i]] + [ops[i]["cost"] + ops[i]["late"]])
@@ -110,7 +114,7 @@ def rank_program(g, core, T, topo):
         return
     N = len(T.cores)
     qobj = {"v": g.vector, "s": g.scalar, "t": g.tensor, "g": g, "d": g.sync}
-    ops = []
+    ops, rows = [], {}
     recs = {}
     turn = {}
 
@@ -133,7 +137,11 @@ def rank_program(g, core, T, topo):
                 old = [r for r in old if not (lo <= r[0] and r[1] <= hi)]
             recs[name] = old + [(lo, hi, wr, i)]
         pred.discard(i)
-        ops.append({"q": q, "pred": sorted(pred), "emit": emit, "cost": cost, "late": late, "sem": sem})
+        key = (q, out[1][0][0] if out[1] else None)
+        row = [rows[key]] if key in rows and rows[key] not in pred else []
+        if key[1] in ROWS and q != "t":
+            rows[key] = i
+        ops.append({"row": row, "q": q, "pred": sorted(pred), "emit": emit, "cost": cost, "late": late, "sem": sem})
 
     def R(name, a=0, b=None, st=1):
         buf, base, w = PACK[name] if name in PACK else (name, 0, SCRATCH[name][1][1])
@@ -141,6 +149,9 @@ def rank_program(g, core, T, topo):
         ap = T[buf][:, base + a:base + b] if st == 1 else T[buf][:, base + a:base + b:st]
         size = 0 if buf in PSUM else 4 if SCRATCH[buf][2].endswith("32") else 2
         return (ap, [(buf, base + a, base + b)], -(-(b - a) // st), size, False)
+
+    def H(name, h, w=128):
+        return R(name, w * h, w * h + w)
 
     def C(name, j):
         return R(name, j, j + 1)
@@ -172,8 +183,9 @@ def rank_program(g, core, T, topo):
     def scan(out, a, b, o0, o1):
         op("v", out, [a, b], lambda e: e.tensor_tensor_scan(out[0], a[0], b[0], 0.0, o0, o1), cycles(out, [a, b], None))
 
-    def act(out, a, fn=Fn.Copy):
-        op("s", out, [a], lambda e: e.activation(out[0], a[0], fn), cycles(out, [a], 1))
+    def act(out, a, fn=Fn.Copy, scale=1.0, bias=0.0):
+        ins = [a] + [s for s in (scale, bias) if isinstance(s, tuple)]
+        op("s", out, ins, lambda e: e.activation(out[0], a[0], fn, bias=sc(bias), scale=sc(scale)), cycles(out, [a], 1))
 
     def mm(out, l, r, start=True, stop=True):
         op("t", out, [l, r], lambda e: e.matmul(out[0], l[0], r[0], start, stop), TENSOR * max(LEAST, r[2]) * (4 if l[3] == 4 else 1))
@@ -236,13 +248,16 @@ def rank_program(g, core, T, topo):
     ts(R("jt", 0, 128), R("ji", 0, 128), 4, Op.arith_shift_right)
     tc(R("qd16"), R("jt", 0, 128))
     ts(R("boh"), R("qd16"), R("pdiv"), Op.is_equal)
-    ts(R("bo"), R("qd16"), R("pdiv"), Op.is_equal)
-    for name, c in (("ob8h", 1), ("ob4h", 4), ("ob8", 1), ("om8", -0.125), ("o16", 16), ("o32", 32), ("om16", -16)):
+    act(R("bo"), R("boh"))
+    for name, c in (("ob8h", 1), ("ob4h", 4), ("ob8", 1)):
         ts(R(name), R("jf", 0, 8), R("pdiv"), Op.is_equal, float(c), Op.mult)
+    for name, c in (("om8", -0.125), ("o16", 16), ("o32", 32), ("om16", -16)):
+        act(R(name), R("ob8"), scale=float(c))
     for k in range(3):
-        ts(R("ob24", 8 * k, 8 * k + 8), R("jf", 0, 8), R("pdiv"), Op.is_equal)
-    for name, c in (("idb", 1), ("idn", -1), ("id256", 256), ("idk", 16384), ("idm", -0.0625), ("idf", 1), ("id4", 4)):
-        ts(R(name), R("jf", 0, 128), R("pcol"), Op.is_equal, float(c), Op.mult)
+        act(H("ob24", k, 8), R("ob8"))
+    ts(R("idb"), R("jf", 0, 128), R("pcol"), Op.is_equal)
+    for name, c in (("idn", -1), ("id256", 256), ("idk", 16384), ("idm", -0.0625), ("idf", 1), ("id4", 4)):
+        act(R(name), R("idb"), scale=float(c))
     ts(R("negm"), R("pat16"), R("p16"), Op.not_equal, -4096.0, Op.mult)
     ts(R("rst"), R("pat16"), 0.0, Op.is_equal, -8192.0, Op.mult)
     ts(R("big"), R("pat16", 0, 128), 0.0, Op.is_equal, 2.0 ** 20, Op.mult)
@@ -252,21 +267,22 @@ def rank_program(g, core, T, topo):
     ts(R("jt", 0, 128), R("ji", 0, 128), 3, Op.arith_shift_right, 7, Op.bitwise_and)
     ts(R("patc"), R("jt", 0, 128), -32.0, Op.add)
     fill(R("ones"), 1.0)
-    fill(R("quar"), -2.0 ** -14)
-    ts(R("is0"), R("pcol"), 0.0, Op.is_equal)
-    ts(R("rowc"), R("pat16", 0, 128), R("is0"), Op.mult)
+    act(R("quar"), R("ones"), scale=-2.0 ** -14)
+    act(R("rowc"), R("pat16", 0, 128), scale=1.0 / 128)
     for k, c in enumerate((-1.0, -1.0, -5.0)):
-        ts(R("crow", 16 * k, 16 * k + 16), R("ones", 0, 16), R("is0"), Op.mult, c, Op.mult)
-    ts(R("brow"), R("ones", 0, 16), R("is0"), Op.mult, float(B0), Op.mult)
-    ts(R("tmp", 0, 128), R("jf", 0, 128), R("pcol"), Op.is_gt, -2.0 ** -14, Op.mult)
-    ts(R("tm2", 0, 128), R("idb"), 1.0 / 32, Op.mult)
-    tt(R("tri"), R("tmp", 0, 128), R("tm2", 0, 128), Op.add)
-    ts(R("i128"), R("jf", 0, 128), 0.0, Op.add)
+        act(H("crow", k, 16), R("ones", 0, 16), scale=c / 128)
+    act(R("brow"), R("ones", 0, 16), scale=B0 / 128)
+    ts(R("tri"), R("jf", 0, 128), R("pcol"), Op.is_gt, -2.0 ** -14, Op.mult)
+    act(R("id32"), R("idb"), scale=1.0 / 32)
+    act(R("i128"), R("jf", 0, 128))
     ts(R("dump"), R("jf", 0, 8), 16.0, Op.mult, R("p16"), Op.add)
-    ts(R("q16"), R("dump"), 16.0, Op.mult)
-    ts(R("odd"), R("p16"), 2.0, Op.mult, 1.0, Op.add)
-    ts(R("odd32"), R("odd"), 32.0, Op.mult)
-    ts(R("bow"), R("bo"), R("odd"), Op.mult)
+    act(R("q16"), R("dump"), scale=16.0)
+    act(R("odd"), R("p16"), scale=2.0, bias=1.0)
+    act(R("odd32"), R("p16"), scale=64.0, bias=32.0)
+    act(R("bow"), R("bo"), scale=R("odd"))
+    for k, nv in enumerate(SHARES):
+        ts(R("tm2", 128, 256), R("pat16", 0, 128), float(nv), Op.is_ge, 16.0, Op.mult)
+        tt(H("bs", k), R("tm2", 128, 256), R("bo"), Op.mult)
     for c in range(15):
         if c != 7:
             fill(R("eb", 256 * c + 128 * (c >= 8), 272 * c + 16), 0.0)
@@ -277,17 +293,14 @@ def rank_program(g, core, T, topo):
     tc(R("als"), R("a0i"))
     tt(R("os"), IND(R("als"), R("e16")), R("mask16"), Op.mult)
 
-    RB, KB, SB = ("ps0", "ps7"), ("ps2", "ps5"), ("ps6", "ps7", "ps0")
-
-    def H(name, h, w=128):
-        return R(name, w * h, w * h + w)
+    RB, KB = ("ps0", "ps7"), ("ps2", "ps5")
 
     def states(t, h):
         mm(R(RB[h], 0, 128), R("idb"), H("negm", h), True, False)
         mm(R(RB[h], 0, 128), R("boh"), H("os", h), False, False)
         mm(R(RB[h], 128, 256), R("boh"), H("os", h), False, True)
         scan(H("sl", h), H("rst", h), R(RB[h], 0, 128), Op.add, Op.max)
-        tc(H("arow", h), R(RB[h], 128, 256))
+        act(H("arow", h), R(RB[h], 128, 256))
         tt(H("dg", h), H("sl", h), R(RB[h], 128, 256), Op.is_equal)
         tc(H("alu", h, 8), R("sl", 128 * h + 15, 128 * h + 128, 16))
         tc(H("suu", h), IND(R("sui", 0, 2048), H("alu", h, 8)))
@@ -312,10 +325,10 @@ def rank_program(g, core, T, topo):
         ts(R("alo"), R("ail"), 127, Op.bitwise_and)
         tc(R("alou"), R("alo"))
         act(R("gc_"), IND(R("cw"), R("alou")))
-        mm(R("ps6", 0, 256), R("id256"), R("ah"), True, False)
+        mm(R("ps0", 256, 512), R("id256"), R("ah"), True, False)
         for h in (0, 1):
-            mm(H("ps6", h), H("gc_", h), R("idb"), False, h == 1)
-        scan(R("lk"), R("rst"), R("ps6", 0, 256), Op.add, Op.max)
+            mm(H("ps0", 2 + h), H("gc_", h), R("idb"), False, h == 1)
+        scan(R("lk"), R("rst"), R("ps0", 256, 512), Op.add, Op.max)
         tc(R("lki"), R("lk", 15, 256, 16))
         ts(R("hfi", 0, 16), R("lki"), 3, Op.arith_shift_right, 3, Op.bitwise_and)
         ts(R("hfi", 16, 32), R("lki"), 7, Op.bitwise_and)
@@ -348,6 +361,7 @@ def rank_program(g, core, T, topo):
         ts(R("sou"), R("ps1", 80, 96), 0.375, Op.add)
         act(R("sp"), IND(R("sui"), R("sou")))
         mm(R("ps3", 384, 400), R("idm"), R("bn", 16, 32), True, False)
+        mm(R("ps3", 384, 400), R("id32"), R("bn", 0, 16), False, False)
         mm(R("ps3", 384, 400), R("tri"), R("bn", 0, 16), False, False)
         mm(R("ps3", 385, 400, 2), R("quar"), R("bn", 0, 16, 2), False, True)
         if t < ASKS:
@@ -402,12 +416,8 @@ def rank_program(g, core, T, topo):
             send(1 + (t + 1) % (N - 1), 0, R("zin%d" % (t + 1)), R(zn), "rz%d" % (t + 1))
 
     def dist(t):
-        zn, nv = "zz%d" % (t + 1), 16 - NS[t]
-        if t == 0 or NS[t] != NS[t - 1]:
-            ts(R("tm2", 128, 256), R("pat16", 0, 128), float(nv), Op.is_ge, 16.0, Op.mult)
-            tt(R("bs"), R("tm2", 128, 256), R("bo"), Op.mult)
-        parts = -(-NS[t] // 4)
-        chunks = [(h, list(range(nv, 16))[k::parts]) for h in (0, 1) for k in range(parts)]
+        zn = "zz%d" % (t + 1)
+        chunks = [(h, range(m, min(m + 4, 16))) for h in (0, 1) for m in range(16 - NS[t][h], 16, 4)]
 
         def cc(h, m):
             return R("cc", 2048 * h + m, 2048 * h + 2048, 16)
@@ -415,28 +425,25 @@ def rank_program(g, core, T, topo):
         def mx(h, m):
             return H("mx", 16 * h + m)
 
-        place = {}
         for k, (h, ms) in enumerate(chunks):
-            bank = SB[k % len(SB)]
+            bank = RB[k % 2]
             for j, m in enumerate(ms):
                 mm(H(bank, j), R("idb"), cc(h, m), j == 0, False)
             for j, m in enumerate(ms):
                 mm(H(bank, j), R("idn"), H(zn, h), False, j == len(ms) - 1)
-            at = 16 * h + nv + sum(len(c[1]) for c in chunks[:k] if c[0] == h)
-            act(R("mx", 128 * at, 128 * (at + len(ms))), R(bank, 0, 128 * len(ms)), Fn.Abs)
-            for j, m in enumerate(ms):
-                place[h, m] = at + j
+            act(R("mx", 128 * (16 * h + ms[0]), 128 * (16 * h + ms[-1] + 1)), R(bank, 0, 128 * len(ms)), Fn.Abs)
         for h in (0, 1):
+            nv = 16 - NS[t][h]
             mm(R(KB[h], 0, 128), R("ones"), R("rowc"), True, False)
             for m in range(nv):
                 mm(R(KB[h], m, 128, 16), cc(h, m), R("om16"), False, False)
-            if NS[t]:
-                mm(R(KB[h], 0, 128), H(zn, h), R("bs"), False, False)
+            if 0 < nv < 16:
+                mm(R(KB[h], 0, 128), H(zn, h), H("bs", SHARES.index(nv)), False, False)
             for m in range(nv):
                 tt(mx(h, m), cc(h, m), H("ps3", h), Op.max)
                 mm(R(KB[h], m, 128, 16), mx(h, m), R("o32"), False, m == 15)
             for m in range(nv, 16):
-                mm(R(KB[h], m, 128, 16), H("mx", place[h, m]), R("o16"), False, m == 15)
+                mm(R(KB[h], m, 128, 16), mx(h, m), R("o16"), False, m == 15)
 
     def choose(t, h):
         scan(H("ksc", h), R("big"), R(KB[h], 0, 128), Op.add, Op.min)
@@ -447,26 +454,26 @@ def rank_program(g, core, T, topo):
 
     def answer(t):
         qpin = R("qpin%d" % t)
+        mm(R("ps4", 0, 256), R("bow"), R("zin%d" % t))
+        tc(R("ui"), R("ps4", 0, 256))
+        ts(R("uu"), R("ui"), 4095, Op.bitwise_and)
+        ts(R("ps4", 256, 512), R("uu"), R("odd32"), Op.add)
+        tt(R("pr"), R("uu"), R("ps4", 256, 512), Op.mult)
+        ts(R("ux"), R("pr"), 5, Op.arith_shift_right, 8191, Op.bitwise_and)
         ts(R("dq", 0, 8), qpin, 14, Op.arith_shift_right)
         ts(R("dq", 8, 16), qpin, 2, Op.arith_shift_right, 4095, Op.bitwise_and)
         tc(R("dqu"), R("dq"))
         act(R("zq"), IND(R("zin%d" % t), R("dqu", 0, 8)))
         act(R("goal"), IND(R("xw"), R("dqu", 8, 16)))
-        mm(R("ps4", 0, 128), R("bow"), R("zq"))
-        mm(R("ps3", 256, 384), R("idn"), R("zq"), True, False)
-        mm(R("ps3", 256, 384), R("idb"), R("goal"), False, True)
-        tc(R("ui"), R("ps4", 0, 128))
-        ts(R("uu"), R("ui"), 4095, Op.bitwise_and)
-        ts(R("ps4", 128, 256), R("uu"), R("odd32"), Op.add)
-        tt(R("pr"), R("uu"), R("ps4", 128, 256), Op.mult)
-        ts(R("ux"), R("pr"), 5, Op.arith_shift_right, 8191, Op.bitwise_and)
-        tc(R("cou"), R("ux"))
+        mm(R("ps6", 0, 128), R("idn"), R("zq"), True, False)
+        mm(R("ps6", 0, 128), R("idb"), R("goal"), False, True)
+        tc(R("cou"), IND(R("ux"), R("dqu", 0, 8)))
         for k in range(2):
             act(H("cand", k, 1024), IND(R("bank", B0), H("cou", k, 64)))
         mm(R("ps4", 256, 384), R("ones"), R("rowc"), True, False)
         for m in range(16):
             mm(R("ps4", 256 + m, 384, 16), R("cand", m, 2048, 16), R("om16"), False, False)
-            tt(H("mq", m), R("cand", m, 2048, 16), R("ps3", 256, 384), Op.max)
+            tt(H("mq", m), R("cand", m, 2048, 16), R("ps6", 0, 128), Op.max)
             mm(R("ps4", 256 + m, 384, 16), H("mq", m), R("o32"), False, m == 15)
         scan(R("kq"), R("big"), R("ps4", 256, 384), Op.add, Op.min)
         tc(R("ki"), R("kq", 15, 128, 16))

@@ -3,7 +3,8 @@ from concourse.mybir import AluOpType as Op, ActivationFunctionType as Fn
 STEPS = 4
 ASKS = STEPS - 1
 NS = [(8, 0)] * 4
-SHARES = sorted({16 - n for x in NS for n in x} - {0, 16})
+NQ = 4
+SHARES = sorted({16 - n for x in NS + [(NQ,)] for n in x} - {0, 16})
 B0, BD = 192, 8384
 X0 = B0 // 4
 PSUM = ["ps%d" % i for i in range(8)]
@@ -11,22 +12,21 @@ SCRATCH = {}
 for _n in PSUM:
     SCRATCH[_n] = ("psum", [128, 512], "float32")
 WIDE = {"xw": (X0 + 2048, "bfloat16"), "sui": (4096, "int32"), "bank": (BD, "bfloat16"), "cc": (4096, "bfloat16"), "mx": (4096, "bfloat16"),
-        "cand": (2048, "bfloat16"), "mq": (2048, "bfloat16"), "eb": (4096, "bfloat16"), "hot": (2048, "bfloat16")}
+        "cand": (2048, "bfloat16"), "mq": (2048, "float16"), "eb": (4096, "bfloat16"), "hot": (2048, "bfloat16")}
 for _t in range(STEPS + 1):
     WIDE["zz%d" % _t] = (256, "bfloat16")
 for _n, (_w, _d) in WIDE.items():
     SCRATCH[_n] = ("sbuf", [128, _w], _d)
 NARROW = {
-    "float32": "pcol 1 p16 1 pdiv 1 odd 1 odd32 1 p8 1 is0 1 jf 256 pat16 256 patc 128 mask16 256 qd16 128 tmp 256 tm2 256 dump 8 idf 128 id4 128 "
-               "als 16 sl 256 y 16 put 16 w7 16 w 16 pv 16 ca 256 cb 128 cb2 128 qs 64 alof 16 lk 256 sp 256 ksc 256 kmin 256 kq 128 arf 256 "
-               "ohf 128 oyf 128",
-    "int32": "ci 1 ci2 1 ci3 1 ci4 1 ji 256 jt 256 hi0 128 fi0 128 a0i 16 ail 16 alo 16 ait 16 ahit 16 alot 16 lki 16 hfi 32 xi 16 x3 16 ri 16 rlo 16 "
-             "rhi 16 v1 8 dq 16 ui 256 uu 256 pr 256 ux 256 ki 8 mi 8 w1 128 w2 128 w3 128",
-    "uint16": "e16 16 et16 16 e15 16 e8 8 alu 16 alou 16 suu 256 offu 16 sou 16 dqu 16 cou 128 seu 8",
-    "bfloat16": "bo 128 bow 128 ob8 8 ob24 24 om8 8 o16 8 o32 8 om16 8 idb 128 idn 128 id256 128 idk 128 idm 128 id32 128 tri 128 ones 128 quar 128 i128 128 "
-                "negm 256 rst 256 big 128 keep 64 gneg 64 lanb 16 rowc 128 crow 48 brow 16 q16 8 bs 512 dg 256 bn 32 ay 256 zs 256 oh 256 goal 128 "
-                "zq 128 aq 128 gc_ 256 ah 256 hfb 32 cw 128 ut 128",
-    "float16": "boh 128 ob8h 8 ob4h 8 arow 256 os 256"}
+    "float32": "pcol 1 p16 1 pdiv 1 odd 1 odd32 1 p8 1 huge 1 p8h 2 pat8 64 jf 128 pat16 256 patc 128 mask16 256 qd16 128 tmp 128 tm2 128 dump 8 "
+               "idf 128 id4 128 sl 256 y 16 put 16 w7 16 w 16 pv 16 ca 256 cb 128 cb2 128 qs 64 alof 16 sp 256 ksc 256 kmin 256 arf 256 ohf 128 oyf 128",
+    "int32": "ci 1 ci2 1 ci3 1 ci4 1 hi0 128 fi0 128 a0i 16 ail 16 alo 16 ait 16 ahit 16 alot 16 lk 256 hfi 32 xi 16 x3 16 ri 16 rlo 16 "
+             "rhi 16 v1 8 dq 16 ui 256 uu 256 pr 256 ux 256 kq 128 mi 8 w1 128 w2 128 w3 128",
+    "uint16": "e16 16 et16 16 e15 8 e8 8 alu 16 alou 16 suu 256 offu 16 sou 16 dqu 16 cou 128 seu 8",
+    "bfloat16": "bo 128 bow 128 ob8 8 ob24 24 om8 8 o16 8 o32 8 om16 8 idb 128 idn 128 id256 128 idk 128 idm 128 id32 128 tri 128 ones 128 quar 128 "
+                "i128 128 negm 256 rst 256 big 256 keep 64 gneg 64 lanb 16 rowc 128 crow 48 brow 16 q16 8 bs 512 dg 256 bn 32 ay 256 zs 256 oh 256 "
+                "goal 128 zq 128 wq 128 aq 128 gc_ 256 ah 256 hfb 32 cw 128 ut 128",
+    "float16": "boh 128 ob8h 8 ob4h 8 o16h 8 o32h 8 arow 256 os 256"}
 PACK = {}
 for _d, _t in NARROW.items():
     _at, _f = 0, _t.split()
@@ -41,70 +41,76 @@ for _t in range(ASKS):
 LOADS = ["la", "ls", "lx", "lh0", "lf0", "lz", "lg"]
 SEMAPHORES = ["sv", "ss", "st", "sg", "sent", "sout"] + LOADS + ["%s%d" % (n, t) for t in range(ASKS) for n in ("rp", "rz", "ra")]
 
-GATHER, SCATTER, LEAST, WAKE, HOP, DMA, BYTES = 1.56, 3.8, 64, 130, 1800, 1500, 200
-TENSOR, PATIENCE, SWEEPS = 0.75, 0.25, 6
+GATHER, SCATTER, LEAST, WAKE, HOP, FIRST, DMA, BYTES, TENSOR = 1.56, 3.8, 64, 130, 1800, 2500, 1500, 450, 0.75
+PATIENCE, BUSY, SWEEPS, SHAKE = 0.25, 2, 30, 2000
 ROWS = ("cc", "cand", "mx", "mq", "eb", "hot")
 ORDER = []
 
 
 def plan(ops):
     n = len(ops)
-    succ = [[] for _ in ops]
+    cost, late = [o["cost"] for o in ops], [o["late"] for o in ops]
+    fore, back = [[] for _ in ops], [[] for _ in ops]
     for i, o in enumerate(ops):
-        for p in o["pred"] + o["row"]:
-            succ[p].append(i)
+        for p in o["pred"]:
+            lag = 0 if "t" in cost[p] and "t" in cost[i] else late[p] + WAKE
+            fore[p].append((i, lag))
+            back[i].append((p, lag))
 
-    def lag(p, i):
-        if p in ops[i]["row"]:
-            return ops[p]["cost"]
-        return ops[p]["cost"] + ops[p]["late"] + (0 if ops[p]["q"] == ops[i]["q"] == "t" else WAKE)
-
-    def sweep(before, after, gap, ready, way):
+    def sweep(before, after, ready, way):
         left = [len(x) for x in before]
         pool = {q: [] for q in "vstgd"}
         free = {q: 0.0 for q in pool}
         for i in range(n):
             if not left[i]:
-                pool[ops[i]["q"]].append(i)
-        order, end = [], [0.0] * n
+                for q in cost[i]:
+                    pool[q].append(i)
+        order, end, coming = [], [0.0] * n, {}
         while len(order) < n:
-            best = None
+            coming.pop("v", None)
             for q, L in pool.items():
-                if L:
+                if q == "v":
+                    L = [i for i in L if "s" not in cost[i] or free["s"] > max(free["v"], ready[i]) + BUSY * cost[i]["v"]]
+                if L and q not in coming:
                     now = max(free[q], min(ready[i] for i in L))
-                    pick = max((i for i in L if ready[i] <= now), key=lambda i: (way[i], -i))
-                    soon = [i for i in L if way[i] > way[pick] and ready[i] < now + PATIENCE * ops[pick]["cost"]]
-                    if soon:
-                        pick = max(soon, key=lambda i: (way[i], -i))
-                    at = max(now, ready[pick])
-                    if best is None or at < best[0]:
-                        best = (at, pick)
-            at, i = best
-            q = ops[i]["q"]
-            pool[q].remove(i)
-            free[q] = end[i] = at + ops[i]["cost"]
-            order.append(i)
-            for s in after[i]:
-                ready[s] = max(ready[s], at + gap(i, s))
+                    pick = max((i for i in L if ready[i] <= now), key=lambda i: way[i])
+                    pick = max((i for i in L if ready[i] <= now + PATIENCE * cost[pick][q]), key=lambda i: way[i])
+                    coming[q] = (max(now, ready[pick]), q != "s", pick, q)
+            at, _, i, q = min(coming.values())
+            for x in cost[i]:
+                pool[x].remove(i)
+                coming.pop(x, None)
+            free[q] = end[i] = at + cost[i][q]
+            order.append((i, q))
+            for s, lag in after[i]:
+                ready[s] = max(ready[s], end[i] + lag)
                 left[s] -= 1
                 if not left[s]:
-                    pool[ops[s]["q"]].append(s)
+                    for x in cost[s]:
+                        pool[x].append(s)
+                        coming.pop(x, None)
         return order, end
 
-    pred = [o["pred"] + o["row"] for o in ops]
-    way = [0.0] * n
+    way, row = [0.0] * n, {}
     for i in range(n - 1, -1, -1):
-        way[i] = max([lag(i, s) + way[s] for s in succ[i]] + [ops[i]["cost"] + ops[i]["late"]])
-    best = None
-    for _ in range(SWEEPS):
+        way[i] = max(cost[i].values()) + max([lag + way[s] for s, lag in fore[i]] + [late[i], row.get(ops[i]["row"], 0)])
+        if ops[i]["row"]:
+            row[ops[i]["row"]] = way[i]
+    best, seed = None, 1
+    for k in range(SWEEPS):
         for i in range(n):
-            if ops[i]["sem"] and not pred[i]:
+            if ops[i]["sem"] and not back[i]:
                 way[i] = 1e9 - i
-        order, end = sweep(pred, succ, lag, [0.0] * n, way)
-        total = max(end[i] + ops[i]["late"] for i in range(n))
+        order, end = sweep(back, fore, [0.0] * n, way)
+        total = max(end[i] + late[i] for i in range(n))
         if best is None or total < best[0]:
-            best = (total, order)
-        way = sweep(succ, pred, lambda s, p: ops[s]["cost"] + lag(p, s) - ops[p]["cost"], [0.0 if succ[i] else float(ops[i]["late"]) for i in range(n)], end)[1]
+            best = (total, order, end)
+        if k % 3 == 2:
+            end = list(best[2])
+            for i in range(n):
+                seed = (seed * 1103515245 + 12345) % 2 ** 31
+                end[i] += SHAKE * seed / 2 ** 31
+        way = sweep(fore, back, [0.0 if fore[i] else float(late[i]) for i in range(n)], end)[1]
     return best[1]
 
 
@@ -114,7 +120,7 @@ def rank_program(g, core, T, topo):
         return
     N = len(T.cores)
     qobj = {"v": g.vector, "s": g.scalar, "t": g.tensor, "g": g, "d": g.sync}
-    ops, rows = [], {}
+    ops = []
     recs = {}
     turn = {}
 
@@ -127,7 +133,7 @@ def rank_program(g, core, T, topo):
                     pred.add(r[3])
         for name in sorted({x[0] for _, x in refs if x[0] in PSUM}):
             has, cur, prev = turn.get(name, (q, [], []))
-            if has != q:
+            if has != q or q == "vs":
                 cur, prev = [], cur
             pred.update(prev + (cur[-1:] if q == "t" else []))
             turn[name] = (q, cur + [i], prev)
@@ -137,11 +143,10 @@ def rank_program(g, core, T, topo):
                 old = [r for r in old if not (lo <= r[0] and r[1] <= hi)]
             recs[name] = old + [(lo, hi, wr, i)]
         pred.discard(i)
-        key = (q, out[1][0][0] if out[1] else None)
-        row = [rows[key]] if key in rows and rows[key] not in pred else []
-        if key[1] in ROWS and q != "t":
-            rows[key] = i
-        ops.append({"row": row, "q": q, "pred": sorted(pred), "emit": emit, "cost": cost, "late": late, "sem": sem})
+        row = (q, out[1][0][0]) if out[1] and out[1][0][0] in ROWS else None
+        if q != "vs":
+            emit, cost = {q: emit}, {q: cost}
+        ops.append({"row": row, "pred": sorted(pred), "emit": emit, "cost": cost, "late": late, "sem": sem})
 
     def R(name, a=0, b=None, st=1):
         buf, base, w = PACK[name] if name in PACK else (name, 0, SCRATCH[name][1][1])
@@ -187,11 +192,15 @@ def rank_program(g, core, T, topo):
         ins = [a] + [s for s in (scale, bias) if isinstance(s, tuple)]
         op("s", out, ins, lambda e: e.activation(out[0], a[0], fn, bias=sc(bias), scale=sc(scale)), cycles(out, [a], 1))
 
+    def cp(out, a):
+        op("vs", out, [a], {"v": lambda e: e.tensor_copy(out[0], a[0]), "s": lambda e: e.activation(out[0], a[0], Fn.Copy)},
+           {"v": cycles(out, [a], None), "s": cycles(out, [a], 1)})
+
     def mm(out, l, r, start=True, stop=True):
         op("t", out, [l, r], lambda e: e.matmul(out[0], l[0], r[0], start, stop), TENSOR * max(LEAST, r[2]) * (4 if l[3] == 4 else 1))
 
-    def iota(out, pattern, cm):
-        op("g", out, [], lambda e: e.iota(out[0], pattern, 0, cm), 160 + 2 * out[2])
+    def iota(out, pattern, base=0, cm=0):
+        op("g", out, [], lambda e: e.iota(out[0], pattern, base, cm, allow_small_or_imprecise_dtypes=True), 160 + 2 * out[2])
 
     def fill(out, c):
         op("v", out, [], lambda e: e.memset(out[0], c), cycles(out, [out], None))
@@ -204,13 +213,13 @@ def rank_program(g, core, T, topo):
 
     sends, arrive = [0], {}
 
-    def send(to, frm, out, src, sem):
+    def send(to, out, src, sem):
         dst, peer = T.cores[(rank + to) % N], T.cores[(rank - to) % N]
         rid, pid = topo.addr(dst)[:2]
         arrive[sem] = len(topo.engines(peer, core))
         sends[0] += len(topo.engines(core, dst))
         op("g", out, [src], lambda e: e.remote_dma(out[0], src[0], T.sem[sem], T.sem["sent"], pid, rid, topo.mask(core, dst)),
-           HOP / 4, HOP + 128 * out[2] * out[3] / 80, (sem, arrive[sem]))
+           HOP / 4 + (0 if len(arrive) > 1 else FIRST), HOP + 128 * out[2] * out[3] / 80, (sem, arrive[sem]))
 
     outs = [0]
 
@@ -226,72 +235,65 @@ def rank_program(g, core, T, topo):
     load("d", R("xw", X0), T.xs[:, :], "lx")
     load("d", R("bank", B0), T.gs[:, :], "lg")
 
-    iota(R("ci"), [[1, 1]], 1)
-    iota(R("ji"), [[1, 256]], 0)
-    iota(R("sui", 2048, 4096), [[1, 2048]], 0)
-    tc(R("pcol"), R("ci"))
-    tc(R("jf"), R("ji"))
+    iota(R("ci"), [[1, 1]], 0, 1)
+    iota(R("pat16"), [[0, 16], [1, 16]])
+    iota(R("jf"), [[1, 128]])
+    iota(R("qd16"), [[1, 8], [0, 16]])
+    iota(R("lanb"), [[0, 8], [128, 2]], 0, 1)
+    iota(R("patc"), [[0, 2], [1, 8], [0, 8]], -32)
+    iota(R("pat8"), [[0, 8], [1, 8]])
+    iota(R("sui", 2048, 4096), [[1, 2048]])
+    fill(R("ones"), 1.0)
+    fill(R("huge"), 2.0 ** 20)
+    cp(R("pcol"), R("ci"))
     for name, tmp, c, o in (("p16", "ci2", 15, Op.bitwise_and), ("pdiv", "ci3", 4, Op.arith_shift_right), ("p8", "ci4", 7, Op.bitwise_and)):
         ts(R(tmp), R("ci"), c, o)
-        tc(R(name), R(tmp))
-    ts(R("jt"), R("ji"), 15, Op.bitwise_and)
-    tc(R("pat16"), R("jt"))
+        cp(R(name), R(tmp))
     ts(R("mask16"), R("pat16"), R("p16"), Op.is_equal)
-    tc(R("e16"), R("ji", 0, 16))
-    ts(R("e15"), R("jf", 0, 16), 16.0, Op.mult, 15.0, Op.add)
+    tc(R("e16"), R("pat16", 0, 16))
+    ts(R("e15"), R("pat16", 0, 8), 16.0, Op.mult, 15.0, Op.add)
     for h in (0, 1):
-        ts(R("et16", 8 * h, 8 * h + 8), R("jf", 0, 8), 2.0, Op.mult, float(h), Op.add)
-        ts(R("e8", 4 * h, 4 * h + 4), R("jf", 0, 4), 0.0, Op.mult, R("p8"), Op.add)
-        ts(R("e8", 4 * h, 4 * h + 4), R("e8", 4 * h, 4 * h + 4), 2.0, Op.mult, float(h), Op.add)
-        ts(R("lanb", h, 16, 2), R("jf", 0, 8), 0.0, Op.mult, R("pcol"), Op.add)
-    ts(R("lanb", 1, 16, 2), R("lanb", 1, 16, 2), 128.0, Op.add)
-    ts(R("jt", 0, 128), R("ji", 0, 128), 4, Op.arith_shift_right)
-    tc(R("qd16"), R("jt", 0, 128))
+        ts(H("et16", h, 8), R("pat16", 0, 8), 2.0, Op.mult, float(h), Op.add)
+        act(C("p8h", h), R("p8"), scale=2.0, bias=float(h))
+        ts(H("e8", h, 4), R("pat16", 0, 4), 0.0, Op.mult, C("p8h", h), Op.add)
     ts(R("boh"), R("qd16"), R("pdiv"), Op.is_equal)
-    act(R("bo"), R("boh"))
-    for name, c in (("ob8h", 1), ("ob4h", 4), ("ob8", 1)):
-        ts(R(name), R("jf", 0, 8), R("pdiv"), Op.is_equal, float(c), Op.mult)
-    for name, c in (("om8", -0.125), ("o16", 16), ("o32", 32), ("om16", -16)):
+    cp(R("bo"), R("boh"))
+    ts(R("ob8"), R("pat16", 0, 8), R("pdiv"), Op.is_equal)
+    for name, c in (("ob8h", 1), ("ob4h", 4), ("om8", -0.125), ("o16", 16), ("o32", 32), ("om16", -16), ("o16h", 16), ("o32h", 32)):
         act(R(name), R("ob8"), scale=float(c))
     for k in range(3):
-        act(H("ob24", k, 8), R("ob8"))
-    ts(R("idb"), R("jf", 0, 128), R("pcol"), Op.is_equal)
-    for name, c in (("idn", -1), ("id256", 256), ("idk", 16384), ("idm", -0.0625), ("idf", 1), ("id4", 4)):
+        cp(H("ob24", k, 8), R("ob8"))
+    ts(R("idb"), R("jf"), R("pcol"), Op.is_equal)
+    for name, c in (("idn", -1), ("id256", 256), ("idk", 16384), ("idm", -0.0625), ("id32", 1 / 32), ("idf", 1), ("id4", 4)):
         act(R(name), R("idb"), scale=float(c))
-    ts(R("negm"), R("pat16"), R("p16"), Op.not_equal, -4096.0, Op.mult)
-    ts(R("rst"), R("pat16"), 0.0, Op.is_equal, -8192.0, Op.mult)
-    ts(R("big"), R("pat16", 0, 128), 0.0, Op.is_equal, 2.0 ** 20, Op.mult)
-    ts(R("jt", 128, 192), R("ji", 0, 64), 7, Op.bitwise_and)
-    ts(R("keep"), R("jt", 128, 192), 0.0, Op.not_equal)
-    ts(R("gneg"), R("jt", 128, 192), R("pdiv"), Op.not_equal, -2.0 ** 31, Op.mult)
-    ts(R("jt", 0, 128), R("ji", 0, 128), 3, Op.arith_shift_right, 7, Op.bitwise_and)
-    ts(R("patc"), R("jt", 0, 128), -32.0, Op.add)
-    fill(R("ones"), 1.0)
+    act(R("negm"), R("mask16"), scale=4096.0, bias=-4096.0)
+    act(R("big"), R("pat16"), Fn.Relu, scale=-2.0 ** 20, bias=R("huge"))
+    act(R("rst"), R("big"), scale=-2.0 ** -7)
+    act(R("keep"), R("pat8"), Fn.Sign)
+    ts(R("gneg"), R("pat8"), R("pdiv"), Op.not_equal, -2.0 ** 31, Op.mult)
     act(R("quar"), R("ones"), scale=-2.0 ** -14)
     act(R("rowc"), R("pat16", 0, 128), scale=1.0 / 128)
     for k, c in enumerate((-1.0, -1.0, -5.0)):
         act(H("crow", k, 16), R("ones", 0, 16), scale=c / 128)
     act(R("brow"), R("ones", 0, 16), scale=B0 / 128)
-    ts(R("tri"), R("jf", 0, 128), R("pcol"), Op.is_gt, -2.0 ** -14, Op.mult)
-    act(R("id32"), R("idb"), scale=1.0 / 32)
-    act(R("i128"), R("jf", 0, 128))
-    ts(R("dump"), R("jf", 0, 8), 16.0, Op.mult, R("p16"), Op.add)
+    ts(R("tri"), R("jf"), R("pcol"), Op.is_gt, -2.0 ** -14, Op.mult)
+    cp(R("i128"), R("jf"))
+    act(R("dump"), R("pat16", 0, 8), Fn.Identity, scale=16.0, bias=R("p16"))
     act(R("q16"), R("dump"), scale=16.0)
     act(R("odd"), R("p16"), scale=2.0, bias=1.0)
     act(R("odd32"), R("p16"), scale=64.0, bias=32.0)
     act(R("bow"), R("bo"), scale=R("odd"))
     for k, nv in enumerate(SHARES):
-        ts(R("tm2", 128, 256), R("pat16", 0, 128), float(nv), Op.is_ge, 16.0, Op.mult)
-        tt(H("bs", k), R("tm2", 128, 256), R("bo"), Op.mult)
+        ts(R("tm2"), R("pat16", 0, 128), float(nv), Op.is_ge, 16.0, Op.mult)
+        tt(H("bs", k), R("tm2"), R("bo"), Op.mult)
     for c in range(15):
         if c != 7:
             fill(R("eb", 256 * c + 128 * (c >= 8), 272 * c + 16), 0.0)
     fill(R("bank", 0, B0), 0.0)
     fill(R("xw", 0, X0), 0.0)
-    ts(R("tmp", 128, 256), R("hi0"), 8.0, Op.mult)
-    tt(R("cw"), R("tmp", 128, 256), R("fi0"), Op.add)
-    tc(R("als"), R("a0i"))
-    tt(R("os"), IND(R("als"), R("e16")), R("mask16"), Op.mult)
+    act(R("tmp"), R("hi0"), scale=8.0)
+    tt(R("cw"), R("tmp"), R("fi0"), Op.add)
+    tt(R("os"), IND(R("a0i"), R("e16")), R("mask16"), Op.mult)
 
     RB, KB = ("ps0", "ps7"), ("ps2", "ps5")
 
@@ -300,15 +302,14 @@ def rank_program(g, core, T, topo):
         mm(R(RB[h], 0, 128), R("boh"), H("os", h), False, False)
         mm(R(RB[h], 128, 256), R("boh"), H("os", h), False, True)
         scan(H("sl", h), H("rst", h), R(RB[h], 0, 128), Op.add, Op.max)
-        act(H("arow", h), R(RB[h], 128, 256))
+        cp(H("arow", h), R(RB[h], 128, 256))
         tt(H("dg", h), H("sl", h), R(RB[h], 128, 256), Op.is_equal)
-        tc(H("alu", h, 8), R("sl", 128 * h + 15, 128 * h + 128, 16))
-        tc(H("suu", h), IND(R("sui", 0, 2048), H("alu", h, 8)))
-        for k in (2 * h, 2 * h + 1):
-            act(H("cc", k, 1024), IND(R("xw", X0), H("suu", k, 64)))
+        cp(H("alu", h, 8), R("sl", 128 * h + 15, 128 * h + 128, 16))
+        cp(H("suu", h), IND(R("sui", 0, 2048), H("alu", h, 8)))
+        for k in range(4 * h, 4 * h + 4):
+            cp(H("cc", k, 512), IND(R("xw", X0), H("suu", k, 32)))
 
     def places(t):
-        al = R("sl", 15, 256, 16)
         for h in (0, 1):
             mm(R("ps1", 160 + h, 176, 2), H("os", h), R("ob8h"), h == 0, h == 1 and t == ASKS)
         if t < ASKS:
@@ -316,23 +317,22 @@ def rank_program(g, core, T, topo):
             mm(R("ps1", 176, 192), R("idk"), R("lanb"), False, False)
             for h in (0, 1):
                 mm(R("ps1", 176 + h, 192, 2), H("os", h), R("ob4h"), False, h == 1)
-        tc(R("ait"), R("ps1", 160, 176))
+        cp(R("ait"), R("ps1", 160, 176))
         ts(R("ahit"), R("ait"), 7, Op.arith_shift_right)
         ts(R("alot"), R("ait"), 127, Op.bitwise_and)
-        tc(R("alof"), R("alot"))
+        cp(R("alof"), R("alot"))
         tt(R("ah"), IND(R("ahit"), R("et16")), R("pat16"), Op.is_equal)
-        tc(R("ail"), al)
+        cp(R("ail"), R("sl", 15, 256, 16))
         ts(R("alo"), R("ail"), 127, Op.bitwise_and)
-        tc(R("alou"), R("alo"))
-        act(R("gc_"), IND(R("cw"), R("alou")))
+        cp(R("alou"), R("alo"))
+        cp(R("gc_"), IND(R("cw"), R("alou")))
         mm(R("ps0", 256, 512), R("id256"), R("ah"), True, False)
         for h in (0, 1):
             mm(H("ps0", 2 + h), H("gc_", h), R("idb"), False, h == 1)
         scan(R("lk"), R("rst"), R("ps0", 256, 512), Op.add, Op.max)
-        tc(R("lki"), R("lk", 15, 256, 16))
-        ts(R("hfi", 0, 16), R("lki"), 3, Op.arith_shift_right, 3, Op.bitwise_and)
-        ts(R("hfi", 16, 32), R("lki"), 7, Op.bitwise_and)
-        tc(R("hfb"), R("hfi"))
+        ts(R("hfi", 0, 16), R("lk", 15, 256, 16), 3, Op.arith_shift_right, 3, Op.bitwise_and)
+        ts(R("hfi", 16, 32), R("lk", 15, 256, 16), 7, Op.bitwise_and)
+        cp(R("hfb"), R("hfi"))
         mm(R("ps1", 0, 48), R("ones"), R("crow"), True, False)
         for h in (0, 1):
             mm(R("ps1", h, 48, 2), H("dg", h), R("ob24"), False, False)
@@ -347,11 +347,13 @@ def rank_program(g, core, T, topo):
 
     def offsets(t):
         al = R("sl", 15, 256, 16)
-        tc(R("xi"), R("ps1", 0, 16))
+        cp(R("xi"), R("ps1", 0, 16))
         ts(R("bn"), R("ps1", 16, 48), 0.0, Op.is_ge, -16384.0, Op.mult)
+        ts(R("x3"), R("xi"), 3, Op.bitwise_and)
+        if t < ASKS:
+            tt(R("pv"), R("x3"), R("ps1", 176, 192), Op.add)
         mm(R("ps1", 64, 80), R("id4"), al, True, False)
         mm(R("ps1", 80, 96), R("idf"), al, False, False)
-        ts(R("x3"), R("xi"), 3, Op.bitwise_and)
         tt(R("y"), R("x3"), R("bn", 0, 16), Op.add)
         tt(R("ay"), IND(R("y"), R("et16")), R("mask16"), Op.mult)
         for k, o in ((64, "ob8"), (80, "om8")):
@@ -359,20 +361,19 @@ def rank_program(g, core, T, topo):
                 mm(R("ps1", k + 8 * h, k + 8 * h + 8), H("ay", h), R(o), False, k == 80 and h == 1)
         ts(R("offu"), R("ps1", 64, 80), 16.0, Op.add)
         ts(R("sou"), R("ps1", 80, 96), 0.375, Op.add)
-        act(R("sp"), IND(R("sui"), R("sou")))
+        cp(R("sp"), IND(R("sui"), R("sou")))
         mm(R("ps3", 384, 400), R("idm"), R("bn", 16, 32), True, False)
         mm(R("ps3", 384, 400), R("id32"), R("bn", 0, 16), False, False)
         mm(R("ps3", 384, 400), R("tri"), R("bn", 0, 16), False, False)
         mm(R("ps3", 385, 400, 2), R("quar"), R("bn", 0, 16, 2), False, True)
         if t < ASKS:
-            tc(R("ri"), R("ps3", 384, 400))
+            cp(R("ri"), R("ps3", 384, 400))
         ts(R("put"), R("ps3", 384, 400), -384.0, Op.is_lt)
         ts(R("w7"), R("bn", 0, 16), 7.0 / 16384, Op.mult, 7.0, Op.add)
         tt(R("w"), R("put"), R("w7"), Op.add)
 
     def ask(t):
         qp = R("qp%d" % t)
-        tt(R("pv"), R("x3"), R("ps1", 176, 192), Op.add)
         ts(R("rlo"), R("ri"), 15, Op.bitwise_and)
         ts(R("rhi"), R("ri"), 4, Op.arith_shift_right)
         tt(R("cb"), IND(R("rhi"), R("e8")), R("patc"), Op.is_equal)
@@ -382,8 +383,8 @@ def rank_program(g, core, T, topo):
         for h in (0, 1):
             mm(R("ps1", 96, 160), H("ca", h), H("cb2", h, 64), False, h == 1)
         scan(R("qs"), R("keep"), R("ps1", 96, 160), Op.mult, Op.max)
-        tc(qp, R("qs", 7, 64, 8))
-        send(1 + t % (N - 1), 0, R("qpin%d" % t), qp, "rp%d" % t)
+        cp(qp, R("qs", 7, 64, 8))
+        send(1 + t % (N - 1), R("qpin%d" % t), qp, "rp%d" % t)
         ts(R("v1"), qp, 16383, Op.bitwise_and)
         tt(R("offr%d" % t), R("v1"), R("dump"), Op.max)
 
@@ -393,16 +394,16 @@ def rank_program(g, core, T, topo):
             col = 2 * (k % 8) + k // 8
             ts(H("hot", k), R("i128"), C("alof", col), Op.is_equal, C("w", col), Op.mult)
             mm(R("ps1", 192 + 16 * (k % 8), 208 + 16 * (k % 8)), H("hot", k), H("ah", k, 16), False, k == 15)
-        act(R("ut"), R("ps1", 192, 320))
+        cp(R("ut"), R("ps1", 192, 320))
         mm(R("ps1", 320, 448), R("ut"), R("idb"))
         if t < ASKS:
-            act(R("cw"), R("ps1", 320, 448))
+            cp(R("cw"), R("ps1", 320, 448))
         else:
-            tc(R("w1"), R("ps1", 320, 448))
+            cp(R("w1"), R("ps1", 320, 448))
             ts(R("w2"), R("w1"), 3, Op.arith_shift_right, 3, Op.bitwise_and)
             ts(R("w3"), R("w1"), 7, Op.bitwise_and)
-            tc(R("ohf"), R("w2"))
-            tc(R("oyf"), R("w3"))
+            cp(R("ohf"), R("w2"))
+            cp(R("oyf"), R("w3"))
 
     def pops(t):
         zn = "zz%d" % (t + 1)
@@ -413,7 +414,7 @@ def rank_program(g, core, T, topo):
         ts(R(zn), R("zs"), 0.0, Op.max, 255.0, Op.min)
         mm(R("ps3", 0, 256), R("idb"), R(zn))
         if t + 1 < ASKS:
-            send(1 + (t + 1) % (N - 1), 0, R("zin%d" % (t + 1)), R(zn), "rz%d" % (t + 1))
+            send(1 + (t + 1) % (N - 1), R("zin%d" % (t + 1)), R(zn), "rz%d" % (t + 1))
 
     def dist(t):
         zn = "zz%d" % (t + 1)
@@ -446,46 +447,54 @@ def rank_program(g, core, T, topo):
                 mm(R(KB[h], m, 128, 16), mx(h, m), R("o16"), False, m == 15)
 
     def choose(t, h):
-        scan(H("ksc", h), R("big"), R(KB[h], 0, 128), Op.add, Op.min)
-        act(H("kmin", h), IND(H("ksc", h), R("e15", 0, 8)))
+        scan(H("ksc", h), R("big", 0, 128), R(KB[h], 0, 128), Op.add, Op.min)
+        cp(H("kmin", h), IND(H("ksc", h), R("e15")))
         tt(H("oh", h), H("kmin", h), R(KB[h], 0, 128), Op.is_equal)
         mm(R(KB[h], 128, 256), H("oh", h), R("idb"))
         tt(H("os", h), R(KB[h], 128, 256), H("sp", h), Op.mult)
 
     def answer(t):
-        qpin = R("qpin%d" % t)
+        qpin, nv = R("qpin%d" % t), 16 - NQ
         mm(R("ps4", 0, 256), R("bow"), R("zin%d" % t))
-        tc(R("ui"), R("ps4", 0, 256))
+        cp(R("ui"), R("ps4", 0, 256))
         ts(R("uu"), R("ui"), 4095, Op.bitwise_and)
-        ts(R("ps4", 256, 512), R("uu"), R("odd32"), Op.add)
+        act(R("ps4", 256, 512), R("uu"), Fn.Identity, bias=R("odd32"))
         tt(R("pr"), R("uu"), R("ps4", 256, 512), Op.mult)
         ts(R("ux"), R("pr"), 5, Op.arith_shift_right, 8191, Op.bitwise_and)
         ts(R("dq", 0, 8), qpin, 14, Op.arith_shift_right)
         ts(R("dq", 8, 16), qpin, 2, Op.arith_shift_right, 4095, Op.bitwise_and)
-        tc(R("dqu"), R("dq"))
-        act(R("zq"), IND(R("zin%d" % t), R("dqu", 0, 8)))
-        act(R("goal"), IND(R("xw"), R("dqu", 8, 16)))
-        mm(R("ps6", 0, 128), R("idn"), R("zq"), True, False)
-        mm(R("ps6", 0, 128), R("idb"), R("goal"), False, True)
-        tc(R("cou"), IND(R("ux"), R("dqu", 0, 8)))
+        cp(R("dqu"), R("dq"))
+        cp(R("zq"), IND(R("zin%d" % t), R("dqu", 0, 8)))
+        cp(R("goal"), IND(R("xw"), R("dqu", 8, 16)))
+        mm(R("ps3", 256, 384), R("idn"), R("zq"), True, False)
+        mm(R("ps3", 256, 384), R("idb"), R("goal"), False, True)
+        cp(R("wq"), R("ps3", 256, 384))
+        cp(R("cou"), IND(R("ux"), R("dqu", 0, 8)))
         for k in range(2):
-            act(H("cand", k, 1024), IND(R("bank", B0), H("cou", k, 64)))
+            cp(H("cand", k, 1024), IND(R("bank", B0), H("cou", k, 64)))
         mm(R("ps4", 256, 384), R("ones"), R("rowc"), True, False)
-        for m in range(16):
+        mm(R("ps4", 256, 384), R("wq"), H("bs", SHARES.index(nv)), False, False)
+        for a in range(nv, 16, 4):
+            for j in range(4):
+                mm(H("ps6", j), R("idb"), R("cand", a + j, 2048, 16), j == 0, False)
+                mm(H("ps6", j), R("idn"), R("wq"), False, j == 3)
+            act(R("mq", 128 * a, 128 * a + 512), R("ps6"), Fn.Abs)
+        for m in range(nv):
             mm(R("ps4", 256 + m, 384, 16), R("cand", m, 2048, 16), R("om16"), False, False)
-            tt(H("mq", m), R("cand", m, 2048, 16), R("ps6", 0, 128), Op.max)
-            mm(R("ps4", 256 + m, 384, 16), H("mq", m), R("o32"), False, m == 15)
-        scan(R("kq"), R("big"), R("ps4", 256, 384), Op.add, Op.min)
-        tc(R("ki"), R("kq", 15, 128, 16))
-        ts(R("mi"), R("ki"), 15, Op.bitwise_and)
+            tt(H("mq", m), R("cand", m, 2048, 16), R("ps3", 256, 384), Op.max)
+            mm(R("ps4", 256 + m, 384, 16), H("mq", m), R("o32h"), False, False)
+        for m in range(nv, 16):
+            mm(R("ps4", 256 + m, 384, 16), H("mq", m), R("o16h"), False, m == 15)
+        scan(R("kq"), R("big", 0, 128), R("ps4", 256, 384), Op.add, Op.min)
+        ts(R("mi"), R("kq", 15, 128, 16), 15, Op.bitwise_and)
         tt(R("aq"), IND(R("mi"), R("e16", 0, 8)), R("mask16", 0, 128), Op.mult)
         mm(R("ps4", 384, 392), R("idb"), R("q16"), True, False)
         mm(R("ps4", 384, 392), R("aq"), R("ob8"), False, True)
-        tc(R("seu"), R("ps4", 384, 392))
-        act(R("an%d" % t), IND(R("cand"), R("seu")))
-        send(-1 - t % (N - 1), 0, R("anin%d" % t), R("an%d" % t), "ra%d" % t)
+        cp(R("seu"), R("ps4", 384, 392))
+        cp(R("an%d" % t), IND(R("cand"), R("seu")))
+        send(-1 - t % (N - 1), R("anin%d" % t), R("an%d" % t), "ra%d" % t)
 
-    send(1, 0, R("zin0"), R("zz0"), "rz0")
+    send(1, R("zin0"), R("zz0"), "rz0")
     for h in (0, 1):
         states(0, h)
     for t in range(STEPS):
@@ -504,7 +513,7 @@ def rank_program(g, core, T, topo):
                 states(t + 1, h)
             else:
                 mm(R(RB[h], 128, 256), R("boh"), H("os", h))
-                act(H("arf", h), R(RB[h], 128, 256))
+                cp(H("arf", h), R(RB[h], 128, 256))
     store("d", T.yz[:, :], R("zz%d" % STEPS)[0], R("zz%d" % STEPS))
     buf, base, w = PACK["arf"]
     store("d", T.ya[:, :], T[buf][0:128:16, base:base + w], R("arf"))
@@ -527,16 +536,15 @@ def rank_program(g, core, T, topo):
 
     if not ORDER:
         ORDER.extend(plan(ops))
-    for i in ORDER:
-        o = ops[i]
-        q, todo = o["q"], {}
+    for i, q in ORDER:
+        o, todo = ops[i], {}
         for p in o["pred"]:
             sem, n, snap = done[p]
-            if not q == ops[p]["q"] == "t" and todo.get(sem, (0,))[0] < n:
+            if not (q == "t" and sem == "st") and todo.get(sem, (0,))[0] < n:
                 todo[sem] = (n, snap)
         for sem in sorted(todo, key=lambda s: -len(todo[s][1])):
             need(q, sem, todo[sem][0], todo[sem][1])
-        ins = o["emit"](qobj[q])
+        ins = o["emit"][q](qobj[q])
         if o["sem"] is None:
             count[q] += 1
             ins.then_inc(T.sem[qsem[q]], 1)

@@ -18,14 +18,14 @@ for _t in range(STEPS + 1):
 for _n, (_w, _d) in WIDE.items():
     SCRATCH[_n] = ("sbuf", [128, _w], _d)
 NARROW = {
-    "float32": "pcol 1 p16 1 pdiv 1 odd 1 odd32 1 p8 1 huge 1 p8h 2 pat8 64 jf 128 pat16 256 patc 128 mask16 256 qd16 128 tmp 128 tm2 128 dump 8 "
-               "idf 128 id4 128 sl 256 y 16 put 16 w7 16 w 16 pv 16 ca 256 cb 128 cb2 128 qs 64 alof 16 sp 256 ksc 256 kmin 256 arf 256 ohf 128 oyf 128",
-    "int32": "ci 1 ci2 1 ci3 1 ci4 1 hi0 128 fi0 128 a0i 16 ail 16 alo 16 ait 16 ahit 16 alot 16 lk 256 hfi 32 xi 16 x3 16 ri 16 rlo 16 "
-             "rhi 16 v1 8 dq 16 ui 256 uu 256 pr 256 ux 256 kq 128 mi 8 w1 128 w2 128 w3 128",
+    "float32": "p16 1 pdiv 1 odd 1 odd32 1 p8 1 huge 1 p8h 2 pat8 64 jf 128 pat16 256 pat192 256 patc 128 mask16 256 qd16 128 tmp 128 dump 8 "
+               "idf 128 id4 128 als 16 uy 256 y 16 put 16 w7 16 w 16 pv 16 ca 256 cb 128 cb2 128 qs 64 alof 16 atf 16 sp 256 arf 256 ohf 128 oyf 128",
+    "int32": "ci 1 ci2 1 ci3 1 ci4 1 hi0 128 fi0 128 a0i 16 sl 256 alo 16 lk 256 hfi 32 xi 16 x3 16 ri 16 rlo 16 rhi 16 v1 8 dq 8 pr 256 ux 256 "
+             "kq 128 ksc 256 ks 256 mi 8 w1 128 w2 128 w3 128",
     "uint16": "e16 16 et16 16 e15 8 e8 8 alu 16 alou 16 suu 256 offu 16 sou 16 dqu 16 cou 128 seu 8",
-    "bfloat16": "bo 128 bow 128 ob8 8 ob24 24 om8 8 o16 8 o32 8 om16 8 idb 128 idn 128 id256 128 idk 128 idm 128 id32 128 tri 128 ones 128 quar 128 "
-                "i128 128 negm 256 rst 256 big 256 keep 64 gneg 64 lanb 16 rowc 128 crow 48 brow 16 q16 8 bs 512 dg 256 bn 32 ay 256 zs 256 oh 256 "
-                "goal 128 zq 128 wq 128 aq 128 gc_ 256 ah 256 hfb 32 cw 128 ut 128",
+    "bfloat16": "bo 128 bo16 128 bow 128 ob8 8 ob24 24 om8 8 o16 8 o32 8 om16 8 idb 128 idn 128 id256 128 idk 128 idm 128 id32 128 idu 128 tri 128 "
+                "ones 128 quar 128 i128 128 negm 256 rst 256 big 256 keep 64 gneg 64 lanb 16 rowc 128 crow 48 brow 16 urow 256 q16 8 bs 512 dg 256 "
+                "bn 32 ay 256 zs 256 oh 256 zq 128 wq 128 uk 256 ahb 16 aq 128 gc_ 256 ah 256 hfb 32 cw 128 ut 128",
     "float16": "boh 128 ob8h 8 ob4h 8 o16h 8 o32h 8 arow 256 os 256"}
 PACK = {}
 for _d, _t in NARROW.items():
@@ -41,21 +41,44 @@ for _t in range(ASKS):
 LOADS = ["la", "ls", "lx", "lh0", "lf0", "lz", "lg"]
 SEMAPHORES = ["sv", "ss", "st", "sg", "sent", "sout"] + LOADS + ["%s%d" % (n, t) for t in range(ASKS) for n in ("rp", "rz", "ra")]
 
-GATHER, SCATTER, LEAST, WAKE, HOP, FIRST, DMA, BYTES, TENSOR = 1.56, 3.8, 64, 130, 1800, 2500, 1500, 450, 0.75
-PATIENCE, BUSY, SWEEPS, SHAKE = 0.25, 2, 30, 2000
+GATHER, SCATTER, LEAST, WAKE, HOP, FIRST, DMA, BYTES, LINES, TENSOR = 1.56, 3.8, 64, 250, 2300, 3000, 1500, 400, 300, 0.65
+PACES = [(1.15, 1.7, 0), (1.0, 1.56, -600), (1.3, 1.95, 1500), (1.1, 1.15, -600), (1.45, 1.5, 0)]
+PATIENCE, BUSY, SOON, SWEEPS, SHAKE = 0.35, 2.5, 300, 300, 2500
+MOVES, SLACK = 1800, 60
 ROWS = ("cc", "cand", "mx", "mq", "eb", "hot")
 ORDER = []
 
 
 def plan(ops):
     n = len(ops)
-    cost, late = [o["cost"] for o in ops], [o["late"] for o in ops]
+    paces = [[{q: f * (c + o["gather"] * (r - GATHER)) if q in "vst" else c for q, c in o["cost"].items()} for o in ops] for f, r, _ in PACES]
+    cost, late = paces[0], [o["late"] for o in ops]
+    hop = [bool(o["sem"]) and "g" in o["cost"] for o in ops]
     fore, back = [[] for _ in ops], [[] for _ in ops]
     for i, o in enumerate(ops):
         for p in o["pred"]:
             lag = 0 if "t" in cost[p] and "t" in cost[i] else late[p] + WAKE
             fore[p].append((i, lag))
             back[i].append((p, lag))
+
+    waits = [[[(p, lag + far * hop[p]) for p, lag in x] for x in back] for _, _, far in PACES]
+    last_ones = [i for i in range(n) if not fore[i]]
+
+    def replay(order):
+        total, runs = 0.0, []
+        for costs, edges, pace in zip(paces, waits, PACES):
+            free, last, end, why = dict.fromkeys("vstgd", 0.0), dict.fromkeys("vstgd"), [0.0] * n, [None] * n
+            for i, q in order:
+                at, w, behind = free[q], last[q], True
+                for p, lag in edges[i]:
+                    if end[p] + lag >= at:
+                        at, w, behind = end[p] + lag, p, False
+                free[q] = end[i] = at + costs[i][q]
+                last[q], why[i] = i, (w, behind)
+            i = max(last_ones, key=lambda i: end[i] + late[i])
+            total += (end[i] + late[i]) / pace[0]
+            runs.append((i, why))
+        return total, runs
 
     def sweep(before, after, ready, way):
         left = [len(x) for x in before]
@@ -70,7 +93,8 @@ def plan(ops):
             coming.pop("v", None)
             for q, L in pool.items():
                 if q == "v":
-                    L = [i for i in L if "s" not in cost[i] or free["s"] > max(free["v"], ready[i]) + BUSY * cost[i]["v"]]
+                    L = [i for i in L if "s" not in cost[i] or max(free["v"], ready[i]) + BUSY * cost[i]["v"] < free["s"] + sum(
+                        cost[j]["s"] for j in pool["s"] if way[j] > way[i] and ready[j] <= ready[i] + SOON)]
                 if L and q not in coming:
                     now = max(free[q], min(ready[i] for i in L))
                     pick = max((i for i in L if ready[i] <= now), key=lambda i: way[i])
@@ -102,15 +126,52 @@ def plan(ops):
             if ops[i]["sem"] and not back[i]:
                 way[i] = 1e9 - i
         order, end = sweep(back, fore, [0.0] * n, way)
-        total = max(end[i] + late[i] for i in range(n))
+        total = replay(order)[0]
         if best is None or total < best[0]:
             best = (total, order, end)
-        if k % 3 == 2:
-            end = list(best[2])
+        if k % 2 == 1:
+            end, shift = list(best[2]), {}
             for i in range(n):
-                seed = (seed * 1103515245 + 12345) % 2 ** 31
-                end[i] += SHAKE * seed / 2 ** 31
+                if ops[i]["part"] not in shift:
+                    seed = (seed * 1103515245 + 12345) % 2 ** 31
+                    shift[ops[i]["part"]] = SHAKE * (seed / 2 ** 30 - 1) * (seed >> 8 & 3 == 0)
+                end[i] += shift[ops[i]["part"]]
         way = sweep(fore, back, [0.0 if fore[i] else float(late[i]) for i in range(n)], end)[1]
+    order = best[1]
+    total, runs = replay(order)
+    best = (total, order)
+    for k in range(MOVES):
+        seed = (seed * 1103515245 + 12345) % 2 ** 31
+        i, why = runs[(seed >> 10) % len(runs)]
+        pairs = []
+        while why[i][0] is not None:
+            if why[i][1]:
+                pairs.append((why[i][0], i))
+            i = why[i][0]
+        j, i = pairs[(seed >> 4) % len(pairs)]
+        at = {x: p for p, (x, _) in enumerate(order)}
+        new, either = None, [x for x in (i, j) if len(cost[x]) > 1]
+        if either and seed >> 20 & 3 == 0:
+            x = either[seed >> 22 & 1 and -1]
+            new = list(order)
+            new[at[x]] = (x, "v" if order[at[x]][1] == "s" else "s")
+        elif not ops[j]["sem"] or back[j]:
+            between = order[at[j]:at[i] + 1]
+            need, queues, first = {p for p, _ in back[i]}, set(), [between[-1]]
+            for x, q in between[-2::-1]:
+                if x in need or q in queues:
+                    first.append((x, q))
+                    need.update(p for p, _ in back[x])
+                    queues.add(q)
+            if first[-1][0] != j:
+                moved = {x for x, _ in first}
+                new = order[:at[j]] + first[::-1] + [y for y in between if y[0] not in moved] + order[at[i] + 1:]
+        if new:
+            tried = replay(new)
+            if tried[0] <= total + SLACK * (1 - k / MOVES):
+                order, (total, runs) = new, tried
+                if total < best[0]:
+                    best = (total, order)
     return best[1]
 
 
@@ -120,7 +181,7 @@ def rank_program(g, core, T, topo):
         return
     N = len(T.cores)
     qobj = {"v": g.vector, "s": g.scalar, "t": g.tensor, "g": g, "d": g.sync}
-    ops = []
+    ops, part = [], [0]
     recs = {}
     turn = {}
 
@@ -146,12 +207,16 @@ def rank_program(g, core, T, topo):
         row = (q, out[1][0][0]) if out[1] and out[1][0][0] in ROWS else None
         if q != "vs":
             emit, cost = {q: emit}, {q: cost}
-        ops.append({"row": row, "pred": sorted(pred), "emit": emit, "cost": cost, "late": late, "sem": sem})
+        ops.append({"part": part[0], "row": row, "pred": sorted(pred), "emit": emit, "cost": cost, "late": late, "sem": sem,
+                    "gather": out[2] if ins and ins[0][4] else 0})
 
-    def R(name, a=0, b=None, st=1):
+    def next_part():
+        part[0] += 1
+
+    def R(name, a=0, b=None, st=1, half=None):
         buf, base, w = PACK[name] if name in PACK else (name, 0, SCRATCH[name][1][1])
         b = w if b is None else b
-        ap = T[buf][:, base + a:base + b] if st == 1 else T[buf][:, base + a:base + b:st]
+        ap = T[buf][slice(None) if half is None else slice(64 * half, 64 * half + 64), base + a:base + b:st]
         size = 0 if buf in PSUM else 4 if SCRATCH[buf][2].endswith("32") else 2
         return (ap, [(buf, base + a, base + b)], -(-(b - a) // st), size, False)
 
@@ -196,11 +261,19 @@ def rank_program(g, core, T, topo):
         op("vs", out, [a], {"v": lambda e: e.tensor_copy(out[0], a[0]), "s": lambda e: e.activation(out[0], a[0], Fn.Copy)},
            {"v": cycles(out, [a], None), "s": cycles(out, [a], 1)})
 
+    def lin(out, a, scale, bias):
+        op("vs", out, [a], {"v": lambda e: e.tensor_scalar(out[0], a[0], scale, bias, Op.mult, Op.add),
+                            "s": lambda e: e.activation(out[0], a[0], Fn.Copy, bias=bias, scale=scale)},
+           {"v": cycles(out, [a], None), "s": cycles(out, [a], 1)})
+
     def mm(out, l, r, start=True, stop=True):
         op("t", out, [l, r], lambda e: e.matmul(out[0], l[0], r[0], start, stop), TENSOR * max(LEAST, r[2]) * (4 if l[3] == 4 else 1))
 
     def iota(out, pattern, base=0, cm=0):
         op("g", out, [], lambda e: e.iota(out[0], pattern, base, cm, allow_small_or_imprecise_dtypes=True), 160 + 2 * out[2])
+
+    def select(out, a, pattern, o, base, cm):
+        op("g", out, [a], lambda e: e.affine_select(out[0], a[0], pattern, o, 0.0, base, cm), 205 + 2 * out[2])
 
     def fill(out, c):
         op("v", out, [], lambda e: e.memset(out[0], c), cycles(out, [out], None))
@@ -208,7 +281,7 @@ def rank_program(g, core, T, topo):
     loaded = [DMA]
 
     def load(q, out, src, sem):
-        loaded[0] += 128 * out[2] * out[3] / BYTES
+        loaded[0] += 128 * out[2] * out[3] / BYTES + LINES
         op(q, out, [], lambda e: e.dma_start(out[0], src), LEAST, loaded[0], (sem, 16))
 
     sends, arrive = [0], {}
@@ -229,8 +302,8 @@ def rank_program(g, core, T, topo):
 
     load("d", R("a0i"), T.a0[:, :], "la")
     load("s", R("hi0"), T.hd0[:, :], "lh0")
+    load("d", R("zz0"), T.z0[:, :], "lz")
     load("s", R("fi0"), T.fl0[:, :], "lf0")
-    load("s", R("zz0"), T.z0[:, :], "lz")
     load("d", R("sui", 0, 2048), T.su[:, :], "ls")
     load("d", R("xw", X0), T.xs[:, :], "lx")
     load("d", R("bank", B0), T.gs[:, :], "lg")
@@ -245,13 +318,13 @@ def rank_program(g, core, T, topo):
     iota(R("sui", 2048, 4096), [[1, 2048]])
     fill(R("ones"), 1.0)
     fill(R("huge"), 2.0 ** 20)
-    cp(R("pcol"), R("ci"))
+    fill(R("urow"), 6144.0)
     for name, tmp, c, o in (("p16", "ci2", 15, Op.bitwise_and), ("pdiv", "ci3", 4, Op.arith_shift_right), ("p8", "ci4", 7, Op.bitwise_and)):
         ts(R(tmp), R("ci"), c, o)
         cp(R(name), R(tmp))
     ts(R("mask16"), R("pat16"), R("p16"), Op.is_equal)
     tc(R("e16"), R("pat16", 0, 16))
-    ts(R("e15"), R("pat16", 0, 8), 16.0, Op.mult, 15.0, Op.add)
+    lin(R("e15"), R("pat16", 0, 8), 16.0, 15.0)
     for h in (0, 1):
         ts(H("et16", h, 8), R("pat16", 0, 8), 2.0, Op.mult, float(h), Op.add)
         act(C("p8h", h), R("p8"), scale=2.0, bias=float(h))
@@ -263,8 +336,8 @@ def rank_program(g, core, T, topo):
         act(R(name), R("ob8"), scale=float(c))
     for k in range(3):
         cp(H("ob24", k, 8), R("ob8"))
-    ts(R("idb"), R("jf"), R("pcol"), Op.is_equal)
-    for name, c in (("idn", -1), ("id256", 256), ("idk", 16384), ("idm", -0.0625), ("id32", 1 / 32), ("idf", 1), ("id4", 4)):
+    select(R("idb"), R("ones"), [[-1, 128]], Op.is_equal, 0, 1)
+    for name, c in (("idn", -1), ("id256", 256), ("idk", 16384), ("idm", -0.0625), ("id32", 1 / 32), ("idf", 1), ("id4", 4), ("idu", -4096)):
         act(R(name), R("idb"), scale=float(c))
     act(R("negm"), R("mask16"), scale=4096.0, bias=-4096.0)
     act(R("big"), R("pat16"), Fn.Relu, scale=-2.0 ** 20, bias=R("huge"))
@@ -276,16 +349,17 @@ def rank_program(g, core, T, topo):
     for k, c in enumerate((-1.0, -1.0, -5.0)):
         act(H("crow", k, 16), R("ones", 0, 16), scale=c / 128)
     act(R("brow"), R("ones", 0, 16), scale=B0 / 128)
-    ts(R("tri"), R("jf"), R("pcol"), Op.is_gt, -2.0 ** -14, Op.mult)
-    cp(R("i128"), R("jf"))
+    select(R("tri"), R("quar"), [[1, 128]], Op.is_gt, 0, -1)
+    act(R("i128"), R("jf"), scale=1 / 128)
+    act(R("pat192"), R("pat16"), bias=192.0)
     act(R("dump"), R("pat16", 0, 8), Fn.Identity, scale=16.0, bias=R("p16"))
     act(R("q16"), R("dump"), scale=16.0)
     act(R("odd"), R("p16"), scale=2.0, bias=1.0)
     act(R("odd32"), R("p16"), scale=64.0, bias=32.0)
     act(R("bow"), R("bo"), scale=R("odd"))
+    act(R("bo16"), R("boh"), scale=16.0)
     for k, nv in enumerate(SHARES):
-        ts(R("tm2"), R("pat16", 0, 128), float(nv), Op.is_ge, 16.0, Op.mult)
-        tt(H("bs", k), R("tm2"), R("bo"), Op.mult)
+        select(H("bs", k), R("bo16"), [[0, 8], [1, 16]], Op.is_ge, -nv, 0)
     for c in range(15):
         if c != 7:
             fill(R("eb", 256 * c + 128 * (c >= 8), 272 * c + 16), 0.0)
@@ -303,11 +377,13 @@ def rank_program(g, core, T, topo):
         mm(R(RB[h], 128, 256), R("boh"), H("os", h), False, True)
         scan(H("sl", h), H("rst", h), R(RB[h], 0, 128), Op.add, Op.max)
         cp(H("arow", h), R(RB[h], 128, 256))
+        cp(H("als", h, 8), R("sl", 128 * h + 15, 128 * h + 128, 16))
         tt(H("dg", h), H("sl", h), R(RB[h], 128, 256), Op.is_equal)
+        next_part()
         cp(H("alu", h, 8), R("sl", 128 * h + 15, 128 * h + 128, 16))
         cp(H("suu", h), IND(R("sui", 0, 2048), H("alu", h, 8)))
-        for k in range(4 * h, 4 * h + 4):
-            cp(H("cc", k, 512), IND(R("xw", X0), H("suu", k, 32)))
+        for k in (2 * h, 2 * h + 1):
+            (tc if (t, k) == (0, 1) else cp)(H("cc", k, 1024), IND(R("xw", X0), H("suu", k, 64)))
 
     def places(t):
         for h in (0, 1):
@@ -317,13 +393,11 @@ def rank_program(g, core, T, topo):
             mm(R("ps1", 176, 192), R("idk"), R("lanb"), False, False)
             for h in (0, 1):
                 mm(R("ps1", 176 + h, 192, 2), H("os", h), R("ob4h"), False, h == 1)
-        cp(R("ait"), R("ps1", 160, 176))
-        ts(R("ahit"), R("ait"), 7, Op.arith_shift_right)
-        ts(R("alot"), R("ait"), 127, Op.bitwise_and)
-        cp(R("alof"), R("alot"))
-        tt(R("ah"), IND(R("ahit"), R("et16")), R("pat16"), Op.is_equal)
-        cp(R("ail"), R("sl", 15, 256, 16))
-        ts(R("alo"), R("ail"), 127, Op.bitwise_and)
+        lin(R("ahb"), R("ps1", 160, 176), 1 / 128, 191.5 + 1 / 256)
+        lin(R("atf"), R("ps1", 160, 176), 1 / 128, 192.0)
+        tt(R("alof"), R("atf"), R("ahb"), Op.subtract)
+        tt(R("ah"), IND(R("ahb"), R("et16")), R("pat192"), Op.is_equal)
+        ts(R("alo"), R("sl", 15, 256, 16), 127, Op.bitwise_and)
         cp(R("alou"), R("alo"))
         cp(R("gc_"), IND(R("cw"), R("alou")))
         mm(R("ps0", 256, 512), R("id256"), R("ah"), True, False)
@@ -333,11 +407,12 @@ def rank_program(g, core, T, topo):
         ts(R("hfi", 0, 16), R("lk", 15, 256, 16), 3, Op.arith_shift_right, 3, Op.bitwise_and)
         ts(R("hfi", 16, 32), R("lk", 15, 256, 16), 7, Op.bitwise_and)
         cp(R("hfb"), R("hfi"))
+        next_part()
         mm(R("ps1", 0, 48), R("ones"), R("crow"), True, False)
         for h in (0, 1):
             mm(R("ps1", h, 48, 2), H("dg", h), R("ob24"), False, False)
         for c in range(15):
-            ts(R("eb", 272 * c + 16, 256 * c + 256), R("arow", 16 * c + 16, 256), C("sl", 16 * c + 15), Op.is_equal)
+            ts(R("eb", 272 * c + 16, 256 * c + 256), R("arow", 16 * c + 16, 256), C("als", c), Op.is_equal)
             for h in (0, 1) if c < 7 else (1,):
                 mm(R("ps1", h, 48, 2), H("eb", 2 * c + h), R("ob24"), False, False)
         for h in (0, 1):
@@ -346,43 +421,43 @@ def rank_program(g, core, T, topo):
                 mm(R("ps1", 16 * k + h, 16 * k + 16, 2), R("idn"), H("hfb", 2 + h, 8), False, h == 1 and k == 2)
 
     def offsets(t):
-        al = R("sl", 15, 256, 16)
         cp(R("xi"), R("ps1", 0, 16))
         ts(R("bn"), R("ps1", 16, 48), 0.0, Op.is_ge, -16384.0, Op.mult)
         ts(R("x3"), R("xi"), 3, Op.bitwise_and)
         if t < ASKS:
             tt(R("pv"), R("x3"), R("ps1", 176, 192), Op.add)
-        mm(R("ps1", 64, 80), R("id4"), al, True, False)
-        mm(R("ps1", 80, 96), R("idf"), al, False, False)
+        mm(R("ps1", 64, 80), R("id4"), R("als"), True, False)
+        mm(R("ps1", 80, 96), R("idf"), R("als"), False, False)
         tt(R("y"), R("x3"), R("bn", 0, 16), Op.add)
         tt(R("ay"), IND(R("y"), R("et16")), R("mask16"), Op.mult)
         for k, o in ((64, "ob8"), (80, "om8")):
             for h in (0, 1):
                 mm(R("ps1", k + 8 * h, k + 8 * h + 8), H("ay", h), R(o), False, k == 80 and h == 1)
-        ts(R("offu"), R("ps1", 64, 80), 16.0, Op.add)
-        ts(R("sou"), R("ps1", 80, 96), 0.375, Op.add)
+        lin(R("offu"), R("ps1", 64, 80), 1.0, 16.0)
+        lin(R("sou"), R("ps1", 80, 96), 1.0, 0.375)
         cp(R("sp"), IND(R("sui"), R("sou")))
+        next_part()
         mm(R("ps3", 384, 400), R("idm"), R("bn", 16, 32), True, False)
         mm(R("ps3", 384, 400), R("id32"), R("bn", 0, 16), False, False)
         mm(R("ps3", 384, 400), R("tri"), R("bn", 0, 16), False, False)
         mm(R("ps3", 385, 400, 2), R("quar"), R("bn", 0, 16, 2), False, True)
         if t < ASKS:
             cp(R("ri"), R("ps3", 384, 400))
+            lin(R("rhi"), R("ps3", 384, 400), 1 / 16, -15 / 32)
         ts(R("put"), R("ps3", 384, 400), -384.0, Op.is_lt)
-        ts(R("w7"), R("bn", 0, 16), 7.0 / 16384, Op.mult, 7.0, Op.add)
+        lin(R("w7"), R("bn", 0, 16), 7.0 / 16384, 7.0)
         tt(R("w"), R("put"), R("w7"), Op.add)
 
     def ask(t):
         qp = R("qp%d" % t)
         ts(R("rlo"), R("ri"), 15, Op.bitwise_and)
-        ts(R("rhi"), R("ri"), 4, Op.arith_shift_right)
         tt(R("cb"), IND(R("rhi"), R("e8")), R("patc"), Op.is_equal)
         tt(R("ca"), IND(R("rlo"), R("et16")), R("pat16"), Op.is_equal)
         tt(R("cb2"), IND(R("pv"), R("e8")), R("cb"), Op.mult)
-        mm(R("ps1", 96, 160), R("idb"), R("gneg"), True, False)
+        mm(R("ps6", 256, 320), R("idb"), R("gneg"), True, False)
         for h in (0, 1):
-            mm(R("ps1", 96, 160), H("ca", h), H("cb2", h, 64), False, h == 1)
-        scan(R("qs"), R("keep"), R("ps1", 96, 160), Op.mult, Op.max)
+            mm(R("ps6", 256, 320), H("ca", h), H("cb2", h, 64), False, h == 1)
+        scan(R("qs"), R("keep"), R("ps6", 256, 320), Op.mult, Op.max)
         cp(qp, R("qs", 7, 64, 8))
         send(1 + t % (N - 1), R("qpin%d" % t), qp, "rp%d" % t)
         ts(R("v1"), qp, 16383, Op.bitwise_and)
@@ -394,6 +469,7 @@ def rank_program(g, core, T, topo):
             col = 2 * (k % 8) + k // 8
             ts(H("hot", k), R("i128"), C("alof", col), Op.is_equal, C("w", col), Op.mult)
             mm(R("ps1", 192 + 16 * (k % 8), 208 + 16 * (k % 8)), H("hot", k), H("ah", k, 16), False, k == 15)
+        next_part()
         cp(R("ut"), R("ps1", 192, 320))
         mm(R("ps1", 320, 448), R("ut"), R("idb"))
         if t < ASKS:
@@ -448,43 +524,49 @@ def rank_program(g, core, T, topo):
 
     def choose(t, h):
         scan(H("ksc", h), R("big", 0, 128), R(KB[h], 0, 128), Op.add, Op.min)
-        cp(H("kmin", h), IND(H("ksc", h), R("e15")))
-        tt(H("oh", h), H("kmin", h), R(KB[h], 0, 128), Op.is_equal)
+        tc(H("ks", h), R(KB[h], 0, 128))
+        tt(H("oh", h), IND(H("ksc", h), R("e15")), H("ks", h), Op.is_equal)
         mm(R(KB[h], 128, 256), H("oh", h), R("idb"))
         tt(H("os", h), R(KB[h], 128, 256), H("sp", h), Op.mult)
 
     def answer(t):
-        qpin, nv = R("qpin%d" % t), 16 - NQ
-        mm(R("ps4", 0, 256), R("bow"), R("zin%d" % t))
-        cp(R("ui"), R("ps4", 0, 256))
-        ts(R("uu"), R("ui"), 4095, Op.bitwise_and)
-        act(R("ps4", 256, 512), R("uu"), Fn.Identity, bias=R("odd32"))
-        tt(R("pr"), R("uu"), R("ps4", 256, 512), Op.mult)
+        qpin, zin = R("qpin%d" % t), R("zin%d" % t)
+        mm(R("ps4", 0, 256), R("bow"), zin)
+        lin(R("uk"), R("ps4", 0, 256), 1 / 4096, 191.5 + 1 / 8192)
+        mm(R("ps4", 256, 512), R("bow"), zin, True, False)
+        mm(R("ps4", 256, 512), R("ones"), R("urow"), False, False)
+        mm(R("ps4", 256, 512), R("idu"), R("uk"), False, True)
+        act(R("uy"), R("ps4", 256, 512), Fn.Identity, bias=R("odd32"))
+        tt(R("pr"), R("uy"), R("ps4", 256, 512), Op.mult)
         ts(R("ux"), R("pr"), 5, Op.arith_shift_right, 8191, Op.bitwise_and)
-        ts(R("dq", 0, 8), qpin, 14, Op.arith_shift_right)
-        ts(R("dq", 8, 16), qpin, 2, Op.arith_shift_right, 4095, Op.bitwise_and)
-        cp(R("dqu"), R("dq"))
-        cp(R("zq"), IND(R("zin%d" % t), R("dqu", 0, 8)))
-        cp(R("goal"), IND(R("xw"), R("dqu", 8, 16)))
-        mm(R("ps3", 256, 384), R("idn"), R("zq"), True, False)
-        mm(R("ps3", 256, 384), R("idb"), R("goal"), False, True)
-        cp(R("wq"), R("ps3", 256, 384))
+        next_part()
+        lin(R("dqu", 0, 8), qpin, 1 / 16384, -0.25)
+        ts(R("dq"), qpin, 2, Op.arith_shift_right, 4095, Op.bitwise_and)
+        cp(R("dqu", 8, 16), R("dq"))
+        cp(R("zq"), IND(zin, R("dqu", 0, 8)))
+        tt(R("wq"), IND(R("xw"), R("dqu", 8, 16)), R("zq"), Op.subtract)
+        mm(R("ps3", 256, 384), R("idb"), R("wq"))
         cp(R("cou"), IND(R("ux"), R("dqu", 0, 8)))
-        for k in range(2):
+        for k in (0, 1):
             cp(H("cand", k, 1024), IND(R("bank", B0), H("cou", k, 64)))
+        next_part()
         mm(R("ps4", 256, 384), R("ones"), R("rowc"), True, False)
-        mm(R("ps4", 256, 384), R("wq"), H("bs", SHARES.index(nv)), False, False)
-        for a in range(nv, 16, 4):
-            for j in range(4):
-                mm(H("ps6", j), R("idb"), R("cand", a + j, 2048, 16), j == 0, False)
-                mm(H("ps6", j), R("idn"), R("wq"), False, j == 3)
-            act(R("mq", 128 * a, 128 * a + 512), R("ps6"), Fn.Abs)
-        for m in range(nv):
-            mm(R("ps4", 256 + m, 384, 16), R("cand", m, 2048, 16), R("om16"), False, False)
-            tt(H("mq", m), R("cand", m, 2048, 16), R("ps3", 256, 384), Op.max)
-            mm(R("ps4", 256 + m, 384, 16), H("mq", m), R("o32h"), False, False)
-        for m in range(nv, 16):
-            mm(R("ps4", 256 + m, 384, 16), H("mq", m), R("o16h"), False, m == 15)
+        mm(R("ps4", 256, 384), R("wq"), H("bs", SHARES.index(16 - NQ)), False, False)
+        for k in (0, 1):
+            keys = [R("ps4", 256 + m, 384, 16, k) for m in range(16)]
+            cand = [R("cand", 1024 * k + m, 1024 * k + 1024, 16) for m in range(16)]
+            for a in range(16 - NQ, 16, 4):
+                for j in range(4):
+                    mm(H("ps6", j, 64), R("idb"), cand[a + j], j == 0, False)
+                    mm(H("ps6", j, 64), R("idn"), H("wq", k, 64), False, j == 3)
+                act(R("mq", 1024 * k + 64 * a, 1024 * k + 64 * a + 256), R("ps6", 0, 256), Fn.Abs)
+            for m in range(16 - NQ):
+                mm(keys[m], cand[m], R("om16"), False, False)
+                tt(H("mq", 16 * k + m, 64), cand[m], H("ps3", 4 + k, 64), Op.max)
+                mm(keys[m], H("mq", 16 * k + m, 64), R("o32h"), False, False)
+            for m in range(16 - NQ, 16):
+                mm(keys[m], H("mq", 16 * k + m, 64), R("o16h"), False, m == 15)
+        next_part()
         scan(R("kq"), R("big", 0, 128), R("ps4", 256, 384), Op.add, Op.min)
         ts(R("mi"), R("kq", 15, 128, 16), 15, Op.bitwise_and)
         tt(R("aq"), IND(R("mi"), R("e16", 0, 8)), R("mask16", 0, 128), Op.mult)
@@ -498,17 +580,14 @@ def rank_program(g, core, T, topo):
     for h in (0, 1):
         states(0, h)
     for t in range(STEPS):
-        places(t)
-        offsets(t)
-        if t < ASKS:
-            ask(t)
-        update(t)
-        pops(t)
-        dist(t)
-        if t < ASKS:
-            answer(t)
+        for f in (places, offsets, ask, update, pops, dist, answer):
+            next_part()
+            if t < ASKS or f not in (ask, answer):
+                f(t)
         for h in (0, 1):
+            next_part()
             choose(t, h)
+            next_part()
             if t + 1 < STEPS:
                 states(t + 1, h)
             else:

from concourse.mybir import AluOpType as Op, ActivationFunctionType as Fn

STEPS = 4
ASKS = STEPS - 1
NS = [(8, 0)] * 4
NQ = 4
SHARES = sorted({16 - n for x in NS + [(NQ,)] for n in x} - {0, 16})
B0, BD = 192, 8384
X0 = B0 // 4
PSUM = ["ps%d" % i for i in range(8)]
SCRATCH = {}
for _n in PSUM:
    SCRATCH[_n] = ("psum", [128, 512], "float32")
WIDE = {"xw": (X0 + 2048, "bfloat16"), "sui": (4096, "int32"), "bank": (BD, "bfloat16"), "cc": (4096, "bfloat16"), "mx": (4096, "bfloat16"),
        "cand": (2048, "bfloat16"), "mq": (2048, "float16"), "eb": (4096, "bfloat16"), "hot": (2048, "bfloat16")}
for _t in range(STEPS + 1):
    WIDE["zz%d" % _t] = (256, "bfloat16")
for _n, (_w, _d) in WIDE.items():
    SCRATCH[_n] = ("sbuf", [128, _w], _d)
NARROW = {
    "float32": "p16 1 pdiv 1 odd 1 odd32 1 p8 1 huge 1 p8h 2 pat8 64 jf 128 pat16 256 pat192 256 patc 128 mask16 256 qd16 128 tmp 128 dump 8 "
               "idf 128 id4 128 als 16 uy 256 y 16 put 16 w7 16 w 16 pv 16 ca 256 cb 128 cb2 128 qs 64 alof 16 atf 16 sp 256 arf 256 ohf 128 oyf 128",
    "int32": "ci 1 ci2 1 ci3 1 ci4 1 hi0 128 fi0 128 a0i 16 sl 256 alo 16 lk 256 hfi 32 xi 16 x3 16 ri 16 rlo 16 rhi 16 v1 8 dq 8 pr 256 ux 256 "
             "kq 128 ksc 256 ks 256 mi 8 w1 128 w2 128 w3 128",
    "uint16": "e16 16 et16 16 e15 8 e8 8 alu 16 alou 16 suu 256 offu 16 sou 16 dqu 16 cou 128 seu 8",
    "bfloat16": "bo 128 bo16 128 bow 128 ob8 8 ob24 24 om8 8 o16 8 o32 8 om16 8 idb 128 idn 128 id256 128 idk 128 idm 128 id32 128 idu 128 tri 128 "
                "ones 128 quar 128 i128 128 negm 256 rst 256 big 256 keep 64 gneg 64 lanb 16 rowc 128 crow 48 brow 16 urow 256 q16 8 bs 512 dg 256 "
                "bn 32 ay 256 zs 256 oh 256 zq 128 wq 128 uk 256 ahb 16 aq 128 gc_ 256 ah 256 hfb 32 cw 128 ut 128",
    "float16": "boh 128 ob8h 8 ob4h 8 o16h 8 o32h 8 arow 256 os 256"}
PACK = {}
for _d, _t in NARROW.items():
    _at, _f = 0, _t.split()
    for _n, _w in zip(_f[::2], _f[1::2]):
        PACK[_n] = ("pk_" + _d, _at, int(_w))
        _at += -(-int(_w) // 16) * 16
    SCRATCH["pk_" + _d] = ("sbuf", [128, _at], _d)
for _t in range(ASKS):
    for _n, _w, _d in (("qp", 8, "int32"), ("an", 128, "bfloat16"), ("qpin", 8, "int32"), ("zin", 256, "bfloat16"), ("anin", 128, "bfloat16"),
                       ("offr", 8, "uint16")):
        SCRATCH["%s%d" % (_n, _t)] = ("sbuf", [128, _w], _d)
LOADS = ["la", "ls", "lx", "lh0", "lf0", "lz", "lg"]
SEMAPHORES = ["sv", "ss", "st", "sg", "sent", "sout"] + LOADS + ["%s%d" % (n, t) for t in range(ASKS) for n in ("rp", "rz", "ra")]

GATHER, SCATTER, LEAST, WAKE, HOP, FIRST, DMA, BYTES, LINES, TENSOR = 1.56, 3.8, 64, 250, 2300, 3000, 1500, 400, 300, 0.65
PACES = [(1.15, 1.7, 0), (1.0, 1.56, -600), (1.3, 1.95, 1500), (1.1, 1.15, -600), (1.45, 1.5, 0)]
PATIENCE, BUSY, SOON, SWEEPS, SHAKE = 0.35, 2.5, 300, 300, 2500
MOVES, SLACK = 1800, 60
ROWS = ("cc", "cand", "mx", "mq", "eb", "hot")
ORDER = []


def plan(ops):
    n = len(ops)
    paces = [[{q: f * (c + o["gather"] * (r - GATHER)) if q in "vst" else c for q, c in o["cost"].items()} for o in ops] for f, r, _ in PACES]
    cost, late = paces[0], [o["late"] for o in ops]
    hop = [bool(o["sem"]) and "g" in o["cost"] for o in ops]
    fore, back = [[] for _ in ops], [[] for _ in ops]
    for i, o in enumerate(ops):
        for p in o["pred"]:
            lag = 0 if "t" in cost[p] and "t" in cost[i] else late[p] + WAKE
            fore[p].append((i, lag))
            back[i].append((p, lag))

    waits = [[[(p, lag + far * hop[p]) for p, lag in x] for x in back] for _, _, far in PACES]
    last_ones = [i for i in range(n) if not fore[i]]

    def replay(order):
        total, runs = 0.0, []
        for costs, edges, pace in zip(paces, waits, PACES):
            free, last, end, why = dict.fromkeys("vstgd", 0.0), dict.fromkeys("vstgd"), [0.0] * n, [None] * n
            for i, q in order:
                at, w, behind = free[q], last[q], True
                for p, lag in edges[i]:
                    if end[p] + lag >= at:
                        at, w, behind = end[p] + lag, p, False
                free[q] = end[i] = at + costs[i][q]
                last[q], why[i] = i, (w, behind)
            i = max(last_ones, key=lambda i: end[i] + late[i])
            total += (end[i] + late[i]) / pace[0]
            runs.append((i, why))
        return total, runs

    def sweep(before, after, ready, way):
        left = [len(x) for x in before]
        pool = {q: [] for q in "vstgd"}
        free = {q: 0.0 for q in pool}
        for i in range(n):
            if not left[i]:
                for q in cost[i]:
                    pool[q].append(i)
        order, end, coming = [], [0.0] * n, {}
        while len(order) < n:
            coming.pop("v", None)
            for q, L in pool.items():
                if q == "v":
                    L = [i for i in L if "s" not in cost[i] or max(free["v"], ready[i]) + BUSY * cost[i]["v"] < free["s"] + sum(
                        cost[j]["s"] for j in pool["s"] if way[j] > way[i] and ready[j] <= ready[i] + SOON)]
                if L and q not in coming:
                    now = max(free[q], min(ready[i] for i in L))
                    pick = max((i for i in L if ready[i] <= now), key=lambda i: way[i])
                    pick = max((i for i in L if ready[i] <= now + PATIENCE * cost[pick][q]), key=lambda i: way[i])
                    coming[q] = (max(now, ready[pick]), q != "s", pick, q)
            at, _, i, q = min(coming.values())
            for x in cost[i]:
                pool[x].remove(i)
                coming.pop(x, None)
            free[q] = end[i] = at + cost[i][q]
            order.append((i, q))
            for s, lag in after[i]:
                ready[s] = max(ready[s], end[i] + lag)
                left[s] -= 1
                if not left[s]:
                    for x in cost[s]:
                        pool[x].append(s)
                        coming.pop(x, None)
        return order, end

    way, row = [0.0] * n, {}
    for i in range(n - 1, -1, -1):
        way[i] = max(cost[i].values()) + max([lag + way[s] for s, lag in fore[i]] + [late[i], row.get(ops[i]["row"], 0)])
        if ops[i]["row"]:
            row[ops[i]["row"]] = way[i]
    best, seed = None, 1
    for k in range(SWEEPS):
        for i in range(n):
            if ops[i]["sem"] and not back[i]:
                way[i] = 1e9 - i
        order, end = sweep(back, fore, [0.0] * n, way)
        total = replay(order)[0]
        if best is None or total < best[0]:
            best = (total, order, end)
        if k % 2 == 1:
            end, shift = list(best[2]), {}
            for i in range(n):
                if ops[i]["part"] not in shift:
                    seed = (seed * 1103515245 + 12345) % 2 ** 31
                    shift[ops[i]["part"]] = SHAKE * (seed / 2 ** 30 - 1) * (seed >> 8 & 3 == 0)
                end[i] += shift[ops[i]["part"]]
        way = sweep(fore, back, [0.0 if fore[i] else float(late[i]) for i in range(n)], end)[1]
    order = best[1]
    total, runs = replay(order)
    best = (total, order)
    for k in range(MOVES):
        seed = (seed * 1103515245 + 12345) % 2 ** 31
        i, why = runs[(seed >> 10) % len(runs)]
        pairs = []
        while why[i][0] is not None:
            if why[i][1]:
                pairs.append((why[i][0], i))
            i = why[i][0]
        j, i = pairs[(seed >> 4) % len(pairs)]
        at = {x: p for p, (x, _) in enumerate(order)}
        new, either = None, [x for x in (i, j) if len(cost[x]) > 1]
        if either and seed >> 20 & 3 == 0:
            x = either[seed >> 22 & 1 and -1]
            new = list(order)
            new[at[x]] = (x, "v" if order[at[x]][1] == "s" else "s")
        elif not ops[j]["sem"] or back[j]:
            between = order[at[j]:at[i] + 1]
            need, queues, first = {p for p, _ in back[i]}, set(), [between[-1]]
            for x, q in between[-2::-1]:
                if x in need or q in queues:
                    first.append((x, q))
                    need.update(p for p, _ in back[x])
                    queues.add(q)
            if first[-1][0] != j:
                moved = {x for x, _ in first}
                new = order[:at[j]] + first[::-1] + [y for y in between if y[0] not in moved] + order[at[i] + 1:]
        if new:
            tried = replay(new)
            if tried[0] <= total + SLACK * (1 - k / MOVES):
                order, (total, runs) = new, tried
                if total < best[0]:
                    best = (total, order)
    return best[1]


def rank_program(g, core, T, topo):
    rank = T.rank_of(core)
    if rank is None:
        return
    N = len(T.cores)
    qobj = {"v": g.vector, "s": g.scalar, "t": g.tensor, "g": g, "d": g.sync}
    ops, part = [], [0]
    recs = {}
    turn = {}

    def op(q, out, ins, emit, cost, late=0, sem=None):
        i, pred = len(ops), set()
        refs = [(False, x) for r in ins for x in r[1]] + [(True, x) for x in out[1]]
        for wr, (name, lo, hi) in refs:
            for r in recs.get(name, ()):
                if r[0] < hi and lo < r[1] and (r[2] or wr):
                    pred.add(r[3])
        for name in sorted({x[0] for _, x in refs if x[0] in PSUM}):
            has, cur, prev = turn.get(name, (q, [], []))
            if has != q or q == "vs":
                cur, prev = [], cur
            pred.update(prev + (cur[-1:] if q == "t" else []))
            turn[name] = (q, cur + [i], prev)
        for wr, (name, lo, hi) in refs:
            old = recs.get(name, [])
            if wr:
                old = [r for r in old if not (lo <= r[0] and r[1] <= hi)]
            recs[name] = old + [(lo, hi, wr, i)]
        pred.discard(i)
        row = (q, out[1][0][0]) if out[1] and out[1][0][0] in ROWS else None
        if q != "vs":
            emit, cost = {q: emit}, {q: cost}
        ops.append({"part": part[0], "row": row, "pred": sorted(pred), "emit": emit, "cost": cost, "late": late, "sem": sem,
                    "gather": out[2] if ins and ins[0][4] else 0})

    def next_part():
        part[0] += 1

    def R(name, a=0, b=None, st=1, half=None):
        buf, base, w = PACK[name] if name in PACK else (name, 0, SCRATCH[name][1][1])
        b = w if b is None else b
        ap = T[buf][slice(None) if half is None else slice(64 * half, 64 * half + 64), base + a:base + b:st]
        size = 0 if buf in PSUM else 4 if SCRATCH[buf][2].endswith("32") else 2
        return (ap, [(buf, base + a, base + b)], -(-(b - a) // st), size, False)

    def H(name, h, w=128):
        return R(name, w * h, w * h + w)

    def C(name, j):
        return R(name, j, j + 1)

    def IND(win, off):
        return (win[0].indirect(off[0]), win[1] + off[1], 16 * off[2], win[3], True)

    def sc(x):
        return x[0] if isinstance(x, tuple) else x

    def cycles(out, ins, rate):
        if ins[0][4]:
            return LEAST + GATHER * out[2]
        if rate is None:
            rate = 0.5 if all(x[3] == 2 for x in [out] + ins) else 1
        return max(LEAST, rate * out[2])

    def tc(out, a):
        op("v", out, [a], lambda e: e.tensor_copy(out[0], a[0]), cycles(out, [a], None))

    def tt(out, a, b, o):
        op("v", out, [a, b], lambda e: e.tensor_tensor(out[0], a[0], b[0], o), cycles(out, [a], 2 if a[3] and b[3] else 1))

    def ts(out, a, s1, o1, s2=None, o2=None):
        ins = [a] + [s for s in (s1, s2) if isinstance(s, tuple)]
        args = (out[0], a[0], sc(s1), None, o1) if o2 is None else (out[0], a[0], sc(s1), sc(s2), o1, o2)
        op("v", out, ins, lambda e: e.tensor_scalar(*args), cycles(out, [a], None))

    def scan(out, a, b, o0, o1):
        op("v", out, [a, b], lambda e: e.tensor_tensor_scan(out[0], a[0], b[0], 0.0, o0, o1), cycles(out, [a, b], None))

    def act(out, a, fn=Fn.Copy, scale=1.0, bias=0.0):
        ins = [a] + [s for s in (scale, bias) if isinstance(s, tuple)]
        op("s", out, ins, lambda e: e.activation(out[0], a[0], fn, bias=sc(bias), scale=sc(scale)), cycles(out, [a], 1))

    def cp(out, a):
        op("vs", out, [a], {"v": lambda e: e.tensor_copy(out[0], a[0]), "s": lambda e: e.activation(out[0], a[0], Fn.Copy)},
           {"v": cycles(out, [a], None), "s": cycles(out, [a], 1)})

    def lin(out, a, scale, bias):
        op("vs", out, [a], {"v": lambda e: e.tensor_scalar(out[0], a[0], scale, bias, Op.mult, Op.add),
                            "s": lambda e: e.activation(out[0], a[0], Fn.Copy, bias=bias, scale=scale)},
           {"v": cycles(out, [a], None), "s": cycles(out, [a], 1)})

    def mm(out, l, r, start=True, stop=True):
        op("t", out, [l, r], lambda e: e.matmul(out[0], l[0], r[0], start, stop), TENSOR * max(LEAST, r[2]) * (4 if l[3] == 4 else 1))

    def iota(out, pattern, base=0, cm=0):
        op("g", out, [], lambda e: e.iota(out[0], pattern, base, cm, allow_small_or_imprecise_dtypes=True), 160 + 2 * out[2])

    def select(out, a, pattern, o, base, cm):
        op("g", out, [a], lambda e: e.affine_select(out[0], a[0], pattern, o, 0.0, base, cm), 205 + 2 * out[2])

    def fill(out, c):
        op("v", out, [], lambda e: e.memset(out[0], c), cycles(out, [out], None))

    loaded = [DMA]

    def load(q, out, src, sem):
        loaded[0] += 128 * out[2] * out[3] / BYTES + LINES
        op(q, out, [], lambda e: e.dma_start(out[0], src), LEAST, loaded[0], (sem, 16))

    sends, arrive = [0], {}

    def send(to, out, src, sem):
        dst, peer = T.cores[(rank + to) % N], T.cores[(rank - to) % N]
        rid, pid = topo.addr(dst)[:2]
        arrive[sem] = len(topo.engines(peer, core))
        sends[0] += len(topo.engines(core, dst))
        op("g", out, [src], lambda e: e.remote_dma(out[0], src[0], T.sem[sem], T.sem["sent"], pid, rid, topo.mask(core, dst)),
           HOP / 4 + (0 if len(arrive) > 1 else FIRST), HOP + 128 * out[2] * out[3] / 80, (sem, arrive[sem]))

    outs = [0]

    def store(q, dst, ap, ref):
        outs[0] += 16
        op(q, (None, []), [ref], lambda e: e.dma_start(dst, ap), LEAST, DMA, ("sout", 16))

    load("d", R("a0i"), T.a0[:, :], "la")
    load("s", R("hi0"), T.hd0[:, :], "lh0")
    load("d", R("zz0"), T.z0[:, :], "lz")
    load("s", R("fi0"), T.fl0[:, :], "lf0")
    load("d", R("sui", 0, 2048), T.su[:, :], "ls")
    load("d", R("xw", X0), T.xs[:, :], "lx")
    load("d", R("bank", B0), T.gs[:, :], "lg")

    iota(R("ci"), [[1, 1]], 0, 1)
    iota(R("pat16"), [[0, 16], [1, 16]])
    iota(R("jf"), [[1, 128]])
    iota(R("qd16"), [[1, 8], [0, 16]])
    iota(R("lanb"), [[0, 8], [128, 2]], 0, 1)
    iota(R("patc"), [[0, 2], [1, 8], [0, 8]], -32)
    iota(R("pat8"), [[0, 8], [1, 8]])
    iota(R("sui", 2048, 4096), [[1, 2048]])
    fill(R("ones"), 1.0)
    fill(R("huge"), 2.0 ** 20)
    fill(R("urow"), 6144.0)
    for name, tmp, c, o in (("p16", "ci2", 15, Op.bitwise_and), ("pdiv", "ci3", 4, Op.arith_shift_right), ("p8", "ci4", 7, Op.bitwise_and)):
        ts(R(tmp), R("ci"), c, o)
        cp(R(name), R(tmp))
    ts(R("mask16"), R("pat16"), R("p16"), Op.is_equal)
    tc(R("e16"), R("pat16", 0, 16))
    lin(R("e15"), R("pat16", 0, 8), 16.0, 15.0)
    for h in (0, 1):
        ts(H("et16", h, 8), R("pat16", 0, 8), 2.0, Op.mult, float(h), Op.add)
        act(C("p8h", h), R("p8"), scale=2.0, bias=float(h))
        ts(H("e8", h, 4), R("pat16", 0, 4), 0.0, Op.mult, C("p8h", h), Op.add)
    ts(R("boh"), R("qd16"), R("pdiv"), Op.is_equal)
    cp(R("bo"), R("boh"))
    ts(R("ob8"), R("pat16", 0, 8), R("pdiv"), Op.is_equal)
    for name, c in (("ob8h", 1), ("ob4h", 4), ("om8", -0.125), ("o16", 16), ("o32", 32), ("om16", -16), ("o16h", 16), ("o32h", 32)):
        act(R(name), R("ob8"), scale=float(c))
    for k in range(3):
        cp(H("ob24", k, 8), R("ob8"))
    select(R("idb"), R("ones"), [[-1, 128]], Op.is_equal, 0, 1)
    for name, c in (("idn", -1), ("id256", 256), ("idk", 16384), ("idm", -0.0625), ("id32", 1 / 32), ("idf", 1), ("id4", 4), ("idu", -4096)):
        act(R(name), R("idb"), scale=float(c))
    act(R("negm"), R("mask16"), scale=4096.0, bias=-4096.0)
    act(R("big"), R("pat16"), Fn.Relu, scale=-2.0 ** 20, bias=R("huge"))
    act(R("rst"), R("big"), scale=-2.0 ** -7)
    act(R("keep"), R("pat8"), Fn.Sign)
    ts(R("gneg"), R("pat8"), R("pdiv"), Op.not_equal, -2.0 ** 31, Op.mult)
    act(R("quar"), R("ones"), scale=-2.0 ** -14)
    act(R("rowc"), R("pat16", 0, 128), scale=1.0 / 128)
    for k, c in enumerate((-1.0, -1.0, -5.0)):
        act(H("crow", k, 16), R("ones", 0, 16), scale=c / 128)
    act(R("brow"), R("ones", 0, 16), scale=B0 / 128)
    select(R("tri"), R("quar"), [[1, 128]], Op.is_gt, 0, -1)
    act(R("i128"), R("jf"), scale=1 / 128)
    act(R("pat192"), R("pat16"), bias=192.0)
    act(R("dump"), R("pat16", 0, 8), Fn.Identity, scale=16.0, bias=R("p16"))
    act(R("q16"), R("dump"), scale=16.0)
    act(R("odd"), R("p16"), scale=2.0, bias=1.0)
    act(R("odd32"), R("p16"), scale=64.0, bias=32.0)
    act(R("bow"), R("bo"), scale=R("odd"))
    act(R("bo16"), R("boh"), scale=16.0)
    for k, nv in enumerate(SHARES):
        select(H("bs", k), R("bo16"), [[0, 8], [1, 16]], Op.is_ge, -nv, 0)
    for c in range(15):
        if c != 7:
            fill(R("eb", 256 * c + 128 * (c >= 8), 272 * c + 16), 0.0)
    fill(R("bank", 0, B0), 0.0)
    fill(R("xw", 0, X0), 0.0)
    act(R("tmp"), R("hi0"), scale=8.0)
    tt(R("cw"), R("tmp"), R("fi0"), Op.add)
    tt(R("os"), IND(R("a0i"), R("e16")), R("mask16"), Op.mult)

    RB, KB = ("ps0", "ps7"), ("ps2", "ps5")

    def states(t, h):
        mm(R(RB[h], 0, 128), R("idb"), H("negm", h), True, False)
        mm(R(RB[h], 0, 128), R("boh"), H("os", h), False, False)
        mm(R(RB[h], 128, 256), R("boh"), H("os", h), False, True)
        scan(H("sl", h), H("rst", h), R(RB[h], 0, 128), Op.add, Op.max)
        cp(H("arow", h), R(RB[h], 128, 256))
        cp(H("als", h, 8), R("sl", 128 * h + 15, 128 * h + 128, 16))
        tt(H("dg", h), H("sl", h), R(RB[h], 128, 256), Op.is_equal)
        next_part()
        cp(H("alu", h, 8), R("sl", 128 * h + 15, 128 * h + 128, 16))
        cp(H("suu", h), IND(R("sui", 0, 2048), H("alu", h, 8)))
        for k in (2 * h, 2 * h + 1):
            (tc if (t, k) == (0, 1) else cp)(H("cc", k, 1024), IND(R("xw", X0), H("suu", k, 64)))

    def places(t):
        for h in (0, 1):
            mm(R("ps1", 160 + h, 176, 2), H("os", h), R("ob8h"), h == 0, h == 1 and t == ASKS)
        if t < ASKS:
            mm(R("ps1", 176, 192), R("ones"), R("brow"), False, False)
            mm(R("ps1", 176, 192), R("idk"), R("lanb"), False, False)
            for h in (0, 1):
                mm(R("ps1", 176 + h, 192, 2), H("os", h), R("ob4h"), False, h == 1)
        lin(R("ahb"), R("ps1", 160, 176), 1 / 128, 191.5 + 1 / 256)
        lin(R("atf"), R("ps1", 160, 176), 1 / 128, 192.0)
        tt(R("alof"), R("atf"), R("ahb"), Op.subtract)
        tt(R("ah"), IND(R("ahb"), R("et16")), R("pat192"), Op.is_equal)
        ts(R("alo"), R("sl", 15, 256, 16), 127, Op.bitwise_and)
        cp(R("alou"), R("alo"))
        cp(R("gc_"), IND(R("cw"), R("alou")))
        mm(R("ps0", 256, 512), R("id256"), R("ah"), True, False)
        for h in (0, 1):
            mm(H("ps0", 2 + h), H("gc_", h), R("idb"), False, h == 1)
        scan(R("lk"), R("rst"), R("ps0", 256, 512), Op.add, Op.max)
        ts(R("hfi", 0, 16), R("lk", 15, 256, 16), 3, Op.arith_shift_right, 3, Op.bitwise_and)
        ts(R("hfi", 16, 32), R("lk", 15, 256, 16), 7, Op.bitwise_and)
        cp(R("hfb"), R("hfi"))
        next_part()
        mm(R("ps1", 0, 48), R("ones"), R("crow"), True, False)
        for h in (0, 1):
            mm(R("ps1", h, 48, 2), H("dg", h), R("ob24"), False, False)
        for c in range(15):
            ts(R("eb", 272 * c + 16, 256 * c + 256), R("arow", 16 * c + 16, 256), C("als", c), Op.is_equal)
            for h in (0, 1) if c < 7 else (1,):
                mm(R("ps1", h, 48, 2), H("eb", 2 * c + h), R("ob24"), False, False)
        for h in (0, 1):
            mm(R("ps1", h, 16, 2), R("idb"), H("hfb", h, 8), False, False)
            for k in (1, 2):
                mm(R("ps1", 16 * k + h, 16 * k + 16, 2), R("idn"), H("hfb", 2 + h, 8), False, h == 1 and k == 2)

    def offsets(t):
        cp(R("xi"), R("ps1", 0, 16))
        ts(R("bn"), R("ps1", 16, 48), 0.0, Op.is_ge, -16384.0, Op.mult)
        ts(R("x3"), R("xi"), 3, Op.bitwise_and)
        if t < ASKS:
            tt(R("pv"), R("x3"), R("ps1", 176, 192), Op.add)
        mm(R("ps1", 64, 80), R("id4"), R("als"), True, False)
        mm(R("ps1", 80, 96), R("idf"), R("als"), False, False)
        tt(R("y"), R("x3"), R("bn", 0, 16), Op.add)
        tt(R("ay"), IND(R("y"), R("et16")), R("mask16"), Op.mult)
        for k, o in ((64, "ob8"), (80, "om8")):
            for h in (0, 1):
                mm(R("ps1", k + 8 * h, k + 8 * h + 8), H("ay", h), R(o), False, k == 80 and h == 1)
        lin(R("offu"), R("ps1", 64, 80), 1.0, 16.0)
        lin(R("sou"), R("ps1", 80, 96), 1.0, 0.375)
        cp(R("sp"), IND(R("sui"), R("sou")))
        next_part()
        mm(R("ps3", 384, 400), R("idm"), R("bn", 16, 32), True, False)
        mm(R("ps3", 384, 400), R("id32"), R("bn", 0, 16), False, False)
        mm(R("ps3", 384, 400), R("tri"), R("bn", 0, 16), False, False)
        mm(R("ps3", 385, 400, 2), R("quar"), R("bn", 0, 16, 2), False, True)
        if t < ASKS:
            cp(R("ri"), R("ps3", 384, 400))
            lin(R("rhi"), R("ps3", 384, 400), 1 / 16, -15 / 32)
        ts(R("put"), R("ps3", 384, 400), -384.0, Op.is_lt)
        lin(R("w7"), R("bn", 0, 16), 7.0 / 16384, 7.0)
        tt(R("w"), R("put"), R("w7"), Op.add)

    def ask(t):
        qp = R("qp%d" % t)
        ts(R("rlo"), R("ri"), 15, Op.bitwise_and)
        tt(R("cb"), IND(R("rhi"), R("e8")), R("patc"), Op.is_equal)
        tt(R("ca"), IND(R("rlo"), R("et16")), R("pat16"), Op.is_equal)
        tt(R("cb2"), IND(R("pv"), R("e8")), R("cb"), Op.mult)
        mm(R("ps6", 256, 320), R("idb"), R("gneg"), True, False)
        for h in (0, 1):
            mm(R("ps6", 256, 320), H("ca", h), H("cb2", h, 64), False, h == 1)
        scan(R("qs"), R("keep"), R("ps6", 256, 320), Op.mult, Op.max)
        cp(qp, R("qs", 7, 64, 8))
        send(1 + t % (N - 1), R("qpin%d" % t), qp, "rp%d" % t)
        ts(R("v1"), qp, 16383, Op.bitwise_and)
        tt(R("offr%d" % t), R("v1"), R("dump"), Op.max)

    def update(t):
        mm(R("ps1", 192, 320), R("cw"), R("idb"), True, False)
        for k in range(16):
            col = 2 * (k % 8) + k // 8
            ts(H("hot", k), R("i128"), C("alof", col), Op.is_equal, C("w", col), Op.mult)
            mm(R("ps1", 192 + 16 * (k % 8), 208 + 16 * (k % 8)), H("hot", k), H("ah", k, 16), False, k == 15)
        next_part()
        cp(R("ut"), R("ps1", 192, 320))
        mm(R("ps1", 320, 448), R("ut"), R("idb"))
        if t < ASKS:
            cp(R("cw"), R("ps1", 320, 448))
        else:
            cp(R("w1"), R("ps1", 320, 448))
            ts(R("w2"), R("w1"), 3, Op.arith_shift_right, 3, Op.bitwise_and)
            ts(R("w3"), R("w1"), 7, Op.bitwise_and)
            cp(R("ohf"), R("w2"))
            cp(R("oyf"), R("w3"))

    def pops(t):
        zn = "zz%d" % (t + 1)
        if t > 0:
            wi, of, src = R("bank"), R("offr%d" % (t - 1)), R("anin%d" % (t - 1))
            op("v", wi, [src, of], lambda e: e.tensor_copy(wi[0].indirect(of[0]), src[0]), LEAST + SCATTER * 128)
        tt(R("zs"), IND(R("bank", B0 - 16), R("offu")), R("zz%d" % t), Op.add)
        ts(R(zn), R("zs"), 0.0, Op.max, 255.0, Op.min)
        mm(R("ps3", 0, 256), R("idb"), R(zn))
        if t + 1 < ASKS:
            send(1 + (t + 1) % (N - 1), R("zin%d" % (t + 1)), R(zn), "rz%d" % (t + 1))

    def dist(t):
        zn = "zz%d" % (t + 1)
        chunks = [(h, range(m, min(m + 4, 16))) for h in (0, 1) for m in range(16 - NS[t][h], 16, 4)]

        def cc(h, m):
            return R("cc", 2048 * h + m, 2048 * h + 2048, 16)

        def mx(h, m):
            return H("mx", 16 * h + m)

        for k, (h, ms) in enumerate(chunks):
            bank = RB[k % 2]
            for j, m in enumerate(ms):
                mm(H(bank, j), R("idb"), cc(h, m), j == 0, False)
            for j, m in enumerate(ms):
                mm(H(bank, j), R("idn"), H(zn, h), False, j == len(ms) - 1)
            act(R("mx", 128 * (16 * h + ms[0]), 128 * (16 * h + ms[-1] + 1)), R(bank, 0, 128 * len(ms)), Fn.Abs)
        for h in (0, 1):
            nv = 16 - NS[t][h]
            mm(R(KB[h], 0, 128), R("ones"), R("rowc"), True, False)
            for m in range(nv):
                mm(R(KB[h], m, 128, 16), cc(h, m), R("om16"), False, False)
            if 0 < nv < 16:
                mm(R(KB[h], 0, 128), H(zn, h), H("bs", SHARES.index(nv)), False, False)
            for m in range(nv):
                tt(mx(h, m), cc(h, m), H("ps3", h), Op.max)
                mm(R(KB[h], m, 128, 16), mx(h, m), R("o32"), False, m == 15)
            for m in range(nv, 16):
                mm(R(KB[h], m, 128, 16), mx(h, m), R("o16"), False, m == 15)

    def choose(t, h):
        scan(H("ksc", h), R("big", 0, 128), R(KB[h], 0, 128), Op.add, Op.min)
        tc(H("ks", h), R(KB[h], 0, 128))
        tt(H("oh", h), IND(H("ksc", h), R("e15")), H("ks", h), Op.is_equal)
        mm(R(KB[h], 128, 256), H("oh", h), R("idb"))
        tt(H("os", h), R(KB[h], 128, 256), H("sp", h), Op.mult)

    def answer(t):
        qpin, zin = R("qpin%d" % t), R("zin%d" % t)
        mm(R("ps4", 0, 256), R("bow"), zin)
        lin(R("uk"), R("ps4", 0, 256), 1 / 4096, 191.5 + 1 / 8192)
        mm(R("ps4", 256, 512), R("bow"), zin, True, False)
        mm(R("ps4", 256, 512), R("ones"), R("urow"), False, False)
        mm(R("ps4", 256, 512), R("idu"), R("uk"), False, True)
        act(R("uy"), R("ps4", 256, 512), Fn.Identity, bias=R("odd32"))
        tt(R("pr"), R("uy"), R("ps4", 256, 512), Op.mult)
        ts(R("ux"), R("pr"), 5, Op.arith_shift_right, 8191, Op.bitwise_and)
        next_part()
        lin(R("dqu", 0, 8), qpin, 1 / 16384, -0.25)
        ts(R("dq"), qpin, 2, Op.arith_shift_right, 4095, Op.bitwise_and)
        cp(R("dqu", 8, 16), R("dq"))
        cp(R("zq"), IND(zin, R("dqu", 0, 8)))
        tt(R("wq"), IND(R("xw"), R("dqu", 8, 16)), R("zq"), Op.subtract)
        mm(R("ps3", 256, 384), R("idb"), R("wq"))
        cp(R("cou"), IND(R("ux"), R("dqu", 0, 8)))
        for k in (0, 1):
            cp(H("cand", k, 1024), IND(R("bank", B0), H("cou", k, 64)))
        next_part()
        mm(R("ps4", 256, 384), R("ones"), R("rowc"), True, False)
        mm(R("ps4", 256, 384), R("wq"), H("bs", SHARES.index(16 - NQ)), False, False)
        for k in (0, 1):
            keys = [R("ps4", 256 + m, 384, 16, k) for m in range(16)]
            cand = [R("cand", 1024 * k + m, 1024 * k + 1024, 16) for m in range(16)]
            for a in range(16 - NQ, 16, 4):
                for j in range(4):
                    mm(H("ps6", j, 64), R("idb"), cand[a + j], j == 0, False)
                    mm(H("ps6", j, 64), R("idn"), H("wq", k, 64), False, j == 3)
                act(R("mq", 1024 * k + 64 * a, 1024 * k + 64 * a + 256), R("ps6", 0, 256), Fn.Abs)
            for m in range(16 - NQ):
                mm(keys[m], cand[m], R("om16"), False, False)
                tt(H("mq", 16 * k + m, 64), cand[m], H("ps3", 4 + k, 64), Op.max)
                mm(keys[m], H("mq", 16 * k + m, 64), R("o32h"), False, False)
            for m in range(16 - NQ, 16):
                mm(keys[m], H("mq", 16 * k + m, 64), R("o16h"), False, m == 15)
        next_part()
        scan(R("kq"), R("big", 0, 128), R("ps4", 256, 384), Op.add, Op.min)
        ts(R("mi"), R("kq", 15, 128, 16), 15, Op.bitwise_and)
        tt(R("aq"), IND(R("mi"), R("e16", 0, 8)), R("mask16", 0, 128), Op.mult)
        mm(R("ps4", 384, 392), R("idb"), R("q16"), True, False)
        mm(R("ps4", 384, 392), R("aq"), R("ob8"), False, True)
        cp(R("seu"), R("ps4", 384, 392))
        cp(R("an%d" % t), IND(R("cand"), R("seu")))
        send(-1 - t % (N - 1), R("anin%d" % t), R("an%d" % t), "ra%d" % t)

    send(1, R("zin0"), R("zz0"), "rz0")
    for h in (0, 1):
        states(0, h)
    for t in range(STEPS):
        for f in (places, offsets, ask, update, pops, dist, answer):
            next_part()
            if t < ASKS or f not in (ask, answer):
                f(t)
        for h in (0, 1):
            next_part()
            choose(t, h)
            next_part()
            if t + 1 < STEPS:
                states(t + 1, h)
            else:
                mm(R(RB[h], 128, 256), R("boh"), H("os", h))
                cp(H("arf", h), R(RB[h], 128, 256))
    store("d", T.yz[:, :], R("zz%d" % STEPS)[0], R("zz%d" % STEPS))
    buf, base, w = PACK["arf"]
    store("d", T.ya[:, :], T[buf][0:128:16, base:base + w], R("arf"))
    store("d", T.yf[:, :], R("oyf")[0], R("oyf"))
    store("d", T.yh[:, :], R("ohf")[0], R("ohf"))

    qsem = {"v": "sv", "s": "ss", "t": "st", "g": "sg"}
    count = {q: 0 for q in qsem}
    known = {q: {} for q in qobj}
    done = {}

    def need(q, sem, n, snap):
        kn = known[q]
        if kn.get(sem, 0) < n:
            qobj[q].wait_ge(T.sem[sem], n)
            kn[sem] = n
            for a, b in snap.items():
                if kn.get(a, 0) < b:
                    kn[a] = b

    if not ORDER:
        ORDER.extend(plan(ops))
    for i, q in ORDER:
        o, todo = ops[i], {}
        for p in o["pred"]:
            sem, n, snap = done[p]
            if not (q == "t" and sem == "st") and todo.get(sem, (0,))[0] < n:
                todo[sem] = (n, snap)
        for sem in sorted(todo, key=lambda s: -len(todo[s][1])):
            need(q, sem, todo[sem][0], todo[sem][1])
        ins = o["emit"][q](qobj[q])
        if o["sem"] is None:
            count[q] += 1
            ins.then_inc(T.sem[qsem[q]], 1)
            done[i] = (qsem[q], count[q], dict(known[q]))
        else:
            if o["sem"][0] not in arrive:
                ins.then_inc(T.sem[o["sem"][0]], 16)
            done[i] = o["sem"] + ({},)
    g.sync.wait_ge(T.sem["sout"], outs[0])
    for q in "vstg":
        need("g", qsem[q], count[q], {})
    for s in LOADS:
        need("g", s, 16, {})
    for s in sorted(arrive):
        need("g", s, arrive[s], {})
    g.wait_ge(T.sem["sent"], sends[0])
